import numpy as np, ml_dtypes
CORES = [23,119,17,113]
N = 4
import mx_ref
BF = ml_dtypes.bfloat16
def entries(a):
    return np.ascontiguousarray(a.T).reshape(-1)
def table(e):
    return np.ascontiguousarray(np.reshape(e, (-1, 16)).T).astype(np.int32)
def cols(t, e):
    v = np.concatenate([t.reshape(128, -1, 4), np.zeros((128, 1, 4), BF)], axis=1)
    return np.ascontiguousarray(v[:, e]).reshape(128, -1)
def f(rng, *shape):
    return mx_ref.flush((rng.standard_normal(shape, dtype=np.float32) * np.exp2(rng.integers(-2, 3, shape[:-1] + (1,)))).astype(BF))
def wide(rng, *shape, cols=0):
    v = rng.standard_normal(shape, dtype=np.float32) * np.exp2(rng.integers(-12, 13, shape)).astype(np.float32)
    if cols: v *= np.repeat(np.exp2(rng.integers(-cols, cols + 1, shape[:-2] + (1, shape[-1] // 4))) * (rng.random(shape[:-2] + (1, shape[-1] // 4)) > 0.0625), 4, axis=-1).astype(np.float32)
    return mx_ref.flush(v.astype(BF))
P, V, R, O, CAP, ALL = 256, 96, 4, 2, 30, 112
HOME = np.concatenate([np.repeat(np.arange(N), P), np.repeat(np.arange(N), V)])
def flat(a):
    return np.concatenate([entries(e) for e in a])
def game(alt, f1, f2):
    first, second = np.concatenate([np.arange(N * P), f1]), np.concatenate([alt, f2])
    stands = np.where(alt >= 0, np.arange(N * P), -1)
    k, leave, to, out = N * P + np.arange(N * V), np.repeat(np.arange(N), V), f1, []
    for t in range(R):
        was = stands[to]
        stands = np.array(stands); stands[to] = k
        out.append((k, leave, to, stands))
        k, at = was[was >= 0], to[was >= 0]
        leave, to = at // P, np.where(first[k] == at, second[k], first[k])
    return out
def draw(rng, lo, hi, aim):
    stands = np.full((N, P), -1)
    for r in range(N):
        p = rng.permutation(P)[:rng.integers(lo, hi + 1)]
        stands[r, p] = r * P + p
    if aim == "long":
        r = int(rng.integers(0, N)); stands[r] = r * P + np.arange(P)
    if aim == "short": stands[int(rng.integers(0, N))] = -1
    stands = stands.reshape(-1); start = stands >= 0
    first, second = np.concatenate([np.arange(N * P), np.full(N * V, -1)]), np.full(N * P + N * V, -1)
    came, total = np.zeros((N * P + N * V, N), bool), np.zeros((N, N), int)
    k, leave, at = N * P + np.arange(N * V), np.repeat(np.arange(N), V), np.full(N * V, -1)
    goal, last = int(rng.integers(0, N)), None
    mark, late = (goal + 1) % N, 0
    for t in range(R):
        used, free, to = np.zeros((N, N), int), np.ones(N * P, bool), np.full(len(k), -1)
        if aim == "long": mask = stands >= 0
        elif aim == "short" and t > 0: mask = stands < 0
        elif aim == "home" and t == 2: mask = np.isin(np.arange(N * P), last)
        elif aim == "peak": mask = np.arange(N * P) // P == goal
        else: mask = np.ones(N * P, bool)
        known = second[k] >= 0
        o = rng.permutation(len(k))
        if aim == "peak": o = np.concatenate([o[HOME[k[o]] == mark], o[HOME[k[o]] != mark]])
        for i in np.concatenate([o[known[o]], o[~known[o]]]):
            j, q, h = k[i], leave[i], HOME[k[i]]
            good = free & np.repeat((used[q] < CAP) & (came[j] | (total[h] < ALL) | (np.arange(N) == h)), P)
            if at[i] >= 0: good[at[i]] = False
            if known[i]:
                x = second[j] if first[j] == at[i] else first[j]
                if not good[x]: return None
            else:
                if (good & mask).any(): good = good & mask
                if not good.any(): return None
                x = rng.choice(np.flatnonzero(good))
                if t == 0: first[j] = x
                else: second[j] = x
            r = x // P
            to[i] = x; free[x] = False; used[q, r] += 1
            if r != h and not came[j, r]: total[h, r] += 1
            came[j, r] = True
        if aim == "long" and len(k) < N * V: return None
        if aim == "short" and ((t == 1 and len(k) == 0) or (t > 1 and len(k) > 0)): return None
        if aim == "home" and t == R - 1 and (to == k).sum() < N * V // 4: return None
        if aim == "peak" and t < 2 and (used[:, goal] < CAP).any(): return None
        if aim == "peak" and t >= 2: late = max(late, int(used[np.arange(N) != goal, goal].max()))
        was = stands[to]; stands[to] = k; last = to
        k, at = was[was >= 0], to[was >= 0]
        leave = at // P
    if aim == "peak" and (late < CAP - 4 or total[mark, goal] < ALL - 1): return None
    j = np.flatnonzero((second < 0) & np.concatenate([start, np.ones(N * V, bool)]))
    x = rng.integers(0, N * P - 1, len(j)); second[j] = x + (x >= first[j])
    return {"alt": np.stack([table(e) for e in second[:N * P].reshape(N, P)]), "f1": np.stack([table(e) for e in first[N * P:].reshape(N, V)]), "f2": np.stack([table(e) for e in second[N * P:].reshape(N, V)])}
def lists(rng, lo, hi, aim=None):
    for i in range(50):
        d = draw(rng, lo, hi, aim)
        if d is not None: return d
    raise RuntimeError("no draw in 50 tries")
def setup_inputs(rng):
    return {"c": f(rng, N, 128, 4 * P), "v": f(rng, N, 128, 4 * V), "w": f(rng, N, 128, 512 * R * O), **lists(rng, P // 2, 7 * P // 8)}
def setup_inputs_long(rng):
    return {**setup_inputs(rng), **lists(rng, 15 * P // 16, 31 * P // 32, "long")}
def setup_inputs_short(rng):
    return {**setup_inputs(rng), **lists(rng, P // 2, P // 2, "short")}
def setup_inputs_home(rng):
    return {**setup_inputs(rng), **lists(rng, 3 * P // 4, 3 * P // 4, "home")}
def setup_inputs_peak(rng):
    return {**setup_inputs(rng), **lists(rng, 7 * P // 8, 7 * P // 8, "peak")}
def setup_inputs_spread(rng):
    d = setup_inputs(rng); d["c"] = wide(rng, N, 128, 4 * P, cols=6); d["v"] = wide(rng, N, 128, 4 * V, cols=6); return d
def check_inputs(d):
    b = []
    alt, f1, f2 = flat(d["alt"]), flat(d["f1"]), flat(d["f2"])
    if alt.min() < -1 or alt.max() >= N * P or (alt == np.arange(N * P)).any(): b.append("alt")
    if f1.min() < 0 or f1.max() >= N * P: b.append("f1")
    if f2.min() < 0 or f2.max() >= N * P or (f1 == f2).any(): b.append("f2")
    if b: return b
    came = np.zeros((N * P + N * V, N), bool)
    for k, leave, to, stands in game(alt, f1, f2):
        if len(set(to.tolist())) != len(to): return b + ["two columns go to one place in one round"]
        n = np.zeros((N, N), int); np.add.at(n, (leave, to // P), 1)
        if n.max() > CAP: b.append("more than CAP columns from one rank to one rank in one round")
        came[k, to // P] = True
    for q in range(N):
        for r in range(N):
            if q != r and came[HOME == q, r].sum() > ALL: b.append("more than ALL columns of one rank come to another one")
    return b
def reference(c, v, w, alt, f1, f2):
    every = np.concatenate([c[r] for r in range(N)] + [v[r] for r in range(N)], axis=1)
    y = np.zeros((N, 128, R * O * P), np.float32)
    for t, (k, leave, to, stands) in enumerate(game(flat(alt), flat(f1), flat(f2))):
        for r in range(N):
            q = mx_ref.quantize(cols(every, stands[P * r:P * r + P]))
            for i in range(O * t, O * t + O):
                y[r][:, P * i:P * i + P] = mx_ref.matmul(mx_ref.quantize(w[r][:, 512 * i:512 * i + 512]), q)
    return {"y": y}

@@ -1,0 +1,497 @@
+from concourse.bass import DstId, RemoteDMATransfer
+from concourse.mybir import dt, AluOpType as Op, ActivationFunctionType as Act
+
+N, P, V, R, O = 4, 256, 96, 4, 2
+SLOTS = 112
+OWN = SLOTS + V + P
+WIN = OWN + 3 * SLOTS
+ST = 24
+FLAG = 2
+PLACES = 3072
+F32, I32, U16, BF, CODE, PL = "float32", "int32", "uint16", "bfloat16", "float8_e4m3fn_x4", "uint8"
+
+
+def _s(n, t):
+    return ("sbuf", [128, n], t)
+
+
+SCRATCH = {
+    "xl": _s(20, I32), "pcol": _s(1, I32), "pci": _s(7, I32), "pcf": _s(9, F32), "pk": _s(8, F32), "lane": _s(1, F32),
+    "k8": _s(8, F32), "pos": _s(8, F32), "ke": _s(8, F32), "xi": _s(120, I32), "xf": _s(48, F32), "ss": _s(14, F32),
+    "land": _s(4 * ST, U16), "dd": _s(8 * ST, F32), "fri": _s(4 * ST, F32),
+    "eli": _s(92, F32), "el": _s(92, U16), "ex": _s(1408, F32), "tab": _s(PLACES + 384, F32), "ev": _s(384, F32), "to0": _s(24, F32), "tou": _s(24, U16),
+    "gc": _s(384, F32), "mxi": _s(24, F32), "mx": _s(24, F32), "x2": _s(24, F32), "y2": _s(24, F32), "lcf": _s(24, F32), "lc": _s(24, U16), "w1": _s(24, F32),
+    "ne3": _s(16, F32), "df3": _s(16, F32), "pr3": _s(16, F32), "r3": _s(16, F32),
+    "dmi": _s(14, F32), "dum": _s(14, F32), "vai": _s(224, F32), "val": _s(224, F32),
+    "bli": _s(4, F32), "bl": _s(4, U16), "lli": _s(2, F32), "ll": _s(2, U16),
+    "rke": _s(14, F32), "sm": _s(3, F32), "sm8": _s(3, F32), "own14": _s(14, F32), "msk": _s(42, F32), "any1": _s(14, F32), "any2": _s(14, F32),
+    "ein": _s(448, F32), "dix": _s(448, F32), "fst": _s(448, F32), "scs": _s(448, F32), "d0": _s(352, F32),
+    "oss": _s(448, F32), "spm": _s(42, F32), "b0a": _s(14, F32), "b0": _s(14, F32), "b1": _s(14, F32),
+    "fo1": _s(3, F32), "fo2": _s(3, F32), "fo3": _s(3, F32), "fof": _s(4, U16), "lst": _s(616, F32),
+    "un": _s(352, F32), "sc": _s(352, F32), "osd": _s(352, F32), "cm": _s(33, F32), "cs1": _s(11, F32), "cs2": _s(11, F32),
+    "fl": _s(11, F32), "bb": _s(11, F32), "fb": _s(11, F32), "of1": _s(11, F32), "ofd": _s(12, U16),
+    "olt": _s(384, F32), "zb": _s(32, F32), "zt": _s(32, F32), "zg": _s(64, F32), "zh": _s(64, F32), "loff": _s(32, U16),
+    "lin": _s(24, U16), "mv": _s(WIN, F32), "m": _s(4 * OWN, F32),
+    "sn": _s(768, F32), "ts": _s(256, F32), "ido": _s(64, U16), "mg": _s(1024, F32), "om": _s(1024, F32), "off": _s(64, U16),
+    "cv": _s(4 * OWN, BF), "qo": _s(OWN, CODE), "qop": _s(OWN, PL), "q": _s(WIN, CODE), "qp": _s(WIN, PL),
+    "wb": _s(4096, BF), "wq": _s(1024, CODE), "wp": _s(1024, PL), "ys": _s(2048, F32),
+    "ga0": _s(384, F32), "ga2": _s(384, F32),
+    "ps": ("psum", [128, 4096], F32),
+}
+for _t in range(3):
+    SCRATCH["gt%d" % _t] = _s(384, F32)
+    SCRATCH["ti%d" % (_t + 1)] = _s(24, F32)
+    SCRATCH["to%d" % (_t + 1)] = _s(24, U16)
+    SCRATCH["sq%d" % _t] = _s(SLOTS, CODE)
+    SCRATCH["sqp%d" % _t] = _s(SLOTS, PL)
+for _t in range(4):
+    SCRATCH["k%d" % _t] = _s(P, CODE)
+    SCRATCH["kp%d" % _t] = _s(P, PL)
+PART = {n: ("xi", 20 * k, 20) for k, n in enumerate(["xb", "xc", "xd", "xt", "xp", "rk"])}
+PART.update({n: ("xf", 8 * k, 8) for k, n in enumerate(["emp", "p1", "we", "ne", "z1", "z2"])})
+PART.update({"ga1": ("tab", PLACES, 384), "lf": ("dd", 0, 4 * ST), "fr": ("dd", 4 * ST, 4 * ST)})
+
+SEMAPHORES = ["sv", "ss", "st", "sg", "ldx", "ldv", "ldc", "ldw0", "ldw1", "arrl", "arrm", "arrq", "arrp", "lsl", "lsm", "lsq", "lsp", "sty", "own", "sns"]
+
+
+def rank_program(g, core, T, topo):
+    r = T.rank_of(core)
+    if r is None:
+        return
+    others = [x for x in range(N) if x != r]
+    eng = {"v": g.vector, "s": g.scalar, "t": g.tensor, "g": g, "y": g.sync}
+    sem_of = {"v": "sv", "s": "ss", "t": "st", "g": "sg"}
+    cnt, known, log, total = {}, {k: {} for k in eng}, {}, {}
+
+    def clash(a, b):
+        if a[0] >= b[1] or b[0] >= a[1]:
+            return False
+        return not (a[2] == b[2] and a[2] > 1 and (a[0] - b[0]) % a[2])
+
+    def wait(q, tok):
+        s, v, clock, _ = tok
+        if known[q].get(s, 0) >= v:
+            return
+        eng[q].wait_ge(T.sem[s], v)
+        for k, x in list(clock.items()) + [(s, v)]:
+            known[q][k] = max(known[q].get(k, 0), x)
+
+    def order(q, reads, writes):
+        need = []
+        for regs, w in ((reads, False), (writes, True)):
+            for n, lo, hi, st in regs:
+                for l2, h2, s2, w2, tok in log.get(n, []):
+                    if not (w or w2) or not clash((lo, hi, st), (l2, h2, s2)):
+                        continue
+                    if w and not w2 and tok[3] == q:
+                        continue
+                    need.append(tok)
+        for tok in sorted(need, key=lambda t: -t[1]):
+            wait(q, tok)
+
+    def note(reads, writes, tok):
+        for regs, w in ((reads, False), (writes, True)):
+            for n, lo, hi, st in regs:
+                log.setdefault(n, []).append((lo, hi, st, w, tok))
+
+    def run(q, call, reads, writes, listed=False):
+        order(q, reads, writes)
+        s = sem_of[q]
+        cnt[s] = cnt.get(s, 0) + 1
+        call(eng[q]).then_inc(T.sem[s], 1)
+        note(reads, writes, (s, cnt[s], dict(known[q]), "list" if listed else q))
+
+    def load(q, sem, tot, out, in_, region):
+        eng[q].dma_start(out, in_).then_inc(T.sem[sem], 16)
+        total[sem] = tot
+        note([], [region], (sem, tot, {}, "dma"))
+
+    def ap(x):
+        n, lo, hi, st = x
+        return T[n][:, lo:hi] if st == 1 else T[n][:, lo:hi:st]
+
+    def A(n, lo=0, hi=None, st=1):
+        if n in PART:
+            b, o, w = PART[n]
+            return (b, o + lo, o + (w if hi is None else hi), st)
+        return (n, lo, SCRATCH[n][1][1] if hi is None else hi, st)
+
+    def sc_(x):
+        return ap(x) if isinstance(x, tuple) else x
+
+    def aps(*xs):
+        return [x for x in xs if isinstance(x, tuple)]
+
+    def tt(out, a, b, op):
+        run("v", lambda e: e.tensor_tensor(ap(out), ap(a), ap(b), op), [a, b], [out])
+
+    def ts(out, a, s1, op, s2=None, op1=None):
+        if op1 is None:
+            run("v", lambda e: e.tensor_scalar(ap(out), ap(a), sc_(s1), None, op), [a] + aps(s1), [out])
+        else:
+            run("v", lambda e: e.tensor_scalar(ap(out), ap(a), sc_(s1), sc_(s2), op, op1), [a] + aps(s1, s2), [out])
+
+    def cp(out, a, q="v"):
+        if q == "v":
+            run("v", lambda e: e.tensor_copy(ap(out), ap(a)), [a], [out])
+        else:
+            run("s", lambda e: e.activation(ap(out), ap(a), Act.Copy), [a], [out])
+
+    def act(out, a, scale, bias=0.0):
+        run("s", lambda e: e.activation(ap(out), ap(a), Act.Identity, bias=sc_(bias), scale=sc_(scale)), [a] + aps(scale, bias), [out])
+
+    def tr(out, a):
+        run("v", lambda e: e.transpose(ap(out), ap(a)), [a], [out])
+
+    def scan(out, a, b, start, op0, op1):
+        run("v", lambda e: e.tensor_tensor_scan(ap(out), ap(a), ap(b), sc_(start), op0, op1), [a, b] + aps(start), [out])
+
+    def fill(out, c):
+        run("v", lambda e: e.memset(ap(out), c), [], [out])
+
+    def gat(out, win, off, q="v"):
+        if q == "v":
+            run("v", lambda e: e.tensor_copy(ap(out), ap(win).indirect(ap(off))), [win, off], [out], True)
+        else:
+            run("s", lambda e: e.activation(ap(out), ap(win).indirect(ap(off)), Act.Copy), [win, off], [out], True)
+
+    def sca(win, off, a):
+        run("v", lambda e: e.tensor_copy(ap(win).indirect(ap(off)), ap(a)), [off, a], [win])
+
+    def pick(out, win, off):
+        run("v", lambda e: e.tensor_copy(ap(out).bitcast(dt.uint32), ap(win).bitcast(dt.uint32).indirect(ap(off))), [win, off], [out], True)
+
+    def quant(c, p, a):
+        run("v", lambda e: e.quantize_mx(ap(c), ap(p), ap(a)), [a], [c, p])
+
+    def iota(out, pattern, base, mult=0):
+        if SCRATCH[out[0]][2] == F32:
+            run("g", lambda e: e.iota(ap(out), pattern, base, mult, allow_small_or_imprecise_dtypes=True), [], [out])
+        else:
+            run("g", lambda e: e.iota(ap(out), pattern, base, mult), [], [out])
+
+    def pack(a, b):
+        quant(A("wq", a, b), A("wp", a, b), A("wb", 4 * a, 4 * b))
+
+    picked, engs = [], {}
+    for x in sorted(others, key=lambda x: len(topo.engines(core, T.cores[x]))):
+        e = [k for k in topo.engines(core, T.cores[x]) if k not in picked][:4]
+        picked += e
+        engs[x] = e
+
+    def post(sem, lsem, srcs, dsts):
+        order("g", srcs, [])
+        trs = []
+        for j, x in enumerate(others):
+            rid, pid, _ = topo.addr(T.cores[x])
+            s, d = ap(srcs[j]), ap(dsts[j])
+            if SCRATCH[srcs[j][0]][2] == CODE:
+                s, d = s.bitcast(dt.uint8), d.bitcast(dt.uint8)
+            trs.append(RemoteDMATransfer(dst_ids=[DstId(rid=rid, pnc=pid)], dma_engine_mask=sum(1 << k for k in engs[x]), remote_sem=T.sem[sem], src=s, dst=d))
+        g.remote_dma_fused(trs, local_sem=T.sem[lsem])
+        total[lsem] = sum(len(engs[x]) for x in others)
+
+    def arrive(sem, regions):
+        total[sem] = 4 * len(others)
+        note([], regions, (sem, 4 * len(others), {}, "far"))
+
+    jobs = []
+    for b in range(4):
+        jobs.append((T.xl[32 * b:32 * b + 32, 8:11], T.f1[:, :]))
+        jobs.append((T.xl[32 * b:32 * b + 32, 14:17], T.f2[:, :]))
+        jobs.append((T.xl[32 * b:32 * b + 32, 0:8], T.alt[:, :]))
+    for n, c in ((T.f1, 11), (T.f2, 17)):
+        for b in range(3):
+            jobs.append((T.xl[32 * b + 16:32 * b + 48, c:c + 3], n[:, :]))
+        jobs.append((T.xl[0:16, c:c + 3], n[8:16, :]))
+        jobs.append((T.xl[112:128, c:c + 3], n[0:8, :]))
+    for k, (o, i) in enumerate(jobs):
+        eng["ys"[k % 2]].dma_start(o, i).then_inc(T.sem.ldx, 16)
+    total["ldx"] = 16 * len(jobs)
+    note([], [A("xl")], ("ldx", 16 * len(jobs), {}, "dma"))
+    load("y", "ldv", 16, T.cv[:, 4 * SLOTS:4 * SLOTS + 4 * V], T.v[:, :], A("cv", 4 * SLOTS, 4 * SLOTS + 4 * V))
+    load("y", "ldc", 16, T.cv[:, 4 * SLOTS + 4 * V:4 * OWN], T.c[:, :], A("cv", 4 * SLOTS + 4 * V, 4 * OWN))
+    for k in range(2):
+        load("y", "ldw%d" % k, 16, T.wb[:, 2048 * k:2048 * k + 2048], T.w[:, 2048 * k:2048 * k + 2048], A("wb", 2048 * k, 2048 * k + 2048))
+
+    iota(A("pcol"), [[0, 1]], 0, 1)
+    iota(A("k8"), [[32, 8]], P * r)
+    iota(A("fri"), [[OWN, 4], [16, ST]], 16)
+    iota(A("eli", 0, 24), [[ST, 4], [1, 3], [3, 2]], 6)
+    iota(A("eli", 24, 88), [[ST, 4], [1, 8], [0, 2]], 12)
+    iota(A("eli", 88, 92), [[ST, 4]], 12)
+    iota(A("bli"), [[16, 2], [0, 2]], 0)
+    iota(A("lli"), [[8, 2]], 0)
+    iota(A("dmi"), [[16, 14]], 385)
+    iota(A("mxi"), [[16, 24]], PLACES)
+    me, mine = ST * r, (P * r, P * r + P)
+    fill(A("land", me + 20, me + 24), 0)
+    fill(A("cv", 0, 4 * SLOTS), 0.0)
+    fill(A("zb"), 0.0)
+    for k, (sh, m) in enumerate([(0, 31), (0, 1), (1, 15), (4, 1), (0, 15), (1, 7)]):
+        if sh:
+            ts(A("pci", k, k + 1), A("pcol"), sh, Op.arith_shift_right, m, Op.bitwise_and)
+        else:
+            ts(A("pci", k, k + 1), A("pcol"), m, Op.bitwise_and)
+    cp(A("pcf", 0, 6), A("pci", 0, 6))
+
+    def pf(k):
+        return A("pcf", k, k + 1)
+
+    def pk(k):
+        return A("pk", k, k + 1)
+    ts(A("pos"), A("k8"), pf(0), Op.add)
+    ts(A("ke"), A("k8"), pf(0), Op.add, 1025.0, Op.add)
+    ts(pk(0), pf(1), 128.0, Op.mult, pf(2), Op.add)
+    ts(pk(1), pf(1), 48.0, Op.mult, pf(2), Op.add)
+    ts(A("pcf", 8, 9), pf(3), -16.0, Op.mult, -40.0, Op.add)
+    ts(pk(6), pf(1), 32.0, Op.mult, pf(5), Op.add)
+    tt(pk(2), A("pcf", 8, 9), pk(1), Op.add)
+    ts(pk(3), pf(3), 8.0, Op.mult)
+    ts(pk(4), pf(3), -2.0, Op.mult, 1.0, Op.add)
+    ts(pk(5), pf(3), -1.0, Op.mult, 1.0, Op.add)
+    ts(pk(7), pf(0), 3.0, Op.is_gt)
+    ts(A("lane"), pf(0), 32.0, Op.mult, -128.0, Op.add)
+    cp(A("el", 0, 88), A("eli", 0, 88))
+    ts(A("el", 88, 92), A("eli", 88, 92), pf(5), Op.add)
+    ts(A("bl"), A("bli"), pf(4), Op.add)
+    ts(A("ll"), A("lli"), pk(6), Op.add)
+    act(A("fr"), A("fri"), 1.0)
+    for h in range(4):
+        for k, (a, b) in enumerate(((12, 20), (6, 9), (9, 12))):
+            act(A("fr", ST * h + a, ST * h + b), A("fri", ST * h + a, ST * h + b), 1.0, pk(k))
+    for a in (0, 11):
+        cp(A("own14", a, a + 3), A("fr", me + 6, me + 9), "s")
+    gat(A("ex", 1024, 1408), A("fr"), A("el", 0, 24), "s")
+    act(A("ein", 0, 384), A("ex", 1024, 1408), 0.0)
+    act(A("ein", 384, 448), A("ex", 1024, 1088), 0.0)
+    for h in others:
+        gat(A("ex", P * h, P * h + P), A("fr"), A("el", 24 + 16 * h, 40 + 16 * h), "s")
+
+    ts(A("xb"), A("xl"), 255, Op.bitwise_and)
+    ts(A("xc"), A("xl"), 7, Op.arith_shift_right, 1, Op.bitwise_and)
+    ts(A("emp"), A("xl", 0, 8), 0.0, Op.is_lt)
+    ts(A("xd"), A("xc"), -255.0, Op.mult)
+    tt(A("xt"), A("xl"), A("xb"), Op.add)
+    tt(A("we"), A("emp"), A("ke"), Op.mult)
+    tt(A("xp"), A("xt"), A("xd"), Op.add)
+    tt(A("p1"), A("we"), A("pos"), Op.add)
+    cp(A("land", me, me + 6, 2), A("xp", 8, 11))
+    cp(A("land", me + 1, me + 6, 2), A("xp", 11, 14))
+    tt(A("ss", 0, 6), A("xp", 8, 14), A("xp", 14, 20), Op.add)
+    tt(A("ss", 6, 14), A("xp", 0, 8), A("p1"), Op.add)
+    cp(A("land", me + 6, me + 20), A("ss"))
+    post("arrl", "lsl", [A("land", me, me + ST)] * 3, [A("land", me, me + ST)] * 3)
+    iota(A("vai", 0, 48), [[16, 3], [1, 8], [48, 2]], SLOTS)
+    iota(A("vai", 48, 176), [[16, 8], [1, 8], [128, 2]], SLOTS + V)
+    iota(A("vai", 176, 224), [[16, 3], [1, 8], [48, 2]], SLOTS)
+    iota(A("lst", 1, 385), [[0, 3], [1, 128]], 0)
+    iota(A("tab", 1024, 2048), [[2, 1024]], 3072)
+    iota(A("mv"), [[1, WIN]], 0)
+
+    own, zero = A("fr", me + 12, me + 20), float(OWN * r + 1)
+    ts(A("ne"), A("xl", 0, 8), 0.0, Op.is_ge)
+    ts(A("rk"), A("xl"), 8, Op.arith_shift_right)
+    tt(A("z1"), own, A("ne"), Op.mult)
+    ts(A("z2"), A("ne"), -zero, Op.mult, zero, Op.add)
+    tt(A("sm"), A("rk", 14, 17), A("rk", 8, 11), Op.is_equal)
+    cp(A("rke", 0, 3), A("rk", 8, 11))
+    tt(A("own14", 3, 11), A("z1"), A("z2"), Op.add)
+    cp(A("rke", 3, 11), A("rk", 0, 8))
+    ts(A("sm8"), A("sm"), 8.0, Op.mult)
+    tt(A("rke", 11, 14), A("rk", 14, 17), A("sm8"), Op.subtract)
+    act(A("dum"), A("dmi"), 1.0, pf(4))
+    cp(own, A("own14", 3, 11), "s")
+    for j, x in enumerate(others):
+        ts(A("msk", 14 * j, 14 * j + 14), A("rke"), float(x), Op.is_equal)
+    m3 = [A("msk", 14 * j, 14 * j + 14) for j in range(3)]
+    tt(A("any1"), m3[0], m3[1], Op.add)
+    for j in range(3):
+        tt(A("ein", 4 * j + 4, 448, 32), m3[j], A("own14"), Op.mult)
+    tt(A("any2"), A("any1"), m3[2], Op.add)
+    tt(A("ein", FLAG, 448, 32), A("any2"), A("own14"), Op.mult)
+    ts(A("mx"), A("mxi"), pf(4), Op.add, pk(5), Op.mult)
+    tr(A("dix"), A("ein"))
+    run("s", lambda e: e.activation(ap(A("fst")), ap(A("dix")), Act.Sign), [A("dix")], [A("fst")])
+    gat(A("ex", *mine), A("fr"), A("el", 24 + 16 * r, 40 + 16 * r), "s")
+    for j in range(3):
+        act(A("ex", mine[0] + 4 * j + 4, mine[1], 32), A("msk", 14 * j + 3, 14 * j + 11), -2.0, 1.0)
+    act(A("ex", mine[0] + FLAG, mine[1], 32), A("any2", 3, 11), -2.0, 1.0)
+    act(A("val"), A("vai"), 1.0, pk(3))
+    act(A("d0"), A("lst", 1, 353), 0.0, pk(7))
+    quant(A("qo"), A("qop"), A("cv"))
+    tt(A("fo1"), A("any2", 0, 3), A("dum", 0, 3), Op.mult)
+    scan(A("scs"), A("fst"), A("fst"), A("lane"), Op.add, Op.max)
+    tr(A("oss"), A("scs"))
+    tt(A("fo2"), A("dum", 0, 3), A("fo1"), Op.subtract)
+    for j in range(3):
+        tt(A("spm", 14 * j, 14 * j + 14), A("oss", 4 * j + 4, 448, 32), m3[j], Op.mult)
+    tt(A("b0a"), A("spm", 0, 14), A("spm", 14, 28), Op.add)
+    tt(A("b0"), A("b0a"), A("spm", 28, 42), Op.add)
+    tt(A("fo3"), A("b0", 0, 3), A("fo2"), Op.add)
+    tt(A("b1"), A("b0"), A("dum"), Op.subtract)
+    cp(A("fof", 0, 3), A("fo3"))
+    sca(A("lst"), A("fof", 0, 3), A("val", 0, 48))
+    order("y", [A("qo"), A("qop")], [])
+    g.sync.dma_start(T.q[:, 0:OWN].bitcast(dt.uint8), T.qo[:, 0:OWN].bitcast(dt.uint8)).then_inc(T.sem.own, 16)
+    g.sync.dma_start(T.qp[:, 0:OWN], T.qop[:, 0:OWN]).then_inc(T.sem.own, 16)
+    total["own"] = 32
+    note([], [A("q", 0, OWN), A("qp", 0, OWN)], ("own", 32, {}, "dma"))
+
+    arrive("arrl", [A("land", ST * x, ST * x + ST) for x in others])
+    cp(A("lf"), A("land"))
+    gat(A("ex", 0, 1024, 16), A("lf"), A("el", 88, 92))
+    for h in range(4):
+        cp(A("to0", 6 * h, 6 * h + 6), A("lf", ST * h, ST * h + 6), "s")
+    for h in range(4):
+        for k in range(2):
+            cp(A("ex", 1024 + 96 * h + 16 * k, 1120 + 96 * h, 32), A("lf", ST * h + 6 + 3 * k, ST * h + 9 + 3 * k), "s")
+    tr(A("tab", 0, 512), A("ex", 0, 512))
+    cp(A("tou"), A("to0"))
+    tr(A("tab", 512, 1024), A("ex", 512, 1024))
+    first, places = A("tab", 0, 1024), A("tab", 0, PLACES)
+
+    def spread(t, pairs):
+        order("y", [A("sn", P * t, P * t + P)], [A("sn", 0, P)])
+        for p in range(0, 128, 32):
+            for x, z in pairs:
+                g.sync.dma_start(T.sn[p + z:p + z + 1, 0:P], T.sn[p + x:p + x + 1, P * t:P * t + P]).then_inc(T.sem.sns, 16)
+                total["sns"] = total.get("sns", 0) + 16
+
+    gat(A("ga0", 192, 384), first, A("tou", 12, 24), "s")
+    gat(A("ga0", 0, 192), first, A("tou", 0, 12))
+    cp(A("tab", 2048, 3072), A("tab", 1024, 2048), "s")
+    tr(A("gt0"), A("ga0"))
+    tr(A("ev"), A("ex", 1024, 1408))
+    tt(A("ti1"), A("gt0", 0, 384, 16), A("to0"), Op.subtract)
+    cp(A("to1"), A("ti1"))
+    sca(first, A("tou"), A("ev"))
+    gat(A("ga1", 192, 384), places, A("to1", 12, 24), "s")
+    gat(A("ga1", 0, 192), places, A("to1", 0, 12))
+    cp(A("sn", 0, P), A("tab", *mine), "s")
+    tr(A("gt1"), A("ga1"))
+    tt(A("ti2"), A("gt1", 0, 384, 16), A("ti1"), Op.subtract)
+    cp(A("to2"), A("ti2"))
+    act(A("x2"), A("ti2"), pf(3))
+    act(A("y2"), A("ti2"), pk(4))
+    sca(places, A("to1"), A("ga0"))
+    gat(A("ga2", 256, 384), places, A("to2", 16, 24), "s")
+    tt(A("lcf"), A("x2"), A("mx"), Op.add)
+    gat(A("ga2", 0, 256), places, A("to2", 0, 16))
+    cp(A("lc"), A("lcf"))
+    cp(A("sn", P, 2 * P), A("tab", *mine), "s")
+    gat(A("gc"), A("tab"), A("lc"), "s")
+    tr(A("gt2"), A("ga2"))
+    ts(A("w1"), A("gt2", 0, 384, 16), pf(3), Op.mult)
+    tt(A("ti3"), A("w1"), A("y2"), Op.add)
+    cp(A("to3"), A("ti3"))
+    sca(places, A("to3"), A("gc"))
+    spread(1, ((10, 10), (26, 26)))
+
+    run("s", lambda e: e.activation(ap(A("un", 0, 256)), ap(A("tab", *mine)), Act.Relu, scale=-1.0), [A("tab", *mine)], [A("un", 0, 256)])
+    fo = A("land", me, me + 6)
+    run("v", lambda e: e.tensor_tensor(ap(A("un", 256, 352)), ap(first).indirect(ap(fo)), ap(A("dix", 352, 448)), Op.is_equal), [first, fo, A("dix", 352, 448)], [A("un", 256, 352)], True)
+    cp(A("sn", 2 * P, 3 * P), A("tab", *mine), "s")
+    spread(2, ((14, 14), (14, 30), (30, 15), (30, 31)))
+    note([A("sn", P, 3 * P)], [A("sn", 0, P)], ("sns", total["sns"], {}, "dma"))
+    pack(0, 128)
+    for h in range(4):
+        cp(A("m", OWN * h, OWN * h + OWN), A("mv", 0, OWN), "s")
+    scan(A("sc"), A("d0"), A("un"), 0.0, Op.mult, Op.add)
+    tr(A("osd"), A("sc"))
+    for j in range(3):
+        tt(A("cm", 11 * j, 11 * j + 11), A("osd", 4 * j + 4, 352, 32), A("msk", 14 * j + 3, 14 * j + 14), Op.mult)
+    tt(A("fl"), A("any2", 3, 14), A("osd", FLAG, 352, 32), Op.subtract)
+    tt(A("cs1"), A("cm", 0, 11), A("cm", 11, 22), Op.add)
+    tt(A("bb"), A("b1", 3, 14), A("cm", 22, 33), Op.subtract)
+    tt(A("cs2"), A("bb"), A("cs1"), Op.subtract)
+    tt(A("fb"), A("fl"), A("cs2"), Op.mult)
+    tt(A("of1"), A("fb"), A("dum", 3, 14), Op.add)
+    cp(A("ofd", 0, 11), A("of1"))
+    sca(A("lst"), A("ofd", 0, 11), A("val", 48, 224))
+    tr(A("olt"), A("lst", 1, 385))
+    tt(A("zb", 0, 12), A("olt", 0, 384, 32), A("olt", 16, 384, 32), Op.max)
+    tr(A("zt"), A("zb"))
+    gat(A("zg"), A("zt"), A("bl"))
+    tr(A("zh"), A("zg"))
+    gat(A("loff"), A("zh"), A("ll"))
+    lists = [A("loff", 8 * j, 8 * j + 7) for j in range(3)]
+    at = [sorted(y for y in range(N) if y != x).index(r) for x in others]
+    post("arrm", "lsm", [A("loff", 8 * j, 8 * j + 8) for j in range(3)], [A("lin", 8 * k, 8 * k + 8) for k in at])
+    for j in range(3):
+        pick(A("sq%d" % j), A("qo"), lists[j])
+        gat(A("sqp%d" % j), A("qop"), lists[j], "s")
+    land = [(OWN + SLOTS * k, OWN + SLOTS * k + SLOTS) for k in at]
+    post("arrq", "lsq", [A("sq%d" % j) for j in range(3)], [A("q", *x) for x in land])
+    post("arrp", "lsp", [A("sqp%d" % j) for j in range(3)], [A("qp", *x) for x in land])
+
+    tr(A("ts"), A("sn", 0, 256))
+    now = [A("ts", x, 256, 16) for x in (6, 10, 14, 15)]
+    tt(A("ne3"), now[3], now[1], Op.not_equal)
+    tt(A("df3"), now[3], now[2], Op.subtract)
+    cp(A("ido", 0, 16), now[0])
+    tt(A("pr3"), A("ne3"), A("df3"), Op.mult)
+    cp(A("ido", 16, 32), now[1])
+    tt(A("r3"), A("pr3"), now[2], Op.add)
+    cp(A("ido", 32, 48), now[2])
+    cp(A("ido", 48, 64), A("r3"))
+    pack(128, 640)
+    pack(640, 1024)
+    arrive("arrm", [A("lin", 8 * k, 8 * k + 8) for k in range(3)])
+    for k, x in enumerate(others):
+        sca(A("m", OWN * x, OWN * x + OWN), A("lin", 8 * k, 8 * k + 7), A("mv", OWN + SLOTS * k, OWN + SLOTS * k + SLOTS))
+
+    def look(t):
+        a = P * t
+        if t:
+            gat(A("mg", a, a + P), A("m"), A("ido", 16 * t, 16 * t + 16), "s")
+        else:
+            gat(A("mg", 128, 256), A("m"), A("ido", 8, 16), "s")
+            gat(A("mg", 0, 128), A("m"), A("ido", 0, 8))
+
+    def turn(t):
+        a = P * t
+        tr(A("om", a, a + P), A("mg", a, a + P))
+        cp(A("off", 16 * t, 16 * t + 16), A("om", a, a + P, 16))
+
+    arrive("arrq", [A("q", OWN, WIN)])
+    arrive("arrp", [A("qp", OWN, WIN)])
+
+    def table(t):
+        pick(A("k%d" % t), A("q"), A("off", 16 * t, 16 * t + 16))
+        gat(A("kp%d" % t), A("qp"), A("off", 16 * t, 16 * t + 16), "s")
+        for o in range(O):
+            i = O * t + o
+            wq, wp, kq, kp, z = A("wq", 128 * i, 128 * i + 128), A("wp", 128 * i, 128 * i + 128), A("k%d" % t), A("kp%d" % t), A("ps", 512 * i, 512 * i + P)
+            run("t", lambda e: e.matmul_mx(ap(z), ap(wq), ap(wp), ap(kq), ap(kp), True, True), [wq, wp, kq, kp], [z])
+
+    def out(t):
+        for o in range(O):
+            i = O * t + o
+            for b in range(2):
+                cp(A("ys", P * i + 128 * b, P * i + 128 * b + 128), A("ps", 512 * i + b, 512 * i + P, 2), "s" if t < 1 else "vs"[o])
+            reg = A("ys", P * i, P * i + P)
+            order("y", [reg], [])
+            g.sync.dma_start(T.y[:, P * i:P * i + P], ap(reg)).then_inc(T.sem.sty, 16)
+            total["sty"] = total.get("sty", 0) + 16
+    look(0)
+    look(1)
+    look(2)
+    turn(0)
+    turn(1)
+    table(0)
+    look(3)
+    turn(2)
+    table(1)
+    turn(3)
+    out(0)
+    table(2)
+    out(1)
+    table(3)
+    out(2)
+    out(3)
+    for q in ("v", "s", "t", "g"):
+        total[sem_of[q]] = cnt[sem_of[q]]
+    for s in SEMAPHORES:
+        if s in total:
+            g.wait_ge(T.sem[s], total[s])

@@ -3,12 +3,19 @@ from concourse.mybir import dt, AluOpType as Op, ActivationFunctionType as Act
 
 N, P, V, R, O = 4, 256, 96, 4, 2
 SLOTS = 112
-OWN = SLOTS + V + P
+IDS = P + V
+OWN = IDS + 32
 WIN = OWN + 3 * SLOTS
-ST = 24
-FLAG = 2
-PLACES = 3072
+ST, MS = 20, 11
+SHI, SLO, IHI, ILO = 0, 8, 1, 9
+FLAG, ONE = 2, 18
+PLACES = 3088
+MIRROR = 2048.0
+MID = 176
+ZID = N * IDS
+TINY = 2.0 ** -24
 F32, I32, U16, BF, CODE, PL = "float32", "int32", "uint16", "bfloat16", "float8_e4m3fn_x4", "uint8"
+CYCLE, FLOOR, WAKE, PICK, PUT, DMA, HOP = 0.001, 64, 0.12, 1.5, 3.8, 2.0, 2.0
 
 
 def _s(n, t):
@@ -16,42 +23,75 @@ def _s(n, t):
 
 
 SCRATCH = {
-    "xl": _s(20, I32), "pcol": _s(1, I32), "pci": _s(7, I32), "pcf": _s(9, F32), "pk": _s(8, F32), "lane": _s(1, F32),
-    "k8": _s(8, F32), "pos": _s(8, F32), "ke": _s(8, F32), "xi": _s(120, I32), "xf": _s(48, F32), "ss": _s(14, F32),
-    "land": _s(4 * ST, U16), "dd": _s(8 * ST, F32), "fri": _s(4 * ST, F32),
-    "eli": _s(92, F32), "el": _s(92, U16), "ex": _s(1408, F32), "tab": _s(PLACES + 384, F32), "ev": _s(384, F32), "to0": _s(24, F32), "tou": _s(24, U16),
-    "gc": _s(384, F32), "mxi": _s(24, F32), "mx": _s(24, F32), "x2": _s(24, F32), "y2": _s(24, F32), "lcf": _s(24, F32), "lc": _s(24, U16), "w1": _s(24, F32),
-    "ne3": _s(16, F32), "df3": _s(16, F32), "pr3": _s(16, F32), "r3": _s(16, F32),
-    "dmi": _s(14, F32), "dum": _s(14, F32), "vai": _s(224, F32), "val": _s(224, F32),
-    "bli": _s(4, F32), "bl": _s(4, U16), "lli": _s(2, F32), "ll": _s(2, U16),
-    "rke": _s(14, F32), "sm": _s(3, F32), "sm8": _s(3, F32), "own14": _s(14, F32), "msk": _s(42, F32), "any1": _s(14, F32), "any2": _s(14, F32),
-    "ein": _s(448, F32), "dix": _s(448, F32), "fst": _s(448, F32), "scs": _s(448, F32), "d0": _s(352, F32),
-    "oss": _s(448, F32), "spm": _s(42, F32), "b0a": _s(14, F32), "b0": _s(14, F32), "b1": _s(14, F32),
-    "fo1": _s(3, F32), "fo2": _s(3, F32), "fo3": _s(3, F32), "fof": _s(4, U16), "lst": _s(616, F32),
-    "un": _s(352, F32), "sc": _s(352, F32), "osd": _s(352, F32), "cm": _s(33, F32), "cs1": _s(11, F32), "cs2": _s(11, F32),
-    "fl": _s(11, F32), "bb": _s(11, F32), "fb": _s(11, F32), "of1": _s(11, F32), "ofd": _s(12, U16),
-    "olt": _s(384, F32), "zb": _s(32, F32), "zt": _s(32, F32), "zg": _s(64, F32), "zh": _s(64, F32), "loff": _s(32, U16),
-    "lin": _s(24, U16), "mv": _s(WIN, F32), "m": _s(4 * OWN, F32),
-    "sn": _s(768, F32), "ts": _s(256, F32), "ido": _s(64, U16), "mg": _s(1024, F32), "om": _s(1024, F32), "off": _s(64, U16),
+    "xl": _s(28, I32), "xa": _s(32, I32), "z": _s(96, F32), "zc": _s(96, F32), "gl": _s(2, U16), "r32": _s(16, F32),
+    "pci": _s(8, I32), "pcf": _s(16, F32), "pos8": _s(8, F32), "minc": _s(32, F32), "gg": _s(48, F32), "rec": _s(ST, U16),
+    "land": _s(N * ST, U16), "lf": _s(N * ST, F32), "ramp": _s(16, F32), "el": _s(20, U16), "ex": _s(1440, BF), "tab": _s(PLACES, BF),
+    "svf": _s(24, F32), "ev": _s(384, BF), "rk": _s(16, I32), "rkf": _s(14, F32), "ne2": _s(3, F32), "msk": _s(112, F32), "wt": _s(88, F32),
+    "a1": _s(14, F32), "any": _s(14, F32), "u1": _s(14, F32), "u2": _s(14, F32), "occ": _s(8, F32), "hm": _s(8, F32), "hz": _s(8, F32),
+    "kp": _s(3, F32), "einv": _s(192, BF), "dv": _s(192, BF), "d0": _s(P, BF), "d8": _s(112, F32), "scs": _s(448, BF), "oss": _s(448, BF),
+    "pr": _s(112, F32), "sm": _s(112, F32), "c0": _s(14, F32), "kk": _s(14, F32), "b1": _s(14, F32), "b2": _s(14, F32),
+    "dum": _s(14, F32), "dm": _s(14, F32), "adm": _s(14, F32), "stat": _s(14, F32), "fo": _s(4, U16),
+    "vai": _s(176, F32), "val": _s(176, BF), "k0": _s(V, F32), "k1": _s(V, BF), "lst": _s(4000, BF), "ma0": _s(48, F32), "ma": _s(48, F32), "mb": _s(48, F32), "mp": _s(48, F32),
+    "msg": _s(48, BF), "landm": _s(N * MS, BF), "un": _s(V, BF), "sc": _s(IDS, BF), "osd": _s(IDS, BF), "pd": _s(88, F32), "sd": _s(88, F32), "ofd": _s(12, U16),
+    "olt": _s(IDS, BF), "zb": _s(32, BF), "zt": _s(32, BF), "zg": _s(64, BF), "zh": _s(64, BF), "loff": _s(32, U16),
+    "m": _s(1440, BF), "sn": _s(P, BF), "ts": _s(P, BF), "idf": _s(8, F32), "was": _s(16, F32), "ne3": _s(8, F32), "df3": _s(8, F32), "pr3": _s(8, F32),
+    "ido": _s(16, U16), "mg": _s(P, BF), "om": _s(P, BF), "sl": _s(64, F32), "off": _s(64, U16),
     "cv": _s(4 * OWN, BF), "qo": _s(OWN, CODE), "qop": _s(OWN, PL), "q": _s(WIN, CODE), "qp": _s(WIN, PL),
+    "sq": _s(3 * SLOTS, CODE), "sqp": _s(3 * SLOTS, PL),
     "wb": _s(4096, BF), "wq": _s(1024, CODE), "wp": _s(1024, PL), "ys": _s(2048, F32),
-    "ga0": _s(384, F32), "ga2": _s(384, F32),
     "ps": ("psum", [128, 4096], F32),
 }
 for _t in range(3):
-    SCRATCH["gt%d" % _t] = _s(384, F32)
-    SCRATCH["ti%d" % (_t + 1)] = _s(24, F32)
-    SCRATCH["to%d" % (_t + 1)] = _s(24, U16)
-    SCRATCH["sq%d" % _t] = _s(SLOTS, CODE)
-    SCRATCH["sqp%d" % _t] = _s(SLOTS, PL)
+    SCRATCH["ga%d" % _t] = _s(384, BF)
+    SCRATCH["gt%d" % _t] = _s(384, BF)
+    SCRATCH["ta%d" % _t] = _s(24, F32)
+    SCRATCH["ti%d" % _t] = _s(24, F32)
+    SCRATCH["to%d" % _t] = _s(24, U16)
+SCRATCH["ti3"] = _s(24, F32)
 for _t in range(4):
-    SCRATCH["k%d" % _t] = _s(P, CODE)
-    SCRATCH["kp%d" % _t] = _s(P, PL)
-PART = {n: ("xi", 20 * k, 20) for k, n in enumerate(["xb", "xc", "xd", "xt", "xp", "rk"])}
-PART.update({n: ("xf", 8 * k, 8) for k, n in enumerate(["emp", "p1", "we", "ne", "z1", "z2"])})
-PART.update({"ga1": ("tab", PLACES, 384), "lf": ("dd", 0, 4 * ST), "fr": ("dd", 4 * ST, 4 * ST)})
+    SCRATCH["k%dq" % _t] = _s(P, CODE)
+    SCRATCH["k%dp" % _t] = _s(P, PL)
 
-SEMAPHORES = ["sv", "ss", "st", "sg", "ldx", "ldv", "ldc", "ldw0", "ldw1", "arrl", "arrm", "arrq", "arrp", "lsl", "lsm", "lsq", "lsp", "sty", "own", "sns"]
+SEMAPHORES = ["sv", "ss", "st", "sg", "ldx", "ldc", "ldw0", "ldw1", "arrl", "arrm", "arrq", "arrp", "lsl", "lsm", "lsq", "lsp", "sty", "own"]
+
+
+def clash(a, b):
+    if a[0] != b[0] or a[1] >= b[2] or b[1] >= a[2] or a[4] >= b[5] or b[4] >= a[5]:
+        return False
+    return not (a[3] == b[3] and a[3] > 1 and (a[1] - b[1]) % a[3])
+
+
+def in_order(calls):
+    seen = {}
+    for k, c in enumerate(calls):
+        c["after"] = set()
+        for regs, w in ((c["reads"], False), (c["writes"], True)):
+            for x in regs:
+                c["after"] |= {j for y, w2, j in seen.get(x[0], []) if (w or w2) and clash(x, y)}
+        for regs, w in ((c["reads"], False), (c["writes"], True)):
+            for x in regs:
+                seen.setdefault(x[0], []).append((x, w, k))
+    chain = [c["hold"] + c["late"] for c in calls]
+    for k in reversed(range(len(calls))):
+        for j in calls[k]["after"]:
+            chain[j] = max(chain[j], calls[j]["hold"] + calls[j]["late"] + WAKE + chain[k])
+        for j in calls[k]["also"]:
+            chain[j] = max(chain[j], calls[j]["hold"] + chain[k])
+    done, free, left, out = {}, {}, set(range(len(calls))), []
+    while left:
+        start = {k: max([free.get(calls[k]["q"], 0.0)] + [done[j] + WAKE for j in calls[k]["after"]] + [done[j] - calls[j]["late"] for j in calls[k]["also"]])
+                 for k in left if calls[k]["after"] | set(calls[k]["also"]) <= set(done)}
+        best = []
+        for q in {calls[k]["q"] for k in start}:
+            mine = sorted((k for k in start if calls[k]["q"] == q), key=lambda k: (-chain[k], k))
+            fits = [k for k in mine if start[k] + calls[k]["hold"] <= start[mine[0]] + WAKE / 4]
+            best.append((fits + mine)[0])
+        k = min(best, key=lambda k: (start[k], k))
+        free[calls[k]["q"]] = start[k] + calls[k]["hold"]
+        done[k] = start[k] + calls[k]["hold"] + calls[k]["late"]
+        left.remove(k)
+        out.append(calls[k])
+    return out
 
 
 def rank_program(g, core, T, topo):
@@ -61,117 +101,90 @@ def rank_program(g, core, T, topo):
     others = [x for x in range(N) if x != r]
     eng = {"v": g.vector, "s": g.scalar, "t": g.tensor, "g": g, "y": g.sync}
     sem_of = {"v": "sv", "s": "ss", "t": "st", "g": "sg"}
-    cnt, known, log, total = {}, {k: {} for k in eng}, {}, {}
+    calls = []
 
-    def clash(a, b):
-        if a[0] >= b[1] or b[0] >= a[1]:
-            return False
-        return not (a[2] == b[2] and a[2] > 1 and (a[0] - b[0]) % a[2])
-
-    def wait(q, tok):
-        s, v, clock, _ = tok
-        if known[q].get(s, 0) >= v:
-            return
-        eng[q].wait_ge(T.sem[s], v)
-        for k, x in list(clock.items()) + [(s, v)]:
-            known[q][k] = max(known[q].get(k, 0), x)
-
-    def order(q, reads, writes):
-        need = []
-        for regs, w in ((reads, False), (writes, True)):
-            for n, lo, hi, st in regs:
-                for l2, h2, s2, w2, tok in log.get(n, []):
-                    if not (w or w2) or not clash((lo, hi, st), (l2, h2, s2)):
-                        continue
-                    if w and not w2 and tok[3] == q:
-                        continue
-                    need.append(tok)
-        for tok in sorted(need, key=lambda t: -t[1]):
-            wait(q, tok)
-
-    def note(reads, writes, tok):
-        for regs, w in ((reads, False), (writes, True)):
-            for n, lo, hi, st in regs:
-                log.setdefault(n, []).append((lo, hi, st, w, tok))
-
-    def run(q, call, reads, writes, listed=False):
-        order(q, reads, writes)
-        s = sem_of[q]
-        cnt[s] = cnt.get(s, 0) + 1
-        call(eng[q]).then_inc(T.sem[s], 1)
-        note(reads, writes, (s, cnt[s], dict(known[q]), "list" if listed else q))
-
-    def load(q, sem, tot, out, in_, region):
-        eng[q].dma_start(out, in_).then_inc(T.sem[sem], 16)
-        total[sem] = tot
-        note([], [region], (sem, tot, {}, "dma"))
+    def add(q, go, reads, writes, hold, late=0.0, sem=None, n=0, also=()):
+        calls.append(dict(q=q, go=go, reads=list(reads), writes=list(writes), hold=hold, late=late, sem=sem, n=n, also=also))
+        return len(calls) - 1
 
     def ap(x):
-        n, lo, hi, st = x
-        return T[n][:, lo:hi] if st == 1 else T[n][:, lo:hi:st]
+        n, lo, hi, st, p0, p1 = x
+        return T[n][p0:p1, lo:hi] if st == 1 else T[n][p0:p1, lo:hi:st]
+
+    def raw(x):
+        return ap(x).bitcast(dt.uint8) if SCRATCH[x[0]][2] == CODE else ap(x)
 
     def A(n, lo=0, hi=None, st=1):
-        if n in PART:
-            b, o, w = PART[n]
-            return (b, o + lo, o + (w if hi is None else hi), st)
-        return (n, lo, SCRATCH[n][1][1] if hi is None else hi, st)
+        return (n, lo, SCRATCH[n][1][1] if hi is None else hi, st, 0, 128)
 
-    def sc_(x):
-        return ap(x) if isinstance(x, tuple) else x
+    def on(x, p0, p1):
+        return x[:4] + (p0, p1)
+
+    def quad(x, k):
+        return on(x, 32 * k, 32 * k + 32)
+
+    def wide(x):
+        return len(range(x[1], x[2], x[3]))
+
+    def run(q, call, reads, out, per=1.0, by=None):
+        if by is not None:
+            hold = 0.06 + 16 * wide(by) * per * CYCLE
+        else:
+            short = per < 2 and q == "v" and all(SCRATCH[x[0]][2] in (BF, U16) for x in reads[:1] + [out])
+            hold = max(FLOOR, wide(out) * (0.5 if short else per)) * CYCLE
+        add(q, lambda: call(eng[q]).then_inc(T.sem[sem_of[q]], 1), reads + aps(by), [out], hold)
+
+    def load(q, sem, pairs, reads=(), writes=None, late=DMA, also=()):
+        def go():
+            for k, (o, i) in enumerate(pairs):
+                eng[q[k % len(q)]].dma_start(o, i).then_inc(T.sem[sem], 16)
+        return add(q[0], go, reads, writes, 0.06 * len(pairs), late, sem, 16 * len(pairs), also)
+
+    def sc_(x, like):
+        return ap(on(x, like[4], like[5])) if isinstance(x, tuple) else x
 
     def aps(*xs):
         return [x for x in xs if isinstance(x, tuple)]
 
-    def tt(out, a, b, op):
-        run("v", lambda e: e.tensor_tensor(ap(out), ap(a), ap(b), op), [a, b], [out])
+    def via(a, by):
+        return ap(a) if by is None else ap(a).indirect(ap(by))
 
-    def ts(out, a, s1, op, s2=None, op1=None):
-        if op1 is None:
-            run("v", lambda e: e.tensor_scalar(ap(out), ap(a), sc_(s1), None, op), [a] + aps(s1), [out])
-        else:
-            run("v", lambda e: e.tensor_scalar(ap(out), ap(a), sc_(s1), sc_(s2), op, op1), [a] + aps(s1, s2), [out])
+    def tt(out, a, b, op, by=None):
+        run("v", lambda e: e.tensor_tensor(ap(out), via(a, by), ap(b), op), [a, b], out, 2.0 if by is None else PICK, by)
 
-    def cp(out, a, q="v"):
+    def ts(out, a, s1, op, s2=None, op1=None, by=None):
+        more = () if op1 is None else (op1,)
+        run("v", lambda e: e.tensor_scalar(ap(out), via(a, by), sc_(s1, a), sc_(s2, a), op, *more), [a] + aps(s1, s2), out, 1.0 if by is None else PICK, by)
+
+    def cp(out, a, q="v", by=None):
         if q == "v":
-            run("v", lambda e: e.tensor_copy(ap(out), ap(a)), [a], [out])
+            run("v", lambda e: e.tensor_copy(ap(out), via(a, by)), [a], out, 1.0 if by is None else PICK, by)
         else:
-            run("s", lambda e: e.activation(ap(out), ap(a), Act.Copy), [a], [out])
+            run("s", lambda e: e.activation(ap(out), via(a, by), Act.Copy), [a], out, 1.0 if by is None else PICK, by)
 
     def act(out, a, scale, bias=0.0):
-        run("s", lambda e: e.activation(ap(out), ap(a), Act.Identity, bias=sc_(bias), scale=sc_(scale)), [a] + aps(scale, bias), [out])
+        run("s", lambda e: e.activation(ap(out), ap(a), Act.Identity, bias=sc_(bias, a), scale=sc_(scale, a)), [a] + aps(scale, bias), out)
 
     def tr(out, a):
-        run("v", lambda e: e.transpose(ap(out), ap(a)), [a], [out])
+        run("v", lambda e: e.transpose(ap(out), ap(a)), [a], out)
 
-    def scan(out, a, b, start, op0, op1):
-        run("v", lambda e: e.tensor_tensor_scan(ap(out), ap(a), ap(b), sc_(start), op0, op1), [a, b] + aps(start), [out])
+    def scan(out, a, b):
+        run("v", lambda e: e.tensor_tensor_scan(ap(out), ap(a), ap(b), 0.0, Op.mult, Op.add), [a, b], out)
 
     def fill(out, c):
-        run("v", lambda e: e.memset(ap(out), c), [], [out])
-
-    def gat(out, win, off, q="v"):
-        if q == "v":
-            run("v", lambda e: e.tensor_copy(ap(out), ap(win).indirect(ap(off))), [win, off], [out], True)
-        else:
-            run("s", lambda e: e.activation(ap(out), ap(win).indirect(ap(off)), Act.Copy), [win, off], [out], True)
+        run("v", lambda e: e.memset(ap(out), c), [], out)
 
     def sca(win, off, a):
-        run("v", lambda e: e.tensor_copy(ap(win).indirect(ap(off)), ap(a)), [off, a], [win])
+        run("v", lambda e: e.tensor_copy(via(win, off), ap(a)), [a], win, PUT, off)
 
     def pick(out, win, off):
-        run("v", lambda e: e.tensor_copy(ap(out).bitcast(dt.uint32), ap(win).bitcast(dt.uint32).indirect(ap(off))), [win, off], [out], True)
+        run("v", lambda e: e.tensor_copy(ap(out).bitcast(dt.uint32), ap(win).bitcast(dt.uint32).indirect(ap(off))), [win], out, PICK, off)
 
     def quant(c, p, a):
-        run("v", lambda e: e.quantize_mx(ap(c), ap(p), ap(a)), [a], [c, p])
+        add("v", lambda: g.vector.quantize_mx(ap(c), ap(p), ap(a)).then_inc(T.sem.sv, 1), [a], [c, p], 0.27 * wide(a) * CYCLE)
 
     def iota(out, pattern, base, mult=0):
-        if SCRATCH[out[0]][2] == F32:
-            run("g", lambda e: e.iota(ap(out), pattern, base, mult, allow_small_or_imprecise_dtypes=True), [], [out])
-        else:
-            run("g", lambda e: e.iota(ap(out), pattern, base, mult), [], [out])
-
-    def pack(a, b):
-        quant(A("wq", a, b), A("wp", a, b), A("wb", 4 * a, 4 * b))
+        add("g", lambda: g.iota(ap(out), pattern, base, mult, allow_small_or_imprecise_dtypes=True).then_inc(T.sem.sg, 1), [], [out], 0.13 + 2 * wide(out) * CYCLE)
 
     picked, engs = [], {}
     for x in sorted(others, key=lambda x: len(topo.engines(core, T.cores[x]))):
@@ -179,319 +192,288 @@ def rank_program(g, core, T, topo):
         picked += e
         engs[x] = e
 
-    def post(sem, lsem, srcs, dsts):
-        order("g", srcs, [])
-        trs = []
-        for j, x in enumerate(others):
-            rid, pid, _ = topo.addr(T.cores[x])
-            s, d = ap(srcs[j]), ap(dsts[j])
-            if SCRATCH[srcs[j][0]][2] == CODE:
-                s, d = s.bitcast(dt.uint8), d.bitcast(dt.uint8)
-            trs.append(RemoteDMATransfer(dst_ids=[DstId(rid=rid, pnc=pid)], dma_engine_mask=sum(1 << k for k in engs[x]), remote_sem=T.sem[sem], src=s, dst=d))
-        g.remote_dma_fused(trs, local_sem=T.sem[lsem])
-        total[lsem] = sum(len(engs[x]) for x in others)
+    def post(sem, lsem, srcs, dsts, lands, late=HOP, also=()):
+        def go():
+            trs = []
+            for j, x in enumerate(others):
+                rid, pid, _ = topo.addr(T.cores[x])
+                trs.append(RemoteDMATransfer(dst_ids=[DstId(rid=rid, pnc=pid)], dma_engine_mask=sum(1 << k for k in engs[x]), remote_sem=T.sem[sem], src=raw(srcs[j]), dst=raw(dsts[j])))
+            g.remote_dma_fused(trs, local_sem=T.sem[lsem])
+        k = add("g", go, srcs, [], 0.4, 0.0, lsem, 12, also)
+        add("far", None, [], lands, 0.0, late, sem, 12, [k])
+        return k
 
-    def arrive(sem, regions):
-        total[sem] = 4 * len(others)
-        note([], regions, (sem, 4 * len(others), {}, "far"))
+    def turn(x, y):
+        return [h for h in range(N) if h != x].index(y)
+    afar = [x for x in ((0, r), (r + 1, N)) if x[0] < x[1]]
+    mine, myv = (P * r, P * r + P), (1024 + V * r, 1024 + V * r + V)
 
-    jobs = []
-    for b in range(4):
-        jobs.append((T.xl[32 * b:32 * b + 32, 8:11], T.f1[:, :]))
-        jobs.append((T.xl[32 * b:32 * b + 32, 14:17], T.f2[:, :]))
-        jobs.append((T.xl[32 * b:32 * b + 32, 0:8], T.alt[:, :]))
-    for n, c in ((T.f1, 11), (T.f2, 17)):
-        for b in range(3):
-            jobs.append((T.xl[32 * b + 16:32 * b + 48, c:c + 3], n[:, :]))
-        jobs.append((T.xl[0:16, c:c + 3], n[8:16, :]))
-        jobs.append((T.xl[112:128, c:c + 3], n[0:8, :]))
-    for k, (o, i) in enumerate(jobs):
-        eng["ys"[k % 2]].dma_start(o, i).then_inc(T.sem.ldx, 16)
-    total["ldx"] = 16 * len(jobs)
-    note([], [A("xl")], ("ldx", 16 * len(jobs), {}, "dma"))
-    load("y", "ldv", 16, T.cv[:, 4 * SLOTS:4 * SLOTS + 4 * V], T.v[:, :], A("cv", 4 * SLOTS, 4 * SLOTS + 4 * V))
-    load("y", "ldc", 16, T.cv[:, 4 * SLOTS + 4 * V:4 * OWN], T.c[:, :], A("cv", 4 * SLOTS + 4 * V, 4 * OWN))
-    for k in range(2):
-        load("y", "ldw%d" % k, 16, T.wb[:, 2048 * k:2048 * k + 2048], T.w[:, 2048 * k:2048 * k + 2048], A("wb", 2048 * k, 2048 * k + 2048))
+    load("ys", "ldx", [(T.xl[16 * o:16 * o + 16, a:b], n[:, :]) for n, a, b in ((T.alt, 0, 16), (T.f2, 16, 22), (T.f1, 22, 28)) for o in range(2)], [], [quad(A("xl"), 0)], 1.3)
 
-    iota(A("pcol"), [[0, 1]], 0, 1)
-    iota(A("k8"), [[32, 8]], P * r)
-    iota(A("fri"), [[OWN, 4], [16, ST]], 16)
-    iota(A("eli", 0, 24), [[ST, 4], [1, 3], [3, 2]], 6)
-    iota(A("eli", 24, 88), [[ST, 4], [1, 8], [0, 2]], 12)
-    iota(A("eli", 88, 92), [[ST, 4]], 12)
-    iota(A("bli"), [[16, 2], [0, 2]], 0)
-    iota(A("lli"), [[8, 2]], 0)
-    iota(A("dmi"), [[16, 14]], 385)
-    iota(A("mxi"), [[16, 24]], PLACES)
-    me, mine = ST * r, (P * r, P * r + P)
-    fill(A("land", me + 20, me + 24), 0)
-    fill(A("cv", 0, 4 * SLOTS), 0.0)
-    fill(A("zb"), 0.0)
-    for k, (sh, m) in enumerate([(0, 31), (0, 1), (1, 15), (4, 1), (0, 15), (1, 7)]):
-        if sh:
-            ts(A("pci", k, k + 1), A("pcol"), sh, Op.arith_shift_right, m, Op.bitwise_and)
-        else:
-            ts(A("pci", k, k + 1), A("pcol"), m, Op.bitwise_and)
-    cp(A("pcf", 0, 6), A("pci", 0, 6))
+    iota(A("z", 0, 16), [[-6, 2], [1, 8]], 22)
+    iota(A("z", 16, 32), [[-6, 2], [2, 4], [-1, 2]], 23)
+    iota(A("z", 32, 64), [[1, 2], [2, 16]], 0)
+    iota(A("z", 64, 96), [[1, 32]], 0)
+    iota(A("r32"), [[32, 16]], 0)
+    for a in range(0, 1440, 288):
+        fill(A("ex", a, a + 288), 0.0)
+    fill(A("xa"), 0)
+    fill(A("minc"), 4096.0)
+    iota(A("ex", IHI, 1024, 16), [[IDS, 4], [32, 8], [0, 2]], 0)
+    iota(A("ex", 1024 + IHI, 1408, 16), [[IDS, 4], [32, 3], [0, 2]], P)
+    iota(A("ramp"), [[1, 16]], 0)
+    iota(A("vai"), [[32, 11], [1, 16]], -MID)
+    iota(A("k0"), [[1, V]], 1)
+    tr(A("zc"), A("z"))
+    cp(A("gl"), A("zc", 0, 64, 32))
+    i32 = A("zc", 64, 65)
+    ts(A("pos8"), A("r32", 0, 8), i32, Op.add, float(P * r), Op.add)
+    ts(A("minc", 16, 24), A("r32", 0, 8), i32, Op.add, float(P * r + 1024), Op.add)
+    cp(A("pci", 0, 1), i32)
+    for k, (sh, m) in enumerate([(0, 15), (0, 16), (1, 7), (0, 1)]):
+        ts(A("pci", k + 1, k + 2), A("pci", 0, 1), sh, Op.arith_shift_right, m, Op.bitwise_and)
+    cp(A("pcf", 0, 4), A("pci", 1, 5))
+    i16, o16, half, odd, xor0, xor16, lanes, sel0, ll0, isone, tiny = [A("pcf", k, k + 1) for k in range(11)]
+    ts(xor0, o16, -2.0, Op.mult, 16.0, Op.add)
+    tt(xor16, xor0, i32, Op.add)
+    ts(lanes, i32, float(FLAG + 12), Op.is_lt)
+    ts(sel0, i16, 10.0, Op.min, 8.0, Op.mult)
+    ts(ll0, odd, 32.0, Op.mult, half, Op.add)
+    ts(isone, i32, float(ONE), Op.is_equal)
+    ts(tiny, i32, float(ONE), Op.not_equal, TINY, Op.mult)
+    ts(A("el", 0, 3), A("ramp", 0, 3), float(ST), Op.mult, half, Op.add)
+    if r + 1 < N:
+        ts(A("el", 4, 3 + N - r), A("ramp", r + 1, N), float(ST), Op.mult, half, Op.add)
+    ts(sel0, sel0, 7.0, Op.add)
+    ts(A("el", 8, 11), A("ramp", 0, 3), 0.0, Op.mult, sel0, Op.add)
+    ts(A("el", 12, 16, 2), A("ramp", 0, 2), 16.0, Op.mult, i16, Op.add)
+    ts(A("el", 13, 16, 2), A("ramp", 0, 2), 16.0, Op.mult, i16, Op.add)
+    ts(A("el", 16, 18), A("ramp", 0, 2), 8.0, Op.mult, ll0, Op.add)
+    cp(A("el", 18, 19), A("zc", 32, 33))
+    for a in range(1024, PLACES, 344):
+        act(A("tab", a, a + 344), A("ex", 0, 344), 0.0, MIRROR)
+    act(A("ex", ILO, 1408, 16), A("vai", 0, 88), 0.0, i32)
+    act(A("ex", 1024 + 16 + ILO, 1408, 32), A("r32", 0, 12), 0.0, xor16)
+    act(A("ex", ONE, 1408, 32), A("vai", 0, 44), 0.0, 1.0)
+    act(A("d0"), A("tab", 1024, 1024 + P), 0.0, lanes)
+    act(A("d8"), A("vai", 0, 112), 0.0, 1.0)
+    act(A("d8", 0, 112, 8), A("r32", 0, 14), 0.0)
+    act(A("val"), A("vai"), 1.0, o16)
+    act(A("k1"), A("k0"), tiny, isone)
+    act(A("msk"), A("vai", 0, 112), 0.0)
+    act(A("wt"), A("vai", 0, 88), 0.0)
+    act(A("c0", 0, 8), A("r32", 0, 8), 0.0, 1.0 - 3 * SLOTS)
+    act(A("c0", 8, 14), A("r32", 0, 6), 0.0, -4.0 * SLOTS)
+    act(A("ma0"), A("vai", 0, 48), 0.0)
+    act(A("mb"), A("vai", 0, 48), 0.0, 1.0)
+    act(A("zb"), A("vai", 0, 32), 0.0, -float(MID))
+    act(A("hm"), A("r32", 0, 8), 1.0, float(IDS * r - ZID))
+    ts(A("kp"), A("r32", 0, 3), i32, Op.add, 1.0, Op.add)
+    act(A("kp"), A("kp"), TINY)
+    ts(A("kk"), A("r32", 0, 14), i32, Op.add, 2.0, Op.mult)
+    fill(A("einv"), 0.0)
+    act(A("einv", ONE, 192, 32), A("r32", 0, 6), 0.0, 1.0)
+    fill(A("cv", 4 * IDS, 4 * OWN), 0.0)
+    fill(A("lst", 0, IDS), -float(MID))
 
-    def pf(k):
-        return A("pcf", k, k + 1)
+    for k in range(4):
+        ts(quad(A("xa", 0, 28), k), quad(A("xl"), 0), 2047, Op.bitwise_and)
+    tt(A("gg", 14, 46), A("xa"), A("minc"), Op.min, A("gl"))
+    tt(A("gg", 0, 8), A("gg", 30, 38), A("pos8"), Op.add)
+    tt(A("gg", 8, 14), A("gg", 14, 20), A("gg", 22, 28), Op.add)
+    cp(A("rec"), A("gg", 0, ST))
+    post("arrl", "lsl", [A("rec")] * 3, [A("land", ST * r, ST * r + ST)] * 3, [A("land", ST * x, ST * x + ST) for x in others], HOP + 0.8)
+    k = load("y", "ldc", [(T.cv[:, 4 * P:4 * IDS], T.v[:, :]), (T.cv[:, 0:4 * P], T.c[:, :])], [], [A("cv", 0, 4 * IDS), A("rec", 0, 8)], 3.5)
+    for h in range(2):
+        k = load("y", "ldw%d" % h, [(T.wb[:, 2048 * h:2048 * h + 2048], T.w[:, 2048 * h:2048 * h + 2048])], [], [A("wb", 2048 * h, 2048 * h + 2048)], 5.0 + 2 * h, [k])
+    for a in range(0, OWN, 128):
+        quant(A("qo", a, a + 128), A("qop", a, a + 128), A("cv", 4 * a, 4 * a + 512))
+    load("y", "own", [(raw(A("q", 0, OWN)), raw(A("qo"))), (raw(A("qp", 0, OWN)), raw(A("qop")))], [A("qo"), A("qop")], [A("q", 0, OWN), A("qp", 0, OWN)])
+    for a in range(0, 1024, 128):
+        quant(A("wq", a, a + 128), A("wp", a, a + 128), A("wb", 4 * a, 4 * a + 512))
 
-    def pk(k):
-        return A("pk", k, k + 1)
-    ts(A("pos"), A("k8"), pf(0), Op.add)
-    ts(A("ke"), A("k8"), pf(0), Op.add, 1025.0, Op.add)
-    ts(pk(0), pf(1), 128.0, Op.mult, pf(2), Op.add)
-    ts(pk(1), pf(1), 48.0, Op.mult, pf(2), Op.add)
-    ts(A("pcf", 8, 9), pf(3), -16.0, Op.mult, -40.0, Op.add)
-    ts(pk(6), pf(1), 32.0, Op.mult, pf(5), Op.add)
-    tt(pk(2), A("pcf", 8, 9), pk(1), Op.add)
-    ts(pk(3), pf(3), 8.0, Op.mult)
-    ts(pk(4), pf(3), -2.0, Op.mult, 1.0, Op.add)
-    ts(pk(5), pf(3), -1.0, Op.mult, 1.0, Op.add)
-    ts(pk(7), pf(0), 3.0, Op.is_gt)
-    ts(A("lane"), pf(0), 32.0, Op.mult, -128.0, Op.add)
-    cp(A("el", 0, 88), A("eli", 0, 88))
-    ts(A("el", 88, 92), A("eli", 88, 92), pf(5), Op.add)
-    ts(A("bl"), A("bli"), pf(4), Op.add)
-    ts(A("ll"), A("lli"), pk(6), Op.add)
-    act(A("fr"), A("fri"), 1.0)
-    for h in range(4):
-        for k, (a, b) in enumerate(((12, 20), (6, 9), (9, 12))):
-            act(A("fr", ST * h + a, ST * h + b), A("fri", ST * h + a, ST * h + b), 1.0, pk(k))
-    for a in (0, 11):
-        cp(A("own14", a, a + 3), A("fr", me + 6, me + 9), "s")
-    gat(A("ex", 1024, 1408), A("fr"), A("el", 0, 24), "s")
-    act(A("ein", 0, 384), A("ex", 1024, 1408), 0.0)
-    act(A("ein", 384, 448), A("ex", 1024, 1088), 0.0)
-    for h in others:
-        gat(A("ex", P * h, P * h + P), A("fr"), A("el", 24 + 16 * h, 40 + 16 * h), "s")
-
-    ts(A("xb"), A("xl"), 255, Op.bitwise_and)
-    ts(A("xc"), A("xl"), 7, Op.arith_shift_right, 1, Op.bitwise_and)
-    ts(A("emp"), A("xl", 0, 8), 0.0, Op.is_lt)
-    ts(A("xd"), A("xc"), -255.0, Op.mult)
-    tt(A("xt"), A("xl"), A("xb"), Op.add)
-    tt(A("we"), A("emp"), A("ke"), Op.mult)
-    tt(A("xp"), A("xt"), A("xd"), Op.add)
-    tt(A("p1"), A("we"), A("pos"), Op.add)
-    cp(A("land", me, me + 6, 2), A("xp", 8, 11))
-    cp(A("land", me + 1, me + 6, 2), A("xp", 11, 14))
-    tt(A("ss", 0, 6), A("xp", 8, 14), A("xp", 14, 20), Op.add)
-    tt(A("ss", 6, 14), A("xp", 0, 8), A("p1"), Op.add)
-    cp(A("land", me + 6, me + 20), A("ss"))
-    post("arrl", "lsl", [A("land", me, me + ST)] * 3, [A("land", me, me + ST)] * 3)
-    iota(A("vai", 0, 48), [[16, 3], [1, 8], [48, 2]], SLOTS)
-    iota(A("vai", 48, 176), [[16, 8], [1, 8], [128, 2]], SLOTS + V)
-    iota(A("vai", 176, 224), [[16, 3], [1, 8], [48, 2]], SLOTS)
-    iota(A("lst", 1, 385), [[0, 3], [1, 128]], 0)
-    iota(A("tab", 1024, 2048), [[2, 1024]], 3072)
-    iota(A("mv"), [[1, WIN]], 0)
-
-    own, zero = A("fr", me + 12, me + 20), float(OWN * r + 1)
-    ts(A("ne"), A("xl", 0, 8), 0.0, Op.is_ge)
-    ts(A("rk"), A("xl"), 8, Op.arith_shift_right)
-    tt(A("z1"), own, A("ne"), Op.mult)
-    ts(A("z2"), A("ne"), -zero, Op.mult, zero, Op.add)
-    tt(A("sm"), A("rk", 14, 17), A("rk", 8, 11), Op.is_equal)
-    cp(A("rke", 0, 3), A("rk", 8, 11))
-    tt(A("own14", 3, 11), A("z1"), A("z2"), Op.add)
-    cp(A("rke", 3, 11), A("rk", 0, 8))
-    ts(A("sm8"), A("sm"), 8.0, Op.mult)
-    tt(A("rke", 11, 14), A("rk", 14, 17), A("sm8"), Op.subtract)
-    act(A("dum"), A("dmi"), 1.0, pf(4))
-    cp(own, A("own14", 3, 11), "s")
+    def mk(j, a=0, b=14):
+        return A("msk", 8 * a + j, 8 * b, 8) if j < 3 else A("any", a, b)
+    ts(A("rk"), A("xa"), 8, Op.arith_shift_right, by=A("el", 18, 19))
+    ts(A("rkf"), A("rk", 0, 14), float(r), Op.subtract)
+    tt(A("ne2"), A("rk", 8, 11), A("rk", 11, 14), Op.not_equal)
+    ts(A("occ"), A("rk", 0, 8), 4.0, Op.is_lt)
+    tt(A("rkf", 8, 11), A("rkf", 8, 11), A("ne2"), Op.mult)
     for j, x in enumerate(others):
-        ts(A("msk", 14 * j, 14 * j + 14), A("rke"), float(x), Op.is_equal)
-    m3 = [A("msk", 14 * j, 14 * j + 14) for j in range(3)]
-    tt(A("any1"), m3[0], m3[1], Op.add)
+        ts(mk(j), A("rkf"), float(x - r), Op.is_equal)
+    tt(A("hz"), A("hm"), A("occ"), Op.mult)
+    tt(A("a1"), mk(0), mk(1), Op.add)
+    tt(A("any"), A("a1"), mk(2), Op.add)
+    for o in (0, 16):
+        cp(A("ex", mine[0] + o + SHI, mine[1], 32), A("gg", 0, 8), "s")
+        tt(A("ex", mine[0] + o + SLO, mine[1], 32), A("gg", 0, 8), A("ex", mine[0] + o + SHI, mine[1], 32), Op.subtract)
+        act(A("ex", mine[0] + o + IHI, mine[1], 32), A("hz"), 1.0, float(ZID))
+        act(A("ex", mine[0] + o + ILO, mine[1], 32), A("occ"), i32)
+    for j in range(4):
+        act(A("ex", mine[0] + FLAG + 4 * j, mine[1], 32), mk(j, 0, 8), -1.0)
+        tt(A("ex", myv[0] + FLAG + 4 * j, myv[1], 32), mk(j, 8, 11), A("kp"), Op.mult)
+    tr(A("tab", *mine), A("ex", *mine))
+    cp(A("ti0", 6 * r, 6 * r + 6), A("gg", 14, 20), "s")
+    cp(A("svf", 6 * r, 6 * r + 6), A("gg", 8, 14), "s")
+    cp(A("lf", ST * r, ST * r + ST), A("gg", 0, ST), "s")
     for j in range(3):
-        tt(A("ein", 4 * j + 4, 448, 32), m3[j], A("own14"), Op.mult)
-    tt(A("any2"), A("any1"), m3[2], Op.add)
-    tt(A("ein", FLAG, 448, 32), A("any2"), A("own14"), Op.mult)
-    ts(A("mx"), A("mxi"), pf(4), Op.add, pk(5), Op.mult)
-    tr(A("dix"), A("ein"))
-    run("s", lambda e: e.activation(ap(A("fst")), ap(A("dix")), Act.Sign), [A("dix")], [A("fst")])
-    gat(A("ex", *mine), A("fr"), A("el", 24 + 16 * r, 40 + 16 * r), "s")
+        cp(A("einv", FLAG + 4 * j, 96, 32), mk(j, 11, 14), "s")
+        cp(A("einv", 96 + FLAG + 4 * j, 192, 32), mk(j, 8, 11), "s")
+        cp(A("wt", j, 88, 8), mk(j, 0, 11), "s")
+    tt(A("u1"), A("any"), A("a1"), Op.add)
+    tt(A("u2"), A("u1"), mk(0), Op.add)
+    ts(A("b1"), A("u2"), -900.0, Op.mult, 3100.0, Op.add)
+    act(A("b2"), A("u2"), float(SLOTS))
+    tt(A("dum"), A("b1"), A("kk"), Op.add)
+    tt(A("msk", 4, 112, 8), A("b2"), A("c0"), Op.add)
+    tr(A("dv"), A("einv"))
+    scan(A("scs", 0, P), A("d0"), A("tab", *mine))
+    scan(A("scs", P, 448), A("d0", 0, 192), A("dv"))
+    tr(A("oss", 0, P), A("scs", 0, P))
+    tr(A("oss", IDS, 448), A("scs", P, IDS))
+    tr(A("oss", P, IDS), A("scs", IDS, 448))
+    for a, b in ((0, 7), (7, 14)):
+        tt(A("pr", 8 * a, 8 * b), A("oss", 32 * a + FLAG, 32 * b, 4), A("msk", 8 * a, 8 * b), Op.mult)
+    scan(A("sm"), A("d8"), A("pr"))
+    tt(A("dm"), A("dum"), A("sm", 7, 112, 8), Op.add)
+    tt(A("adm"), A("dm"), A("any"), Op.mult)
+    tt(A("stat"), A("dum"), A("adm"), Op.subtract)
+    cp(A("fo", 0, 3), A("stat", 11, 14))
+    act(A("wt", 3, 64, 8), A("dm", 0, 8), -1.0)
+    cp(A("wt", 67, 88, 8), A("dm", 8, 11), "s")
+    cp(A("wt", 4, 88, 8), A("stat", 0, 11), "s")
     for j in range(3):
-        act(A("ex", mine[0] + 4 * j + 4, mine[1], 32), A("msk", 14 * j + 3, 14 * j + 11), -2.0, 1.0)
-    act(A("ex", mine[0] + FLAG, mine[1], 32), A("any2", 3, 11), -2.0, 1.0)
-    act(A("val"), A("vai"), 1.0, pk(3))
-    act(A("d0"), A("lst", 1, 353), 0.0, pk(7))
-    quant(A("qo"), A("qop"), A("cv"))
-    tt(A("fo1"), A("any2", 0, 3), A("dum", 0, 3), Op.mult)
-    scan(A("scs"), A("fst"), A("fst"), A("lane"), Op.add, Op.max)
-    tr(A("oss"), A("scs"))
-    tt(A("fo2"), A("dum", 0, 3), A("fo1"), Op.subtract)
-    for j in range(3):
-        tt(A("spm", 14 * j, 14 * j + 14), A("oss", 4 * j + 4, 448, 32), m3[j], Op.mult)
-    tt(A("b0a"), A("spm", 0, 14), A("spm", 14, 28), Op.add)
-    tt(A("b0"), A("b0a"), A("spm", 28, 42), Op.add)
-    tt(A("fo3"), A("b0", 0, 3), A("fo2"), Op.add)
-    tt(A("b1"), A("b0"), A("dum"), Op.subtract)
-    cp(A("fof", 0, 3), A("fo3"))
-    sca(A("lst"), A("fof", 0, 3), A("val", 0, 48))
-    order("y", [A("qo"), A("qop")], [])
-    g.sync.dma_start(T.q[:, 0:OWN].bitcast(dt.uint8), T.qo[:, 0:OWN].bitcast(dt.uint8)).then_inc(T.sem.own, 16)
-    g.sync.dma_start(T.qp[:, 0:OWN], T.qop[:, 0:OWN]).then_inc(T.sem.own, 16)
-    total["own"] = 32
-    note([], [A("q", 0, OWN), A("qp", 0, OWN)], ("own", 32, {}, "dma"))
+        tt(A("ma0", 16 * j + 8, 16 * j + 11), mk(j, 11, 14), A("sm", 95, 112, 8), Op.mult)
+        act(A("mb", 16 * j + 8, 16 * j + 11), mk(j, 11, 14), -1.0, 1.0)
+    act(A("ma"), A("ma0"), -1.0, -float(MID))
+    sca(A("lst"), A("fo", 0, 3), A("val", 128, 176))
 
-    arrive("arrl", [A("land", ST * x, ST * x + ST) for x in others])
-    cp(A("lf"), A("land"))
-    gat(A("ex", 0, 1024, 16), A("lf"), A("el", 88, 92))
-    for h in range(4):
-        cp(A("to0", 6 * h, 6 * h + 6), A("lf", ST * h, ST * h + 6), "s")
-    for h in range(4):
-        for k in range(2):
-            cp(A("ex", 1024 + 96 * h + 16 * k, 1120 + 96 * h, 32), A("lf", ST * h + 6 + 3 * k, ST * h + 9 + 3 * k), "s")
-    tr(A("tab", 0, 512), A("ex", 0, 512))
-    cp(A("tou"), A("to0"))
-    tr(A("tab", 512, 1024), A("ex", 512, 1024))
-    first, places = A("tab", 0, 1024), A("tab", 0, PLACES)
+    for a, b in afar:
+        cp(A("lf", ST * a, ST * b), A("land", ST * a, ST * b))
+    for a, b in afar:
+        cp(A("ex", P * a + SHI, P * b, 16), A("lf"), "v", A("el", 0, b - a) if a == 0 else A("el", 4, 4 + b - a))
+        tt(A("ex", P * a + SLO, P * b, 16), A("lf"), A("ex", P * a + SHI, P * b, 16), Op.subtract, A("el", 0, b - a) if a == 0 else A("el", 4, 4 + b - a))
+        tr(A("tab", P * a, P * b), A("ex", P * a, P * b))
+    for h in others:
+        cp(A("ti0", 6 * h, 6 * h + 6), A("lf", ST * h + 14, ST * h + 20), "s")
+    for h in others:
+        cp(A("svf", 6 * h, 6 * h + 6), A("lf", ST * h + 8, ST * h + 14), "s")
+    cp(A("ex", 1024 + SHI, 1408, 16), A("svf"), "s")
+    cp(A("to0"), A("ti0"))
+    first, places = A("tab", 0, 1024), A("tab")
 
-    def spread(t, pairs):
-        order("y", [A("sn", P * t, P * t + P)], [A("sn", 0, P)])
-        for p in range(0, 128, 32):
-            for x, z in pairs:
-                g.sync.dma_start(T.sn[p + z:p + z + 1, 0:P], T.sn[p + x:p + x + 1, P * t:P * t + P]).then_inc(T.sem.sns, 16)
-                total["sns"] = total.get("sns", 0) + 16
+    def look(t, win):
+        cp(A("ga%d" % t, 192, 384), win, "s", A("to%d" % t, 12, 24))
+        cp(A("ga%d" % t, 0, 192), win, "v", A("to%d" % t, 0, 12))
 
-    gat(A("ga0", 192, 384), first, A("tou", 12, 24), "s")
-    gat(A("ga0", 0, 192), first, A("tou", 0, 12))
-    cp(A("tab", 2048, 3072), A("tab", 1024, 2048), "s")
-    tr(A("gt0"), A("ga0"))
+    def step(t, p0, into):
+        a = [on(x, p0, 128) for x in (A("gt%d" % t), A("ga%d" % t), A("ta%d" % t), A("gt%d" % t, SHI, 384, 16), A("gt%d" % t, SLO, 384, 16), A("ti%d" % (t + 1)), A("ti%d" % t), A(into))]
+        tr(a[0], a[1])
+        tt(a[2], a[3], a[6], Op.subtract)
+        tt(a[5], a[2], a[4], Op.add)
+        cp(a[7], a[5])
+
+    look(0, first)
+    tt(A("ex", 1024 + SLO, 1408, 16), A("svf"), A("ex", 1024 + SHI, 1408, 16), Op.subtract)
     tr(A("ev"), A("ex", 1024, 1408))
-    tt(A("ti1"), A("gt0", 0, 384, 16), A("to0"), Op.subtract)
-    cp(A("to1"), A("ti1"))
-    sca(first, A("tou"), A("ev"))
-    gat(A("ga1", 192, 384), places, A("to1", 12, 24), "s")
-    gat(A("ga1", 0, 192), places, A("to1", 0, 12))
-    cp(A("sn", 0, P), A("tab", *mine), "s")
-    tr(A("gt1"), A("ga1"))
-    tt(A("ti2"), A("gt1", 0, 384, 16), A("ti1"), Op.subtract)
-    cp(A("to2"), A("ti2"))
-    act(A("x2"), A("ti2"), pf(3))
-    act(A("y2"), A("ti2"), pk(4))
+    step(0, 0, "to1")
+    sca(first, A("to0"), A("ev"))
+    look(1, places)
+    cp(quad(A("sn"), 0), quad(A("tab", *mine), 0), "s")
+    step(1, 0, "to2")
     sca(places, A("to1"), A("ga0"))
-    gat(A("ga2", 256, 384), places, A("to2", 16, 24), "s")
-    tt(A("lcf"), A("x2"), A("mx"), Op.add)
-    gat(A("ga2", 0, 256), places, A("to2", 0, 16))
-    cp(A("lc"), A("lcf"))
-    cp(A("sn", P, 2 * P), A("tab", *mine), "s")
-    gat(A("gc"), A("tab"), A("lc"), "s")
-    tr(A("gt2"), A("ga2"))
-    ts(A("w1"), A("gt2", 0, 384, 16), pf(3), Op.mult)
-    tt(A("ti3"), A("w1"), A("y2"), Op.add)
-    cp(A("to3"), A("ti3"))
-    sca(places, A("to3"), A("gc"))
-    spread(1, ((10, 10), (26, 26)))
+    look(2, places)
+    cp(quad(A("sn"), 1), quad(A("tab", *mine), 1))
+    cp(on(A("ga1"), 64, 128), on(A("ga2"), 64, 128), "s")
+    step(2, 64, "to2")
+    sca(places, A("to2"), A("ga1"))
 
-    run("s", lambda e: e.activation(ap(A("un", 0, 256)), ap(A("tab", *mine)), Act.Relu, scale=-1.0), [A("tab", *mine)], [A("un", 0, 256)])
-    fo = A("land", me, me + 6)
-    run("v", lambda e: e.tensor_tensor(ap(A("un", 256, 352)), ap(first).indirect(ap(fo)), ap(A("dix", 352, 448)), Op.is_equal), [first, fo, A("dix", 352, 448)], [A("un", 256, 352)], True)
-    cp(A("sn", 2 * P, 3 * P), A("tab", *mine), "s")
-    spread(2, ((14, 14), (14, 30), (30, 15), (30, 31)))
-    note([A("sn", P, 3 * P)], [A("sn", 0, P)], ("sns", total["sns"], {}, "dma"))
-    pack(0, 128)
-    for h in range(4):
-        cp(A("m", OWN * h, OWN * h + OWN), A("mv", 0, OWN), "s")
-    scan(A("sc"), A("d0"), A("un"), 0.0, Op.mult, Op.add)
-    tr(A("osd"), A("sc"))
-    for j in range(3):
-        tt(A("cm", 11 * j, 11 * j + 11), A("osd", 4 * j + 4, 352, 32), A("msk", 14 * j + 3, 14 * j + 14), Op.mult)
-    tt(A("fl"), A("any2", 3, 14), A("osd", FLAG, 352, 32), Op.subtract)
-    tt(A("cs1"), A("cm", 0, 11), A("cm", 11, 22), Op.add)
-    tt(A("bb"), A("b1", 3, 14), A("cm", 22, 33), Op.subtract)
-    tt(A("cs2"), A("bb"), A("cs1"), Op.subtract)
-    tt(A("fb"), A("fl"), A("cs2"), Op.mult)
-    tt(A("of1"), A("fb"), A("dum", 3, 14), Op.add)
-    cp(A("ofd", 0, 11), A("of1"))
-    sca(A("lst"), A("ofd", 0, 11), A("val", 48, 224))
-    tr(A("olt"), A("lst", 1, 385))
-    tt(A("zb", 0, 12), A("olt", 0, 384, 32), A("olt", 16, 384, 32), Op.max)
+    tt(A("un"), first, A("k1"), Op.is_equal, A("rec", 14, 20))
+    scan(A("sc", 0, P), A("d0"), A("tab", *mine))
+    scan(A("sc", P, IDS), A("d0", 0, V), A("un"))
+    cp(quad(A("sn"), 2), quad(A("tab", *mine), 0), "s")
+    cp(quad(A("sn"), 3), quad(A("tab", *mine), 3), "s")
+    tr(A("osd", 0, P), A("sc", 0, P))
+    tr(A("osd", P, IDS), A("sc", P, IDS))
+    tt(A("pd", 0, 64), A("osd", FLAG, P, 4), A("wt", 0, 64), Op.mult)
+    tt(A("pd", 64, 88), A("osd", P + FLAG, IDS, 4), A("wt", 64, 88), Op.mult)
+    scan(A("sd"), A("d8", 0, 88), A("pd"))
+    for p in (0, 64):
+        cp(on(A("ofd", 0, 11), p, p + 64), on(A("sd", 7, 88, 8), 0, 64))
+    tt(A("mp"), A("sd"), A("mb"), Op.mult, A("el", 8, 11))
+    for p in (0, 64):
+        tt(on(A("msg"), p, p + 64), on(A("mp"), 0, 64), on(A("ma"), 0, 64), Op.add)
+    post("arrm", "lsm", [A("msg", 16 * j, 16 * j + MS) for j in range(3)], [A("landm", MS * r, MS * r + MS)] * 3, [A("landm", MS * x, MS * x + MS) for x in others])
+    sca(A("lst"), A("ofd", 0, 11), A("val"))
+    tr(A("olt"), A("lst", 0, IDS))
+    tt(A("zb", 0, 11), A("olt", 0, IDS, 32), A("olt", 16, IDS, 32), Op.max)
     tr(A("zt"), A("zb"))
-    gat(A("zg"), A("zt"), A("bl"))
+    cp(A("zg"), A("zt"), "v", A("el", 12, 16))
     tr(A("zh"), A("zg"))
-    gat(A("loff"), A("zh"), A("ll"))
-    lists = [A("loff", 8 * j, 8 * j + 7) for j in range(3)]
-    at = [sorted(y for y in range(N) if y != x).index(r) for x in others]
-    post("arrm", "lsm", [A("loff", 8 * j, 8 * j + 8) for j in range(3)], [A("lin", 8 * k, 8 * k + 8) for k in at])
-    for j in range(3):
-        pick(A("sq%d" % j), A("qo"), lists[j])
-        gat(A("sqp%d" % j), A("qop"), lists[j], "s")
-    land = [(OWN + SLOTS * k, OWN + SLOTS * k + SLOTS) for k in at]
-    post("arrq", "lsq", [A("sq%d" % j) for j in range(3)], [A("q", *x) for x in land])
-    post("arrp", "lsp", [A("sqp%d" % j) for j in range(3)], [A("qp", *x) for x in land])
+    ts(A("loff"), A("zh"), float(MID), Op.add, by=A("el", 16, 18))
+    pick(A("sq"), A("qo"), A("loff", 0, 21))
+    cp(A("sqp"), A("qop"), "s", A("loff", 0, 21))
+    at = [OWN + SLOTS * turn(x, r) for x in others]
+    k = post("arrp", "lsp", [A("sqp", SLOTS * j, SLOTS * j + SLOTS) for j in range(3)], [A("qp", x, x + SLOTS) for x in at], [A("qp", OWN, WIN)])
+    post("arrq", "lsq", [A("sq", SLOTS * j, SLOTS * j + SLOTS) for j in range(3)], [A("q", x, x + SLOTS) for x in at], [A("q", OWN, WIN)], HOP + 0.5, [k])
 
-    tr(A("ts"), A("sn", 0, 256))
-    now = [A("ts", x, 256, 16) for x in (6, 10, 14, 15)]
-    tt(A("ne3"), now[3], now[1], Op.not_equal)
-    tt(A("df3"), now[3], now[2], Op.subtract)
-    cp(A("ido", 0, 16), now[0])
-    tt(A("pr3"), A("ne3"), A("df3"), Op.mult)
-    cp(A("ido", 16, 32), now[1])
-    tt(A("r3"), A("pr3"), now[2], Op.add)
-    cp(A("ido", 32, 48), now[2])
-    cp(A("ido", 48, 64), A("r3"))
-    pack(128, 640)
-    pack(640, 1024)
-    arrive("arrm", [A("lin", 8 * k, 8 * k + 8) for k in range(3)])
-    for k, x in enumerate(others):
-        sca(A("m", OWN * x, OWN * x + OWN), A("lin", 8 * k, 8 * k + 7), A("mv", OWN + SLOTS * k, OWN + SLOTS * k + SLOTS))
+    for h in others:
+        act(A("ex", IDS * h + SLO, IDS * h + IDS, 16), A("vai", 0, 22), 0.0, float(OWN + SLOTS * (turn(r, h) - turn(h, r)) + MID))
+        for o in (0, 16):
+            cp(A("ex", IDS * h + o + SHI, IDS * h + IDS, 32), A("landm", MS * h, MS * h + MS), "s")
+        tr(A("m", IDS * h, IDS * h + IDS), A("ex", IDS * h, IDS * h + IDS))
+    for o in (0, 16):
+        cp(A("ex", IDS * r + o + SLO, IDS * r + IDS, 32), A("r32", 0, 11), "s")
+        act(A("ex", IDS * r + o + SHI, IDS * r + IDS, 32), A("r32", 0, 11), 0.0, i32)
+    act(A("ex", ZID, 1440, 8), A("r32", 0, 4), 0.0, IDS / 2)
+    tr(A("m", IDS * r, IDS * r + IDS), A("ex", IDS * r, IDS * r + IDS))
+    tr(A("m", ZID, 1440), A("ex", ZID, 1440))
+    tr(A("ts"), A("sn"))
+    tt(A("idf"), A("ts", IHI, P, 32), A("ts", ILO, P, 32), Op.add)
+    was = [quad(A("was", 8 * k, 8 * k + 8), 3) for k in range(2)]
+    for k in range(2):
+        cp(was[k], quad(A("idf"), k + 1), "s")
+    tt(quad(A("ne3"), 3), quad(A("idf"), 3), was[0], Op.not_equal)
+    tt(quad(A("df3"), 3), quad(A("idf"), 3), was[1], Op.subtract)
+    tt(quad(A("pr3"), 3), quad(A("ne3"), 3), quad(A("df3"), 3), Op.mult)
+    tt(quad(A("idf"), 3), quad(A("pr3"), 3), was[1], Op.add)
+    for k in range(2):
+        cp(A("ido", k, 16, 2), A("idf"))
+    cp(A("mg", 128, 256), A("m"), "s", A("ido", 8, 16))
+    cp(A("mg", 0, 128), A("m"), "v", A("ido", 0, 8))
+    tr(A("om"), A("mg"))
+    for t in range(R):
+        tt(quad(A("sl", 16 * t, 16 * t + 16), 0), quad(A("om", SHI, P, 16), t), quad(A("om", SLO, P, 16), t), Op.add)
+    for k in range(4):
+        cp(quad(A("off"), k), quad(A("sl"), 0))
 
-    def look(t):
-        a = P * t
-        if t:
-            gat(A("mg", a, a + P), A("m"), A("ido", 16 * t, 16 * t + 16), "s")
-        else:
-            gat(A("mg", 128, 256), A("m"), A("ido", 8, 16), "s")
-            gat(A("mg", 0, 128), A("m"), A("ido", 0, 8))
-
-    def turn(t):
-        a = P * t
-        tr(A("om", a, a + P), A("mg", a, a + P))
-        cp(A("off", 16 * t, 16 * t + 16), A("om", a, a + P, 16))
-
-    arrive("arrq", [A("q", OWN, WIN)])
-    arrive("arrp", [A("qp", OWN, WIN)])
-
-    def table(t):
-        pick(A("k%d" % t), A("q"), A("off", 16 * t, 16 * t + 16))
-        gat(A("kp%d" % t), A("qp"), A("off", 16 * t, 16 * t + 16), "s")
-        for o in range(O):
-            i = O * t + o
-            wq, wp, kq, kp, z = A("wq", 128 * i, 128 * i + 128), A("wp", 128 * i, 128 * i + 128), A("k%d" % t), A("kp%d" % t), A("ps", 512 * i, 512 * i + P)
-            run("t", lambda e: e.matmul_mx(ap(z), ap(wq), ap(wp), ap(kq), ap(kp), True, True), [wq, wp, kq, kp], [z])
-
-    def out(t):
-        for o in range(O):
-            i = O * t + o
-            for b in range(2):
-                cp(A("ys", P * i + 128 * b, P * i + 128 * b + 128), A("ps", 512 * i + b, 512 * i + P, 2), "s" if t < 1 else "vs"[o])
+    for t in range(R):
+        kq, kp = A("k%dq" % t), A("k%dp" % t)
+        cp(kp, A("qp"), "s", A("off", 16 * t, 16 * t + 16))
+        pick(kq, A("q"), A("off", 16 * t, 16 * t + 16))
+        for i in range(O * t, O * t + O):
+            a = [A("ps", 512 * i, 512 * i + P), A("wq", 128 * i, 128 * i + 128), A("wp", 128 * i, 128 * i + 128), kq, kp]
+            add("t", lambda a=a: g.tensor.matmul_mx(*[ap(x) for x in a], True, True).then_inc(T.sem.st, 1), a[1:], a[:1], 0.33)
             reg = A("ys", P * i, P * i + P)
-            order("y", [reg], [])
-            g.sync.dma_start(T.y[:, P * i:P * i + P], ap(reg)).then_inc(T.sem.sty, 16)
-            total["sty"] = total.get("sty", 0) + 16
-    look(0)
-    look(1)
-    look(2)
-    turn(0)
-    turn(1)
-    table(0)
-    look(3)
-    turn(2)
-    table(1)
-    turn(3)
-    out(0)
-    table(2)
-    out(1)
-    table(3)
-    out(2)
-    out(3)
-    for q in ("v", "s", "t", "g"):
-        total[sem_of[q]] = cnt[sem_of[q]]
+            cp(reg, a[0], "vs"[i % 2])
+            load("y", "sty", [(T.y[:, P * i:P * i + P], ap(reg))], [reg], [], DMA + 0.4 * (R * O - i))
+
+    known, log, total = {k: {} for k in eng}, {}, {}
+    for c in in_order(calls):
+        q = c["q"]
+        need = [tok for regs, w in ((c["reads"], False), (c["writes"], True)) for x in regs for y, w2, tok in log.get(x[0], []) if (w or w2) and clash(x, y)]
+        for s, v, clock in sorted(need, key=lambda t: -t[1]):
+            if c["go"] and known[q].get(s, 0) < v:
+                eng[q].wait_ge(T.sem[s], v)
+                for k, x in list(clock.items()) + [(s, v)]:
+                    known[q][k] = max(known[q].get(k, 0), x)
+        if c["go"]:
+            c["go"]()
+        s = c["sem"] or sem_of[q]
+        total[s] = total.get(s, 0) + (c["n"] or 1)
+        for regs, w in ((c["reads"], False), (c["writes"], True)):
+            for x in regs:
+                log.setdefault(x[0], []).append((x, w, (s, total[s], dict(known[q]) if c["go"] else {})))
     for s in SEMAPHORES:
         if s in total:
             g.wait_ge(T.sem[s], total[s])

@@ -9,13 +9,13 @@ WIN = OWN + 3 * SLOTS
 ST, MS = 20, 11
 SHI, SLO, IHI, ILO = 0, 8, 1, 9
 FLAG, ONE = 2, 18
-PLACES = 3088
-MIRROR = 2048.0
+PLACES = 1024 + 3 * 384
+NONE = 8192.0
 MID = 176
 ZID = N * IDS
 TINY = 2.0 ** -24
 F32, I32, U16, BF, CODE, PL = "float32", "int32", "uint16", "bfloat16", "float8_e4m3fn_x4", "uint8"
-CYCLE, FLOOR, WAKE, PICK, PUT, DMA, HOP = 0.001, 64, 0.12, 1.5, 3.8, 2.0, 2.0
+CYCLE, FLOOR, WAKE, PICK, PUT, DMA, HOP = 0.001, 64, 0.16, 1.5, 3.8, 2.0, 2.0
 
 
 def _s(n, t):
@@ -24,10 +24,10 @@ def _s(n, t):
 
 SCRATCH = {
     "xl": _s(28, I32), "xa": _s(32, I32), "z": _s(96, F32), "zc": _s(96, F32), "gl": _s(2, U16), "r32": _s(16, F32),
-    "pci": _s(8, I32), "pcf": _s(16, F32), "pos8": _s(8, F32), "minc": _s(32, F32), "gg": _s(48, F32), "rec": _s(ST, U16),
+    "pci": _s(8, I32), "pcf": _s(16, F32), "pc": _s(32, F32), "gg": _s(32, F32), "r16": _s(24, F32), "dj": _s(24, F32), "f1f": _s(24, F32), "f2f": _s(24, F32), "rec": _s(ST, U16),
     "land": _s(N * ST, U16), "lf": _s(N * ST, F32), "ramp": _s(16, F32), "el": _s(20, U16), "ex": _s(1440, BF), "tab": _s(PLACES, BF),
     "svf": _s(24, F32), "ev": _s(384, BF), "rk": _s(16, I32), "rkf": _s(14, F32), "ne2": _s(3, F32), "msk": _s(112, F32), "wt": _s(88, F32),
-    "a1": _s(14, F32), "any": _s(14, F32), "u1": _s(14, F32), "u2": _s(14, F32), "occ": _s(8, F32), "hm": _s(8, F32), "hz": _s(8, F32),
+    "a1": _s(14, F32), "any": _s(14, F32), "u1": _s(14, F32), "u2": _s(14, F32), "occ": _s(11, F32), "hm": _s(8, F32), "hz": _s(8, F32),
     "kp": _s(3, F32), "einv": _s(192, BF), "dv": _s(192, BF), "d0": _s(P, BF), "d8": _s(112, F32), "scs": _s(448, BF), "oss": _s(448, BF),
     "pr": _s(112, F32), "sm": _s(112, F32), "c0": _s(14, F32), "kk": _s(14, F32), "b1": _s(14, F32), "b2": _s(14, F32),
     "dum": _s(14, F32), "dm": _s(14, F32), "adm": _s(14, F32), "stat": _s(14, F32), "fo": _s(4, U16),
@@ -44,10 +44,9 @@ SCRATCH = {
 for _t in range(3):
     SCRATCH["ga%d" % _t] = _s(384, BF)
     SCRATCH["gt%d" % _t] = _s(384, BF)
-    SCRATCH["ta%d" % _t] = _s(24, F32)
-    SCRATCH["ti%d" % _t] = _s(24, F32)
+    SCRATCH["e%d" % _t] = _s(96, F32)
+    SCRATCH["ti%d" % _t] = _s(96, F32)
     SCRATCH["to%d" % _t] = _s(24, U16)
-SCRATCH["ti3"] = _s(24, F32)
 for _t in range(4):
     SCRATCH["k%dq" % _t] = _s(P, CODE)
     SCRATCH["k%dp" % _t] = _s(P, PL)
@@ -168,8 +167,8 @@ def rank_program(g, core, T, topo):
     def tr(out, a):
         run("v", lambda e: e.transpose(ap(out), ap(a)), [a], out)
 
-    def scan(out, a, b):
-        run("v", lambda e: e.tensor_tensor_scan(ap(out), ap(a), ap(b), 0.0, Op.mult, Op.add), [a, b], out)
+    def scan(out, a, b, op=Op.mult):
+        run("v", lambda e: e.tensor_tensor_scan(ap(out), ap(a), ap(b), 0.0, op, Op.add), [a, b], out)
 
     def fill(out, c):
         run("v", lambda e: e.memset(ap(out), c), [], out)
@@ -209,31 +208,32 @@ def rank_program(g, core, T, topo):
     mine, myv = (P * r, P * r + P), (1024 + V * r, 1024 + V * r + V)
 
     load("ys", "ldx", [(T.xl[16 * o:16 * o + 16, a:b], n[:, :]) for n, a, b in ((T.alt, 0, 16), (T.f2, 16, 22), (T.f1, 22, 28)) for o in range(2)], [], [quad(A("xl"), 0)], 1.3)
+    load("y", "ldc", [(T.cv[:, 4 * P:4 * IDS], T.v[:, :]), (T.cv[:, 0:4 * P], T.c[:, :])], [], [A("cv", 0, 4 * IDS)], 2.5, [0])
 
-    iota(A("z", 0, 16), [[-6, 2], [1, 8]], 22)
-    iota(A("z", 16, 32), [[-6, 2], [2, 4], [-1, 2]], 23)
+    iota(A("z", 0, 16), [[1, 16]], 12)
+    iota(A("z", 16, 32), [[2, 8], [-1, 2]], 13)
     iota(A("z", 32, 64), [[1, 2], [2, 16]], 0)
     iota(A("z", 64, 96), [[1, 32]], 0)
     iota(A("r32"), [[32, 16]], 0)
     for a in range(0, 1440, 288):
         fill(A("ex", a, a + 288), 0.0)
     fill(A("xa"), 0)
-    fill(A("minc"), 4096.0)
+    fill(A("pc"), 0.0)
     iota(A("ex", IHI, 1024, 16), [[IDS, 4], [32, 8], [0, 2]], 0)
     iota(A("ex", 1024 + IHI, 1408, 16), [[IDS, 4], [32, 3], [0, 2]], P)
     iota(A("ramp"), [[1, 16]], 0)
     iota(A("vai"), [[32, 11], [1, 16]], -MID)
     iota(A("k0"), [[1, V]], 1)
+    iota(A("r16"), [[16, 24]], 1024)
     tr(A("zc"), A("z"))
     cp(A("gl"), A("zc", 0, 64, 32))
     i32 = A("zc", 64, 65)
-    ts(A("pos8"), A("r32", 0, 8), i32, Op.add, float(P * r), Op.add)
-    ts(A("minc", 16, 24), A("r32", 0, 8), i32, Op.add, float(P * r + 1024), Op.add)
+    ts(A("pc", 16, 24), A("r32", 0, 8), i32, Op.add, float(P * r), Op.add)
     cp(A("pci", 0, 1), i32)
     for k, (sh, m) in enumerate([(0, 15), (0, 16), (1, 7), (0, 1)]):
         ts(A("pci", k + 1, k + 2), A("pci", 0, 1), sh, Op.arith_shift_right, m, Op.bitwise_and)
     cp(A("pcf", 0, 4), A("pci", 1, 5))
-    i16, o16, half, odd, xor0, xor16, lanes, sel0, ll0, isone, tiny = [A("pcf", k, k + 1) for k in range(11)]
+    i16, o16, half, odd, xor0, xor16, lanes, sel0, ll0, isone, tiny, none, half12 = [A("pcf", k, k + 1) for k in range(13)]
     ts(xor0, o16, -2.0, Op.mult, 16.0, Op.add)
     tt(xor16, xor0, i32, Op.add)
     ts(lanes, i32, float(FLAG + 12), Op.is_lt)
@@ -241,21 +241,26 @@ def rank_program(g, core, T, topo):
     ts(ll0, odd, 32.0, Op.mult, half, Op.add)
     ts(isone, i32, float(ONE), Op.is_equal)
     ts(tiny, i32, float(ONE), Op.not_equal, TINY, Op.mult)
-    ts(A("el", 0, 3), A("ramp", 0, 3), float(ST), Op.mult, half, Op.add)
-    if r + 1 < N:
-        ts(A("el", 4, 3 + N - r), A("ramp", r + 1, N), float(ST), Op.mult, half, Op.add)
+    ts(none, i16, float(SHI), Op.is_equal, NONE, Op.mult)
+    ts(half12, half, 12.0, Op.add)
+    ts(A("el", 0, 8, 2), A("ramp", 0, 4), float(ST), Op.mult, half12, Op.add)
+    act(A("dj"), A("r16"), 1.0, i16)
+    for t in range(3):
+        act(A("e%d" % t), A("vai", 0, 96), 0.0, 4 * NONE)
+        act(A("e%d" % t, 3, 96, 4), A("dj"), 1.0, 384.0 * t)
     ts(sel0, sel0, 7.0, Op.add)
     ts(A("el", 8, 11), A("ramp", 0, 3), 0.0, Op.mult, sel0, Op.add)
     ts(A("el", 12, 16, 2), A("ramp", 0, 2), 16.0, Op.mult, i16, Op.add)
     ts(A("el", 13, 16, 2), A("ramp", 0, 2), 16.0, Op.mult, i16, Op.add)
     ts(A("el", 16, 18), A("ramp", 0, 2), 8.0, Op.mult, ll0, Op.add)
     cp(A("el", 18, 19), A("zc", 32, 33))
-    for a in range(1024, PLACES, 344):
-        act(A("tab", a, a + 344), A("ex", 0, 344), 0.0, MIRROR)
+    for a in range(1024, PLACES - 384, 128):
+        act(A("tab", a, a + 128), A("vai", 0, 128), 0.0, none)
     act(A("ex", ILO, 1408, 16), A("vai", 0, 88), 0.0, i32)
     act(A("ex", 1024 + 16 + ILO, 1408, 32), A("r32", 0, 12), 0.0, xor16)
     act(A("ex", ONE, 1408, 32), A("vai", 0, 44), 0.0, 1.0)
-    act(A("d0"), A("tab", 1024, 1024 + P), 0.0, lanes)
+    for a in (0, 128):
+        act(A("d0", a, a + 128), A("vai", 0, 128), 0.0, lanes)
     act(A("d8"), A("vai", 0, 112), 0.0, 1.0)
     act(A("d8", 0, 112, 8), A("r32", 0, 14), 0.0)
     act(A("val"), A("vai"), 1.0, o16)
@@ -277,18 +282,15 @@ def rank_program(g, core, T, topo):
     fill(A("lst", 0, IDS), -float(MID))
 
     for k in range(4):
-        ts(quad(A("xa", 0, 28), k), quad(A("xl"), 0), 2047, Op.bitwise_and)
-    tt(A("gg", 14, 46), A("xa"), A("minc"), Op.min, A("gl"))
-    tt(A("gg", 0, 8), A("gg", 30, 38), A("pos8"), Op.add)
-    tt(A("gg", 8, 14), A("gg", 14, 20), A("gg", 22, 28), Op.add)
-    cp(A("rec"), A("gg", 0, ST))
+        ts(quad(A("xa", 0, 28), k), quad(A("xl"), 0), int(NONE) - 1, Op.bitwise_and)
+    tt(A("gg"), A("xa"), A("pc"), Op.add, A("gl"))
+    cp(A("rec"), A("gg", 4, 4 + ST))
     post("arrl", "lsl", [A("rec")] * 3, [A("land", ST * r, ST * r + ST)] * 3, [A("land", ST * x, ST * x + ST) for x in others], HOP + 0.8)
-    k = load("y", "ldc", [(T.cv[:, 4 * P:4 * IDS], T.v[:, :]), (T.cv[:, 0:4 * P], T.c[:, :])], [], [A("cv", 0, 4 * IDS), A("rec", 0, 8)], 3.5)
-    for h in range(2):
-        k = load("y", "ldw%d" % h, [(T.wb[:, 2048 * h:2048 * h + 2048], T.w[:, 2048 * h:2048 * h + 2048])], [], [A("wb", 2048 * h, 2048 * h + 2048)], 5.0 + 2 * h, [k])
+    k = load("y", "ldw0", [(T.wb[:, 0:2048], T.w[:, 0:2048])], [], [A("wb", 0, 2048), A("rec", 12, 20)], 3.5)
+    load("y", "ldw1", [(T.wb[:, 2048:4096], T.w[:, 2048:4096])], [], [A("wb", 2048, 4096)], 5.0, [k])
     for a in range(0, OWN, 128):
         quant(A("qo", a, a + 128), A("qop", a, a + 128), A("cv", 4 * a, 4 * a + 512))
-    load("y", "own", [(raw(A("q", 0, OWN)), raw(A("qo"))), (raw(A("qp", 0, OWN)), raw(A("qop")))], [A("qo"), A("qop")], [A("q", 0, OWN), A("qp", 0, OWN)])
+    load("y", "own", [(raw(A("q", 0, OWN)), raw(A("qo"))), (raw(A("qp", 0, OWN)), raw(A("qop")))], [A("qo"), A("qop")], [A("q", 0, OWN), A("qp", 0, OWN)], 12.0)
     for a in range(0, 1024, 128):
         quant(A("wq", a, a + 128), A("wp", a, a + 128), A("wb", 4 * a, 4 * a + 512))
 
@@ -296,26 +298,24 @@ def rank_program(g, core, T, topo):
         return A("msk", 8 * a + j, 8 * b, 8) if j < 3 else A("any", a, b)
     ts(A("rk"), A("xa"), 8, Op.arith_shift_right, by=A("el", 18, 19))
     ts(A("rkf"), A("rk", 0, 14), float(r), Op.subtract)
-    tt(A("ne2"), A("rk", 8, 11), A("rk", 11, 14), Op.not_equal)
-    ts(A("occ"), A("rk", 0, 8), 4.0, Op.is_lt)
-    tt(A("rkf", 8, 11), A("rkf", 8, 11), A("ne2"), Op.mult)
+    ts(A("occ", 0, 8), A("rk", 0, 8), float(N), Op.is_lt)
+    tt(A("occ", 8, 11), A("rk", 8, 11), A("rk", 11, 14), Op.not_equal)
+    tt(A("rkf", 0, 11), A("rkf", 0, 11), A("occ"), Op.mult)
     for j, x in enumerate(others):
         ts(mk(j), A("rkf"), float(x - r), Op.is_equal)
-    tt(A("hz"), A("hm"), A("occ"), Op.mult)
+    ts(A("any"), A("rkf"), 0.0, Op.not_equal)
+    tt(A("hz"), A("hm"), A("occ", 0, 8), Op.mult)
     tt(A("a1"), mk(0), mk(1), Op.add)
-    tt(A("any"), A("a1"), mk(2), Op.add)
     for o in (0, 16):
-        cp(A("ex", mine[0] + o + SHI, mine[1], 32), A("gg", 0, 8), "s")
-        tt(A("ex", mine[0] + o + SLO, mine[1], 32), A("gg", 0, 8), A("ex", mine[0] + o + SHI, mine[1], 32), Op.subtract)
+        cp(A("ex", mine[0] + o + SHI, mine[1], 32), A("gg", 16, 24), "s")
+        tt(A("ex", mine[0] + o + SLO, mine[1], 32), A("gg", 16, 24), A("ex", mine[0] + o + SHI, mine[1], 32), Op.subtract)
         act(A("ex", mine[0] + o + IHI, mine[1], 32), A("hz"), 1.0, float(ZID))
-        act(A("ex", mine[0] + o + ILO, mine[1], 32), A("occ"), i32)
+        act(A("ex", mine[0] + o + ILO, mine[1], 32), A("occ", 0, 8), i32)
     for j in range(4):
         act(A("ex", mine[0] + FLAG + 4 * j, mine[1], 32), mk(j, 0, 8), -1.0)
         tt(A("ex", myv[0] + FLAG + 4 * j, myv[1], 32), mk(j, 8, 11), A("kp"), Op.mult)
     tr(A("tab", *mine), A("ex", *mine))
-    cp(A("ti0", 6 * r, 6 * r + 6), A("gg", 14, 20), "s")
-    cp(A("svf", 6 * r, 6 * r + 6), A("gg", 8, 14), "s")
-    cp(A("lf", ST * r, ST * r + ST), A("gg", 0, ST), "s")
+    cp(A("lf", ST * r, ST * r + ST), A("gg", 4, 4 + ST), "s")
     for j in range(3):
         cp(A("einv", FLAG + 4 * j, 96, 32), mk(j, 11, 14), "s")
         cp(A("einv", 96 + FLAG + 4 * j, 192, 32), mk(j, 8, 11), "s")
@@ -350,16 +350,18 @@ def rank_program(g, core, T, topo):
 
     for a, b in afar:
         cp(A("lf", ST * a, ST * b), A("land", ST * a, ST * b))
-    for a, b in afar:
-        cp(A("ex", P * a + SHI, P * b, 16), A("lf"), "v", A("el", 0, b - a) if a == 0 else A("el", 4, 4 + b - a))
-        tt(A("ex", P * a + SLO, P * b, 16), A("lf"), A("ex", P * a + SHI, P * b, 16), Op.subtract, A("el", 0, b - a) if a == 0 else A("el", 4, 4 + b - a))
-        tr(A("tab", P * a, P * b), A("ex", P * a, P * b))
     for h in others:
-        cp(A("ti0", 6 * h, 6 * h + 6), A("lf", ST * h + 14, ST * h + 20), "s")
-    for h in others:
-        cp(A("svf", 6 * h, 6 * h + 6), A("lf", ST * h + 8, ST * h + 14), "s")
+        cp(A("ex", P * h + SHI, P * h + P, 16), A("lf"), "v", A("el", 2 * h, 2 * h + 1))
+        tt(A("ex", P * h + SLO, P * h + P, 16), A("lf"), A("ex", P * h + SHI, P * h + P, 16), Op.subtract, A("el", 2 * h, 2 * h + 1))
+        tr(A("tab", P * h, P * h + P), A("ex", P * h, P * h + P))
+    for h in range(N):
+        cp(A("f1f", 6 * h, 6 * h + 6), A("lf", ST * h + 6, ST * h + 12), "s")
+    for h in range(N):
+        cp(A("f2f", 6 * h, 6 * h + 6), A("lf", ST * h, ST * h + 6), "s")
+    cp(A("to0"), A("f1f"))
+    act(A("e0", 0, 96, 4), A("f1f"), -1.0)
+    tt(A("svf"), A("f1f"), A("f2f"), Op.add)
     cp(A("ex", 1024 + SHI, 1408, 16), A("svf"), "s")
-    cp(A("to0"), A("ti0"))
     first, places = A("tab", 0, 1024), A("tab")
 
     def look(t, win):
@@ -367,28 +369,33 @@ def rank_program(g, core, T, topo):
         cp(A("ga%d" % t, 0, 192), win, "v", A("to%d" % t, 0, 12))
 
     def step(t, p0, into):
-        a = [on(x, p0, 128) for x in (A("gt%d" % t), A("ga%d" % t), A("ta%d" % t), A("gt%d" % t, SHI, 384, 16), A("gt%d" % t, SLO, 384, 16), A("ti%d" % (t + 1)), A("ti%d" % t), A(into))]
+        a = [on(x, p0, 128) for x in (A("gt%d" % t), A("ga%d" % t), A("ti%d" % t), A("e%d" % t), A("gt%d" % t, SHI, 384, 4), A(into), A("ti%d" % t, 3, 96, 4))]
         tr(a[0], a[1])
-        tt(a[2], a[3], a[6], Op.subtract)
-        tt(a[5], a[2], a[4], Op.add)
-        cp(a[7], a[5])
+        scan(a[2], a[3], a[4], Op.min)
+        cp(a[5], a[6])
+        if t < 2:
+            act(A("e%d" % (t + 1), 0, 96, 4), a[6], -1.0)
+
+    def put(t, win, a):
+        for k in (0, 12):
+            sca(win, A("to%d" % t, k, k + 12), A(a, 16 * k, 16 * k + 192))
 
     look(0, first)
     tt(A("ex", 1024 + SLO, 1408, 16), A("svf"), A("ex", 1024 + SHI, 1408, 16), Op.subtract)
     tr(A("ev"), A("ex", 1024, 1408))
     step(0, 0, "to1")
-    sca(first, A("to0"), A("ev"))
+    put(0, first, "ev")
     look(1, places)
     cp(quad(A("sn"), 0), quad(A("tab", *mine), 0), "s")
     step(1, 0, "to2")
-    sca(places, A("to1"), A("ga0"))
+    put(1, places, "ga0")
     look(2, places)
     cp(quad(A("sn"), 1), quad(A("tab", *mine), 1))
     cp(on(A("ga1"), 64, 128), on(A("ga2"), 64, 128), "s")
     step(2, 64, "to2")
     sca(places, A("to2"), A("ga1"))
 
-    tt(A("un"), first, A("k1"), Op.is_equal, A("rec", 14, 20))
+    tt(A("un"), first, A("k1"), Op.is_equal, A("rec", 6, 12))
     scan(A("sc", 0, P), A("d0"), A("tab", *mine))
     scan(A("sc", P, IDS), A("d0", 0, V), A("un"))
     cp(quad(A("sn"), 2), quad(A("tab", *mine), 0), "s")

@@ -7,15 +7,17 @@ IDS = P + V
 OWN = IDS + 32
 WIN = OWN + 3 * SLOTS
 ST, MS = 20, 11
-SHI, SLO, IHI, ILO = 0, 8, 1, 9
-FLAG, ONE = 2, 18
+SHI, SP, SLO, IHI, ILO = 0, 4, 8, 1, 9
+KEEP = 3
+FLAG = 2
+BIG, BASE = 16384.0, 2048
 PLACES = 1024 + 3 * 384
 NONE = 8192.0
 MID = 176
 ZID = N * IDS
 TINY = 2.0 ** -24
 F32, I32, U16, BF, CODE, PL = "float32", "int32", "uint16", "bfloat16", "float8_e4m3fn_x4", "uint8"
-CYCLE, FLOOR, WAKE, PICK, PUT, DMA, HOP = 0.001, 64, 0.16, 1.5, 3.8, 2.0, 2.0
+CYCLE, FLOOR, WAKE, PICK, PUT, DMA, HOP = 0.001, 64, 0.16, 1.5, 3.8, 2.0, 1.8
 
 
 def _s(n, t):
@@ -23,18 +25,20 @@ def _s(n, t):
 
 
 SCRATCH = {
-    "xl": _s(28, I32), "xa": _s(32, I32), "z": _s(96, F32), "zc": _s(96, F32), "gl": _s(2, U16), "r32": _s(16, F32),
-    "pci": _s(8, I32), "pcf": _s(16, F32), "pc": _s(32, F32), "gg": _s(32, F32), "r16": _s(24, F32), "dj": _s(24, F32), "f1f": _s(24, F32), "f2f": _s(24, F32), "rec": _s(ST, U16),
-    "land": _s(N * ST, U16), "lf": _s(N * ST, F32), "ramp": _s(16, F32), "el": _s(20, U16), "ex": _s(1440, BF), "tab": _s(PLACES, BF),
-    "svf": _s(24, F32), "ev": _s(384, BF), "rk": _s(16, I32), "rkf": _s(14, F32), "ne2": _s(3, F32), "msk": _s(112, F32), "wt": _s(88, F32),
-    "a1": _s(14, F32), "any": _s(14, F32), "u1": _s(14, F32), "u2": _s(14, F32), "occ": _s(11, F32), "hm": _s(8, F32), "hz": _s(8, F32),
-    "kp": _s(3, F32), "einv": _s(192, BF), "dv": _s(192, BF), "d0": _s(P, BF), "d8": _s(112, F32), "scs": _s(448, BF), "oss": _s(448, BF),
-    "pr": _s(112, F32), "sm": _s(112, F32), "c0": _s(14, F32), "kk": _s(14, F32), "b1": _s(14, F32), "b2": _s(14, F32),
-    "dum": _s(14, F32), "dm": _s(14, F32), "adm": _s(14, F32), "stat": _s(14, F32), "fo": _s(4, U16),
-    "vai": _s(176, F32), "val": _s(176, BF), "k0": _s(V, F32), "k1": _s(V, BF), "lst": _s(4000, BF), "ma0": _s(48, F32), "ma": _s(48, F32), "mb": _s(48, F32), "mp": _s(48, F32),
-    "msg": _s(48, BF), "landm": _s(N * MS, BF), "un": _s(V, BF), "sc": _s(IDS, BF), "osd": _s(IDS, BF), "pd": _s(88, F32), "sd": _s(88, F32), "ofd": _s(12, U16),
+    "xl": _s(32, I32), "gi": _s(32, I32), "rci": _s(ST, I32), "z": _s(96, F32), "zc": _s(96, F32), "gl": _s(2, U16), "r32": _s(16, F32),
+    "pci": _s(8, I32), "pcf": _s(17, F32), "r16": _s(24, F32), "dj": _s(24, F32), "f1f": _s(24, F32), "f2f": _s(24, F32), "rec": _s(ST, U16),
+    "land": _s(N * ST, U16), "lf": _s(N * ST, F32), "ramp": _s(16, F32), "el": _s(18, U16), "elf": _s(18, F32), "kb": _s(14, F32),
+    "ex": _s(1440, BF), "tab": _s(PLACES, BF), "svf": _s(24, F32), "ev": _s(384, BF),
+    "rk": _s(14, I32), "rkf": _s(14, F32), "msk": _s(112, F32), "wt": _s(88, F32),
+    "a1": _s(11, F32), "any": _s(14, F32), "occ": _s(11, F32), "hm": _s(8, F32), "hz": _s(8, F32),
+    "kp": _s(3, F32), "kn": _s(3, F32), "einv": _s(192, BF), "dv": _s(192, BF), "d0": _s(P, BF), "w0": _s(112, F32),
+    "scs": _s(448, BF), "oss": _s(448, BF), "pr": _s(33, F32), "pq": _s(33, F32), "sm": _s(112, F32), "kk": _s(14, F32), "b1": _s(14, F32), "b2": _s(14, F32),
+    "dm": _s(11, F32), "fo": _s(4, U16),
+    "vai": _s(176, F32), "val": _s(176, BF), "k0": _s(V, F32), "one": _s(V, F32), "k1": _s(V, BF), "lst": _s(BASE + IDS, BF),
+    "ma0": _s(48, F32), "ma": _s(48, F32), "mb": _s(48, F32), "mc": _s(48, F32), "mp": _s(48, F32), "msg": _s(48, BF), "landm": _s(N * MS, BF),
+    "un": _s(V, BF), "cu": _s(IDS, BF), "mx": _s(IDS, BF), "sc": _s(IDS, BF), "osd": _s(IDS, BF), "sd": _s(88, F32), "ofd": _s(12, U16),
     "olt": _s(IDS, BF), "zb": _s(32, BF), "zt": _s(32, BF), "zg": _s(64, BF), "zh": _s(64, BF), "loff": _s(32, U16),
-    "m": _s(1440, BF), "sn": _s(P, BF), "ts": _s(P, BF), "idf": _s(8, F32), "was": _s(16, F32), "ne3": _s(8, F32), "df3": _s(8, F32), "pr3": _s(8, F32),
+    "m": _s(1440, BF), "sn": _s(P, BF), "ts": _s(P, BF), "idf": _s(32, F32),
     "ido": _s(16, U16), "mg": _s(P, BF), "om": _s(P, BF), "sl": _s(64, F32), "off": _s(64, U16),
     "cv": _s(4 * OWN, BF), "qo": _s(OWN, CODE), "qop": _s(OWN, PL), "q": _s(WIN, CODE), "qp": _s(WIN, PL),
     "sq": _s(3 * SLOTS, CODE), "sqp": _s(3 * SLOTS, PL),
@@ -51,7 +55,7 @@ for _t in range(4):
     SCRATCH["k%dq" % _t] = _s(P, CODE)
     SCRATCH["k%dp" % _t] = _s(P, PL)
 
-SEMAPHORES = ["sv", "ss", "st", "sg", "ldx", "ldc", "ldw0", "ldw1", "arrl", "arrm", "arrq", "arrp", "lsl", "lsm", "lsq", "lsp", "sty", "own"]
+SEMAPHORES = ["sv", "ss", "st", "sg", "ldx", "ldc", "ldw0", "ldw1", "arrl", "arrm", "arrq", "arrp", "lsl", "lsm", "lsq", "lsp", "own", "sty"]
 
 
 def clash(a, b):
@@ -122,6 +126,12 @@ def rank_program(g, core, T, topo):
     def quad(x, k):
         return on(x, 32 * k, 32 * k + 32)
 
+    def low(x):
+        return on(x, 0, 64)
+
+    def high(x):
+        return on(x, 64, 128)
+
     def wide(x):
         return len(range(x[1], x[2], x[3]))
 
@@ -164,11 +174,14 @@ def rank_program(g, core, T, topo):
     def act(out, a, scale, bias=0.0):
         run("s", lambda e: e.activation(ap(out), ap(a), Act.Identity, bias=sc_(bias, a), scale=sc_(scale, a)), [a] + aps(scale, bias), out)
 
+    def const(out, c):
+        act(out, on(A("vai", 0, wide(out)), out[4], out[5]), 0.0, c)
+
     def tr(out, a):
         run("v", lambda e: e.transpose(ap(out), ap(a)), [a], out)
 
-    def scan(out, a, b, op=Op.mult):
-        run("v", lambda e: e.tensor_tensor_scan(ap(out), ap(a), ap(b), 0.0, op, Op.add), [a, b], out)
+    def scan(out, a, b, op=Op.mult, start=0.0):
+        run("v", lambda e: e.tensor_tensor_scan(ap(out), ap(a), ap(b), start, op, Op.add), [a, b], out)
 
     def fill(out, c):
         run("v", lambda e: e.memset(ap(out), c), [], out)
@@ -182,8 +195,8 @@ def rank_program(g, core, T, topo):
     def quant(c, p, a):
         add("v", lambda: g.vector.quantize_mx(ap(c), ap(p), ap(a)).then_inc(T.sem.sv, 1), [a], [c, p], 0.27 * wide(a) * CYCLE)
 
-    def iota(out, pattern, base, mult=0):
-        add("g", lambda: g.iota(ap(out), pattern, base, mult, allow_small_or_imprecise_dtypes=True).then_inc(T.sem.sg, 1), [], [out], 0.13 + 2 * wide(out) * CYCLE)
+    def iota(out, pattern, base):
+        add("g", lambda: g.iota(ap(out), pattern, base, 0, allow_small_or_imprecise_dtypes=True).then_inc(T.sem.sg, 1), [], [out], 0.13 + 2 * wide(out) * CYCLE)
 
     picked, engs = [], {}
     for x in sorted(others, key=lambda x: len(topo.engines(core, T.cores[x]))):
@@ -206,87 +219,91 @@ def rank_program(g, core, T, topo):
         return [h for h in range(N) if h != x].index(y)
     afar = [x for x in ((0, r), (r + 1, N)) if x[0] < x[1]]
     mine, myv = (P * r, P * r + P), (1024 + V * r, 1024 + V * r + V)
+    left = ("left", 0, 1, 1, 0, 128)
 
-    load("ys", "ldx", [(T.xl[16 * o:16 * o + 16, a:b], n[:, :]) for n, a, b in ((T.alt, 0, 16), (T.f2, 16, 22), (T.f1, 22, 28)) for o in range(2)], [], [quad(A("xl"), 0)], 1.3)
+    load("ys", "ldx", [(T.xl[16 * o:16 * o + 16, a:b], n[:, :]) for n, a, b in ((T.alt, 0, 16), (T.f2, 16, 22), (T.f1, 22, 28)) for o in range(2)], [], [quad(A("xl", 0, 28), 0)], 1.3)
     load("y", "ldc", [(T.cv[:, 4 * P:4 * IDS], T.v[:, :]), (T.cv[:, 0:4 * P], T.c[:, :])], [], [A("cv", 0, 4 * IDS)], 2.5, [0])
 
     iota(A("z", 0, 16), [[1, 16]], 12)
     iota(A("z", 16, 32), [[2, 8], [-1, 2]], 13)
     iota(A("z", 32, 64), [[1, 2], [2, 16]], 0)
     iota(A("z", 64, 96), [[1, 32]], 0)
-    iota(A("r32"), [[32, 16]], 0)
+    fill(A("one"), 1.0)
+    scan(A("k0"), A("one"), A("one"))
+    act(A("ramp"), A("k0", 0, 16), 1.0, -1.0)
+    act(A("r32"), A("k0", 0, 16), 32.0, -32.0)
+    act(A("r16"), A("k0", 0, 24), 16.0, 1024.0 - 16)
     for a in range(0, 1440, 288):
         fill(A("ex", a, a + 288), 0.0)
-    fill(A("xa"), 0)
-    fill(A("pc"), 0.0)
-    iota(A("ex", IHI, 1024, 16), [[IDS, 4], [32, 8], [0, 2]], 0)
+    for x in (quad(A("xl", 28, 32), 0), quad(A("xl"), 1), high(A("xl"))):
+        fill(x, 0)
+    iota(A("ex", SP, 1024, 16), [[32, 32], [0, 2]], 0)
     iota(A("ex", 1024 + IHI, 1408, 16), [[IDS, 4], [32, 3], [0, 2]], P)
-    iota(A("ramp"), [[1, 16]], 0)
     iota(A("vai"), [[32, 11], [1, 16]], -MID)
-    iota(A("k0"), [[1, V]], 1)
-    iota(A("r16"), [[16, 24]], 1024)
+    for h in range(N):
+        act(A("ex", P * h + IHI, P * h + P, 16), A("ex", P * h + SP, P * h + P, 16), 1.0, float(V * h))
     tr(A("zc"), A("z"))
     cp(A("gl"), A("zc", 0, 64, 32))
     i32 = A("zc", 64, 65)
-    ts(A("pc", 16, 24), A("r32", 0, 8), i32, Op.add, float(P * r), Op.add)
     cp(A("pci", 0, 1), i32)
-    for k, (sh, m) in enumerate([(0, 15), (0, 16), (1, 7), (0, 1)]):
+    for k, (sh, m) in enumerate([(0, 15), (0, 16), (1, 7), (0, 1), (0, 7)]):
         ts(A("pci", k + 1, k + 2), A("pci", 0, 1), sh, Op.arith_shift_right, m, Op.bitwise_and)
-    cp(A("pcf", 0, 4), A("pci", 1, 5))
-    i16, o16, half, odd, xor0, xor16, lanes, sel0, ll0, isone, tiny, none, half12 = [A("pcf", k, k + 1) for k in range(13)]
-    ts(xor0, o16, -2.0, Op.mult, 16.0, Op.add)
-    tt(xor16, xor0, i32, Op.add)
+    cp(A("pcf", 0, 5), A("pci", 1, 6))
+    i16, o16, half, odd, i8, free, xor0, xor16, lanes, sel0, ll0, less, none, half12, stay, cs, vs = [A("pcf", k, k + 1) for k in range(17)]
+    act(xor0, i32, 1.0, 16.0)
+    act(xor16, o16, -2.0, xor0)
     ts(lanes, i32, float(FLAG + 12), Op.is_lt)
     ts(sel0, i16, 10.0, Op.min, 8.0, Op.mult)
-    ts(ll0, odd, 32.0, Op.mult, half, Op.add)
-    ts(isone, i32, float(ONE), Op.is_equal)
-    ts(tiny, i32, float(ONE), Op.not_equal, TINY, Op.mult)
+    act(sel0, sel0, 1.0, 4.0)
+    ts(stay, i32, float(FLAG + 12), Op.is_equal)
+    act(cs, stay, 1.0 - 2 * BASE, -1.0)
+    act(vs, stay, -1.0 - 2 * BASE, 1.0)
+    act(ll0, odd, 32.0, half)
+    act(less, i32, -1.0)
+    ts(free, i8, float(IHI), Op.not_equal)
     ts(none, i16, float(SHI), Op.is_equal, NONE, Op.mult)
-    ts(half12, half, 12.0, Op.add)
-    ts(A("el", 0, 8, 2), A("ramp", 0, 4), float(ST), Op.mult, half12, Op.add)
+    act(half12, half, 1.0, 12.0)
+    const(A("elf"), 0.0)
+    act(A("elf", 0, 8, 2), A("ramp", 0, 4), float(ST), half12)
+    const(A("elf", 8, 11), sel0)
+    for k in (12, 13):
+        act(A("elf", k, 16, 2), A("ramp", 0, 2), 16.0, i16)
+    act(A("elf", 16, 18), A("ramp", 0, 2), 8.0, ll0)
+    cp(A("el", 0, 8), A("elf", 0, 8))
+    cp(A("el", 8, 18), A("elf", 8, 18))
     act(A("dj"), A("r16"), 1.0, i16)
     for t in range(3):
-        act(A("e%d" % t), A("vai", 0, 96), 0.0, 4 * NONE)
+        const(A("e%d" % t), 4 * NONE)
         act(A("e%d" % t, 3, 96, 4), A("dj"), 1.0, 384.0 * t)
-    ts(sel0, sel0, 7.0, Op.add)
-    ts(A("el", 8, 11), A("ramp", 0, 3), 0.0, Op.mult, sel0, Op.add)
-    ts(A("el", 12, 16, 2), A("ramp", 0, 2), 16.0, Op.mult, i16, Op.add)
-    ts(A("el", 13, 16, 2), A("ramp", 0, 2), 16.0, Op.mult, i16, Op.add)
-    ts(A("el", 16, 18), A("ramp", 0, 2), 8.0, Op.mult, ll0, Op.add)
-    cp(A("el", 18, 19), A("zc", 32, 33))
     for a in range(1024, PLACES - 384, 128):
-        act(A("tab", a, a + 128), A("vai", 0, 128), 0.0, none)
-    act(A("ex", ILO, 1408, 16), A("vai", 0, 88), 0.0, i32)
-    act(A("ex", 1024 + 16 + ILO, 1408, 32), A("r32", 0, 12), 0.0, xor16)
-    act(A("ex", ONE, 1408, 32), A("vai", 0, 44), 0.0, 1.0)
+        const(A("tab", a, a + 128), none)
+    const(A("ex", ILO, 1408, 16), i32)
+    const(A("ex", 1024 + 16 + ILO, 1408, 32), xor16)
+    const(A("ex", KEEP + 8, 1408, 16), 1.0)
     for a in (0, 128):
-        act(A("d0", a, a + 128), A("vai", 0, 128), 0.0, lanes)
-    act(A("d8"), A("vai", 0, 112), 0.0, 1.0)
-    act(A("d8", 0, 112, 8), A("r32", 0, 14), 0.0)
+        const(A("d0", a, a + 128), lanes)
     act(A("val"), A("vai"), 1.0, o16)
-    act(A("k1"), A("k0"), tiny, isone)
-    act(A("msk"), A("vai", 0, 112), 0.0)
-    act(A("wt"), A("vai", 0, 88), 0.0)
-    act(A("c0", 0, 8), A("r32", 0, 8), 0.0, 1.0 - 3 * SLOTS)
-    act(A("c0", 8, 14), A("r32", 0, 6), 0.0, -4.0 * SLOTS)
-    act(A("ma0"), A("vai", 0, 48), 0.0)
-    act(A("mb"), A("vai", 0, 48), 0.0, 1.0)
-    act(A("zb"), A("vai", 0, 32), 0.0, -float(MID))
+    act(A("k1"), A("k0"), TINY)
+    for n, c in (("w0", BIG), ("wt", BIG), ("sd", 0.0), ("ma0", 0.0), ("mb", 1.0)):
+        const(A(n), c)
+    const(A("zb"), -float(MID))
     act(A("hm"), A("r32", 0, 8), 1.0, float(IDS * r - ZID))
-    ts(A("kp"), A("r32", 0, 3), i32, Op.add, 1.0, Op.add)
-    act(A("kp"), A("kp"), TINY)
-    ts(A("kk"), A("r32", 0, 14), i32, Op.add, 2.0, Op.mult)
-    fill(A("einv"), 0.0)
-    act(A("einv", ONE, 192, 32), A("r32", 0, 6), 0.0, 1.0)
+    act(A("kb"), A("r32", 0, 14), 1.0, i32)
+    act(A("kn"), A("kb", 0, 3), 1.0, 1.0)
+    act(A("kp"), A("kn"), TINY)
+    act(A("kk"), A("kb"), -1.0, float(BASE))
+    act(A("b1"), A("kb"), 1.0, BIG - BASE)
+    for a in (0, 96):
+        const(A("einv", a, a + 96), 0.0)
     fill(A("cv", 4 * IDS, 4 * OWN), 0.0)
-    fill(A("lst", 0, IDS), -float(MID))
+    for a in (BASE, BASE + MID):
+        const(A("lst", a, a + MID), -float(MID))
 
+    ts(A("gi"), A("xl"), int(NONE) - 1, Op.bitwise_and, by=A("gl"))
     for k in range(4):
-        ts(quad(A("xa", 0, 28), k), quad(A("xl"), 0), int(NONE) - 1, Op.bitwise_and)
-    tt(A("gg"), A("xa"), A("pc"), Op.add, A("gl"))
-    cp(A("rec"), A("gg", 4, 4 + ST))
-    post("arrl", "lsl", [A("rec")] * 3, [A("land", ST * r, ST * r + ST)] * 3, [A("land", ST * x, ST * x + ST) for x in others], HOP + 0.8)
-    k = load("y", "ldw0", [(T.wb[:, 0:2048], T.w[:, 0:2048])], [], [A("wb", 0, 2048), A("rec", 12, 20)], 3.5)
+        cp(quad(A("rec"), k), quad(A("gi", 4, 4 + ST), 0))
+    post("arrl", "lsl", [A("rec")] * 3 + [left], [A("land", ST * r, ST * r + ST)] * 3, [A("land", ST * x, ST * x + ST) for x in others], HOP + 1.0)
+    k = load("y", "ldw0", [(T.wb[:, 0:2048], T.w[:, 0:2048])], [], [A("wb", 0, 2048), left], 3.5)
     load("y", "ldw1", [(T.wb[:, 2048:4096], T.w[:, 2048:4096])], [], [A("wb", 2048, 4096)], 5.0, [k])
     for a in range(0, OWN, 128):
         quant(A("qo", a, a + 128), A("qop", a, a + 128), A("cv", 4 * a, 4 * a + 512))
@@ -296,8 +313,11 @@ def rank_program(g, core, T, topo):
 
     def mk(j, a=0, b=14):
         return A("msk", 8 * a + j, 8 * b, 8) if j < 3 else A("any", a, b)
-    ts(A("rk"), A("xa"), 8, Op.arith_shift_right, by=A("el", 18, 19))
-    ts(A("rkf"), A("rk", 0, 14), float(r), Op.subtract)
+    cp(A("rci"), A("rec"))
+    ts(A("rk", 0, 8), A("rci", 12, 20), 8, Op.arith_shift_right)
+    ts(A("rk", 8, 14), A("rci", 0, 12, 2), 8, Op.arith_shift_right)
+    ts(A("lf", ST * r, ST * r + ST), A("rec"), i32, Op.add)
+    ts(A("rkf"), A("rk"), float(r), Op.subtract)
     ts(A("occ", 0, 8), A("rk", 0, 8), float(N), Op.is_lt)
     tt(A("occ", 8, 11), A("rk", 8, 11), A("rk", 11, 14), Op.not_equal)
     tt(A("rkf", 0, 11), A("rkf", 0, 11), A("occ"), Op.mult)
@@ -305,114 +325,103 @@ def rank_program(g, core, T, topo):
         ts(mk(j), A("rkf"), float(x - r), Op.is_equal)
     ts(A("any"), A("rkf"), 0.0, Op.not_equal)
     tt(A("hz"), A("hm"), A("occ", 0, 8), Op.mult)
-    tt(A("a1"), mk(0), mk(1), Op.add)
     for o in (0, 16):
-        cp(A("ex", mine[0] + o + SHI, mine[1], 32), A("gg", 16, 24), "s")
-        tt(A("ex", mine[0] + o + SLO, mine[1], 32), A("gg", 16, 24), A("ex", mine[0] + o + SHI, mine[1], 32), Op.subtract)
+        cp(A("ex", mine[0] + o + SHI, mine[1], 32), A("lf", ST * r + 12, ST * r + ST), "s")
+        tt(A("ex", mine[0] + o + SLO, mine[1], 32), A("lf", ST * r + 12, ST * r + ST), A("ex", mine[0] + o + SHI, mine[1], 32), Op.subtract)
         act(A("ex", mine[0] + o + IHI, mine[1], 32), A("hz"), 1.0, float(ZID))
         act(A("ex", mine[0] + o + ILO, mine[1], 32), A("occ", 0, 8), i32)
     for j in range(4):
         act(A("ex", mine[0] + FLAG + 4 * j, mine[1], 32), mk(j, 0, 8), -1.0)
-        tt(A("ex", myv[0] + FLAG + 4 * j, myv[1], 32), mk(j, 8, 11), A("kp"), Op.mult)
+    for b in range(3):
+        act(A("ex", myv[0] + 32 * b + FLAG, myv[0] + 32 * b + FLAG + 12, 4), A("msk", 64 + 8 * b, 67 + 8 * b), A("kp", b, b + 1))
+    tt(A("ex", myv[0] + FLAG + 12, myv[1], 32), mk(3, 8, 11), A("kp"), Op.mult)
     tr(A("tab", *mine), A("ex", *mine))
-    cp(A("lf", ST * r, ST * r + ST), A("gg", 4, 4 + ST), "s")
     for j in range(3):
         cp(A("einv", FLAG + 4 * j, 96, 32), mk(j, 11, 14), "s")
         cp(A("einv", 96 + FLAG + 4 * j, 192, 32), mk(j, 8, 11), "s")
-        cp(A("wt", j, 88, 8), mk(j, 0, 11), "s")
-    tt(A("u1"), A("any"), A("a1"), Op.add)
-    tt(A("u2"), A("u1"), mk(0), Op.add)
-    ts(A("b1"), A("u2"), -900.0, Op.mult, 3100.0, Op.add)
-    act(A("b2"), A("u2"), float(SLOTS))
-    tt(A("dum"), A("b1"), A("kk"), Op.add)
-    tt(A("msk", 4, 112, 8), A("b2"), A("c0"), Op.add)
+        act(A("w0", j, 64, 8), mk(j, 0, 8), 1.0 - SLOTS * j - (4 - j) * BIG, BIG)
+        act(A("w0", 64 + j, 112, 8), mk(j, 8, 14), -SLOTS * (j + 1.0) - (4 - j) * BIG, BIG)
+    act(A("w0", 3, 112, 8), A("any"), -BIG, BIG)
+    act(A("wt", 3, 88, 8), A("any", 0, 11), -BIG, BIG)
+    tt(A("b2"), A("b1"), A("any"), Op.mult)
+    tt(A("w0", 4, 112, 8), A("b2"), A("kk"), Op.add)
+    act(A("a1"), A("any", 0, 11), 2.0 * BASE)
+    tt(A("wt", 4, 88, 8), A("a1"), A("kb", 0, 11), Op.add)
     tr(A("dv"), A("einv"))
     scan(A("scs", 0, P), A("d0"), A("tab", *mine))
     scan(A("scs", P, 448), A("d0", 0, 192), A("dv"))
     tr(A("oss", 0, P), A("scs", 0, P))
     tr(A("oss", IDS, 448), A("scs", P, IDS))
     tr(A("oss", P, IDS), A("scs", IDS, 448))
-    for a, b in ((0, 7), (7, 14)):
-        tt(A("pr", 8 * a, 8 * b), A("oss", 32 * a + FLAG, 32 * b, 4), A("msk", 8 * a, 8 * b), Op.mult)
-    scan(A("sm"), A("d8"), A("pr"))
-    tt(A("dm"), A("dum"), A("sm", 7, 112, 8), Op.add)
-    tt(A("adm"), A("dm"), A("any"), Op.mult)
-    tt(A("stat"), A("dum"), A("adm"), Op.subtract)
-    cp(A("fo", 0, 3), A("stat", 11, 14))
-    act(A("wt", 3, 64, 8), A("dm", 0, 8), -1.0)
-    cp(A("wt", 67, 88, 8), A("dm", 8, 11), "s")
-    cp(A("wt", 4, 88, 8), A("stat", 0, 11), "s")
+    scan(A("sm"), A("oss", FLAG, 448, 4), A("w0"), Op.min, BIG)
+    ts(A("fo", 0, 3), A("sm", 92, 112, 8), -1.0, Op.mult, float(BASE), Op.add)
+    tt(A("dm"), A("sm", 4, 88, 8), A("kb", 0, 11), Op.add)
     for j in range(3):
-        tt(A("ma0", 16 * j + 8, 16 * j + 11), mk(j, 11, 14), A("sm", 95, 112, 8), Op.mult)
+        act(A("pr", 11 * j, 11 * j + 11), A("dm"), -1.0, -BASE - (3 - j) * BIG)
+        tt(A("pq", 11 * j, 11 * j + 11), A("pr", 11 * j, 11 * j + 11), mk(j, 0, 11), Op.mult)
+        act(A("wt", j, 88, 8), A("pq", 11 * j, 11 * j + 11), 1.0, BIG)
+        act(A("ma0", 8 + j, 48, 16), A("msk", 88 + 8 * j, 91 + 8 * j), A("sm", 92 + 8 * j, 93 + 8 * j))
         act(A("mb", 16 * j + 8, 16 * j + 11), mk(j, 11, 14), -1.0, 1.0)
-    act(A("ma"), A("ma0"), -1.0, -float(MID))
+    act(A("mc"), A("mb"), -float(BASE), -float(MID))
+    tt(A("ma"), A("mc"), A("ma0"), Op.subtract)
     sca(A("lst"), A("fo", 0, 3), A("val", 128, 176))
 
     for a, b in afar:
-        cp(A("lf", ST * a, ST * b), A("land", ST * a, ST * b))
+        ts(A("lf", ST * a, ST * b), A("land", ST * a, ST * b), i32, Op.add)
     for h in others:
         cp(A("ex", P * h + SHI, P * h + P, 16), A("lf"), "v", A("el", 2 * h, 2 * h + 1))
         tt(A("ex", P * h + SLO, P * h + P, 16), A("lf"), A("ex", P * h + SHI, P * h + P, 16), Op.subtract, A("el", 2 * h, 2 * h + 1))
         tr(A("tab", P * h, P * h + P), A("ex", P * h, P * h + P))
-    for h in range(N):
-        cp(A("f1f", 6 * h, 6 * h + 6), A("lf", ST * h + 6, ST * h + 12), "s")
-    for h in range(N):
-        cp(A("f2f", 6 * h, 6 * h + 6), A("lf", ST * h, ST * h + 6), "s")
+    for n, a in (("f1f", 6), ("f2f", 0)):
+        for h in range(N):
+            act(A(n, 6 * h, 6 * h + 6), A("lf", ST * h + a, ST * h + a + 6), 1.0, less)
     cp(A("to0"), A("f1f"))
     act(A("e0", 0, 96, 4), A("f1f"), -1.0)
     tt(A("svf"), A("f1f"), A("f2f"), Op.add)
     cp(A("ex", 1024 + SHI, 1408, 16), A("svf"), "s")
+    tt(A("ex", 1024 + SLO, 1408, 16), A("svf"), A("ex", 1024 + SHI, 1408, 16), Op.subtract)
+    tr(A("ev"), A("ex", 1024, 1408))
     first, places = A("tab", 0, 1024), A("tab")
 
     def look(t, win):
         cp(A("ga%d" % t, 192, 384), win, "s", A("to%d" % t, 12, 24))
         cp(A("ga%d" % t, 0, 192), win, "v", A("to%d" % t, 0, 12))
-
-    def step(t, p0, into):
-        a = [on(x, p0, 128) for x in (A("gt%d" % t), A("ga%d" % t), A("ti%d" % t), A("e%d" % t), A("gt%d" % t, SHI, 384, 4), A(into), A("ti%d" % t, 3, 96, 4))]
-        tr(a[0], a[1])
-        scan(a[2], a[3], a[4], Op.min)
-        cp(a[5], a[6])
+        tr(A("gt%d" % t), A("ga%d" % t))
+        scan(A("ti%d" % t), A("e%d" % t), A("gt%d" % t, SHI, 384, 4), Op.min)
         if t < 2:
-            act(A("e%d" % (t + 1), 0, 96, 4), a[6], -1.0)
+            cp(A("to%d" % (t + 1)), A("ti%d" % t, 3, 96, 4))
+            act(A("e%d" % (t + 1), 0, 96, 4), A("ti%d" % t, 3, 96, 4), -1.0)
+        if t > 0:
+            cp(high(A("to%d" % t)), low(A("ti%d" % t, 3, 96, 4)))
+            cp(high(A("ga%d" % (t - 1))), low(A("ga%d" % t)), "s")
 
-    def put(t, win, a):
-        for k in (0, 12):
-            sca(win, A("to%d" % t, k, k + 12), A(a, 16 * k, 16 * k + 192))
+    def put(t, win, a, n):
+        for k in range(0, 24, n):
+            sca(win, A("to%d" % t, k, k + n), A(a, 16 * k, 16 * (k + n)))
 
     look(0, first)
-    tt(A("ex", 1024 + SLO, 1408, 16), A("svf"), A("ex", 1024 + SHI, 1408, 16), Op.subtract)
-    tr(A("ev"), A("ex", 1024, 1408))
-    step(0, 0, "to1")
-    put(0, first, "ev")
+    put(0, first, "ev", 12)
     look(1, places)
     cp(quad(A("sn"), 0), quad(A("tab", *mine), 0), "s")
-    step(1, 0, "to2")
-    put(1, places, "ga0")
-    look(2, places)
-    cp(quad(A("sn"), 1), quad(A("tab", *mine), 1))
-    cp(on(A("ga1"), 64, 128), on(A("ga2"), 64, 128), "s")
-    step(2, 64, "to2")
-    sca(places, A("to2"), A("ga1"))
+    put(1, places, "ga0", 24)
 
     tt(A("un"), first, A("k1"), Op.is_equal, A("rec", 6, 12))
-    scan(A("sc", 0, P), A("d0"), A("tab", *mine))
-    scan(A("sc", P, IDS), A("d0", 0, V), A("un"))
-    cp(quad(A("sn"), 2), quad(A("tab", *mine), 0), "s")
-    cp(quad(A("sn"), 3), quad(A("tab", *mine), 3), "s")
-    tr(A("osd", 0, P), A("sc", 0, P))
-    tr(A("osd", P, IDS), A("sc", P, IDS))
-    tt(A("pd", 0, 64), A("osd", FLAG, P, 4), A("wt", 0, 64), Op.mult)
-    tt(A("pd", 64, 88), A("osd", P + FLAG, IDS, 4), A("wt", 64, 88), Op.mult)
-    scan(A("sd"), A("d8", 0, 88), A("pd"))
-    for p in (0, 64):
-        cp(on(A("ofd", 0, 11), p, p + 64), on(A("sd", 7, 88, 8), 0, 64))
+    act(low(A("cu", 0, P)), high(A("tab", *mine)), cs)
+    act(low(A("cu", P, IDS)), high(A("un")), vs)
+    tt(low(A("mx", 0, P)), low(A("tab", *mine)), low(A("cu", 0, P)), Op.mult)
+    tt(low(A("mx", P, IDS)), low(A("un")), low(A("cu", P, IDS)), Op.mult)
+    for a, b in ((0, P), (P, IDS)):
+        scan(low(A("sc", a, b)), low(A("d0", 0, b - a)), low(A("mx", a, b)))
+        tr(low(A("osd", a, b)), low(A("sc", a, b)))
+    scan(low(A("sd")), low(A("osd", FLAG, IDS, 4)), low(A("wt")), Op.min, BIG)
+    for half_ in (low, high):
+        cp(half_(A("ofd", 0, 11)), low(A("sd", 4, 88, 8)))
     tt(A("mp"), A("sd"), A("mb"), Op.mult, A("el", 8, 11))
-    for p in (0, 64):
-        tt(on(A("msg"), p, p + 64), on(A("mp"), 0, 64), on(A("ma"), 0, 64), Op.add)
+    for half_ in (low, high):
+        tt(half_(A("msg")), low(A("mp")), low(A("ma")), Op.add)
     post("arrm", "lsm", [A("msg", 16 * j, 16 * j + MS) for j in range(3)], [A("landm", MS * r, MS * r + MS)] * 3, [A("landm", MS * x, MS * x + MS) for x in others])
     sca(A("lst"), A("ofd", 0, 11), A("val"))
-    tr(A("olt"), A("lst", 0, IDS))
+    tr(A("olt"), A("lst", BASE, BASE + IDS))
     tt(A("zb", 0, 11), A("olt", 0, IDS, 32), A("olt", 16, IDS, 32), Op.max)
     tr(A("zt"), A("zb"))
     cp(A("zg"), A("zt"), "v", A("el", 12, 16))
@@ -424,28 +433,30 @@ def rank_program(g, core, T, topo):
     k = post("arrp", "lsp", [A("sqp", SLOTS * j, SLOTS * j + SLOTS) for j in range(3)], [A("qp", x, x + SLOTS) for x in at], [A("qp", OWN, WIN)])
     post("arrq", "lsq", [A("sq", SLOTS * j, SLOTS * j + SLOTS) for j in range(3)], [A("q", x, x + SLOTS) for x in at], [A("q", OWN, WIN)], HOP + 0.5, [k])
 
-    for h in others:
-        act(A("ex", IDS * h + SLO, IDS * h + IDS, 16), A("vai", 0, 22), 0.0, float(OWN + SLOTS * (turn(r, h) - turn(h, r)) + MID))
+    cp(quad(A("sn"), 1), quad(A("tab", *mine), 1), "s")
+    act(high(A("tab", *mine)), high(A("d0")), 0.0, free)
+    look(2, places)
+    put(2, places, "ga1", 24)
+    tr(low(A("ts")), low(A("sn")))
+    tr(quad(A("ts"), 2), quad(A("tab", *mine), 0))
+    cp(on(A("tab", *mine), 96, 112), on(A("tab", *mine), 0, 16), "s")
+    tr(quad(A("ts"), 3), quad(A("tab", *mine), 3))
+    scan(A("idf"), A("ts", KEEP, P, 8), A("ts", IHI, P, 8))
+    for k in range(2):
+        cp(A("ido", k, 16, 2), A("idf", 3, 32, 4))
+    for h in range(N):
+        ids = (IDS * h, IDS * h + IDS)
+        if h != r:
+            const(A("ex", ids[0] + SLO, ids[1], 16), float(OWN + SLOTS * (turn(r, h) - turn(h, r)) + MID))
         for o in (0, 16):
-            cp(A("ex", IDS * h + o + SHI, IDS * h + IDS, 32), A("landm", MS * h, MS * h + MS), "s")
-        tr(A("m", IDS * h, IDS * h + IDS), A("ex", IDS * h, IDS * h + IDS))
-    for o in (0, 16):
-        cp(A("ex", IDS * r + o + SLO, IDS * r + IDS, 32), A("r32", 0, 11), "s")
-        act(A("ex", IDS * r + o + SHI, IDS * r + IDS, 32), A("r32", 0, 11), 0.0, i32)
-    act(A("ex", ZID, 1440, 8), A("r32", 0, 4), 0.0, IDS / 2)
-    tr(A("m", IDS * r, IDS * r + IDS), A("ex", IDS * r, IDS * r + IDS))
+            if h != r:
+                cp(A("ex", ids[0] + o + SHI, ids[1], 32), A("landm", MS * h, MS * h + MS), "s")
+            else:
+                cp(A("ex", ids[0] + o + SLO, ids[1], 32), A("r32", 0, 11), "s")
+                const(A("ex", ids[0] + o + SHI, ids[1], 32), i32)
+        tr(A("m", *ids), A("ex", *ids))
+    const(A("ex", ZID, 1440, 8), IDS / 2)
     tr(A("m", ZID, 1440), A("ex", ZID, 1440))
-    tr(A("ts"), A("sn"))
-    tt(A("idf"), A("ts", IHI, P, 32), A("ts", ILO, P, 32), Op.add)
-    was = [quad(A("was", 8 * k, 8 * k + 8), 3) for k in range(2)]
-    for k in range(2):
-        cp(was[k], quad(A("idf"), k + 1), "s")
-    tt(quad(A("ne3"), 3), quad(A("idf"), 3), was[0], Op.not_equal)
-    tt(quad(A("df3"), 3), quad(A("idf"), 3), was[1], Op.subtract)
-    tt(quad(A("pr3"), 3), quad(A("ne3"), 3), quad(A("df3"), 3), Op.mult)
-    tt(quad(A("idf"), 3), quad(A("pr3"), 3), was[1], Op.add)
-    for k in range(2):
-        cp(A("ido", k, 16, 2), A("idf"))
     cp(A("mg", 128, 256), A("m"), "s", A("ido", 8, 16))
     cp(A("mg", 0, 128), A("m"), "v", A("ido", 0, 8))
     tr(A("om"), A("mg"))
@@ -454,16 +465,20 @@ def rank_program(g, core, T, topo):
     for k in range(4):
         cp(quad(A("off"), k), quad(A("sl"), 0))
 
+    last = []
     for t in range(R):
-        kq, kp = A("k%dq" % t), A("k%dp" % t)
-        cp(kp, A("qp"), "s", A("off", 16 * t, 16 * t + 16))
-        pick(kq, A("q"), A("off", 16 * t, 16 * t + 16))
-        for i in range(O * t, O * t + O):
-            a = [A("ps", 512 * i, 512 * i + P), A("wq", 128 * i, 128 * i + 128), A("wp", 128 * i, 128 * i + 128), kq, kp]
-            add("t", lambda a=a: g.tensor.matmul_mx(*[ap(x) for x in a], True, True).then_inc(T.sem.st, 1), a[1:], a[:1], 0.33)
-            reg = A("ys", P * i, P * i + P)
-            cp(reg, a[0], "vs"[i % 2])
-            load("y", "sty", [(T.y[:, P * i:P * i + P], ap(reg))], [reg], [], DMA + 0.4 * (R * O - i))
+        n = P if t else P // 2
+        for a in range(0, P, n):
+            kq, kp, by = A("k%dq" % t, a, a + n), A("k%dp" % t, a, a + n), A("off", 16 * t + a // 16, 16 * t + (a + n) // 16)
+            cp(kp, A("qp"), "s", by)
+            pick(kq, A("q"), by)
+            for i in range(O * t, O * t + O):
+                bank = 512 * (i + (R * O - O) * (a > 0))
+                x = [A("ps", bank, bank + n), A("wq", 128 * i, 128 * i + 128), A("wp", 128 * i, 128 * i + 128), kq, kp]
+                last = [add("t", lambda x=x: g.tensor.matmul_mx(*[ap(y) for y in x], True, True).then_inc(T.sem.st, 1), x[1:], [A("ps", bank, bank + 512)], 1.2 * (n + 16) * CYCLE, also=last)]
+                reg = A("ys", P * i + a, P * i + a + n)
+                cp(reg, x[0], "vs"[i % 2])
+                load("y", "sty", [(T.y[:, reg[1]:reg[2]], ap(reg))], [reg], [], DMA + 0.4 * (R * O - i))
 
     known, log, total = {k: {} for k in eng}, {}, {}
     for c in in_order(calls):

@@ -17,7 +17,7 @@ MID = 176
 ZID = N * IDS
 TINY = 2.0 ** -24
 F32, I32, U16, BF, CODE, PL = "float32", "int32", "uint16", "bfloat16", "float8_e4m3fn_x4", "uint8"
-CYCLE, FLOOR, WAKE, PICK, PUT, DMA, HOP = 0.001, 64, 0.16, 1.5, 3.8, 2.0, 1.8
+CYCLE, FLOOR, WAKE, PICK, PUT, DMA, HOP, NEAR = 0.001, {"v": 64, "s": 90}, 0.16, 1.5, 3.8, 2.0, 1.8, 0.01
 
 
 def _s(n, t):
@@ -26,8 +26,8 @@ def _s(n, t):
 
 SCRATCH = {
     "xl": _s(32, I32), "gi": _s(32, I32), "rci": _s(ST, I32), "z": _s(96, F32), "zc": _s(96, F32), "gl": _s(2, U16), "r32": _s(16, F32),
-    "pci": _s(8, I32), "pcf": _s(17, F32), "r16": _s(24, F32), "dj": _s(24, F32), "f1f": _s(24, F32), "f2f": _s(24, F32), "rec": _s(ST, U16),
-    "land": _s(N * ST, U16), "lf": _s(N * ST, F32), "ramp": _s(16, F32), "el": _s(18, U16), "elf": _s(18, F32), "kb": _s(14, F32),
+    "pci": _s(8, I32), "pcf": _s(17, F32), "e": _s(288, F32), "ff": _s(48, F32), "rec": _s(ST, U16),
+    "land": _s(N * ST, U16), "lf": _s(N * ST, F32), "ramp": _s(2, F32), "el": _s(12, U16), "kb": _s(14, F32),
     "ex": _s(1440, BF), "tab": _s(PLACES, BF), "svf": _s(24, F32), "ev": _s(384, BF),
     "rk": _s(14, I32), "rkf": _s(14, F32), "msk": _s(112, F32), "wt": _s(88, F32),
     "a1": _s(11, F32), "any": _s(14, F32), "occ": _s(11, F32), "hm": _s(8, F32), "hz": _s(8, F32),
@@ -35,9 +35,9 @@ SCRATCH = {
     "scs": _s(448, BF), "oss": _s(448, BF), "pr": _s(33, F32), "pq": _s(33, F32), "sm": _s(112, F32), "kk": _s(14, F32), "b1": _s(14, F32), "b2": _s(14, F32),
     "dm": _s(11, F32), "fo": _s(4, U16),
     "vai": _s(176, F32), "val": _s(176, BF), "k0": _s(V, F32), "one": _s(V, F32), "k1": _s(V, BF), "lst": _s(BASE + IDS, BF),
-    "ma0": _s(48, F32), "ma": _s(48, F32), "mb": _s(48, F32), "mc": _s(48, F32), "mp": _s(48, F32), "msg": _s(48, BF), "landm": _s(N * MS, BF),
+    "ma": _s(6, F32), "mb": _s(9, F32), "mc": _s(3, F32), "msg": _s(3 * MS, BF), "landm": _s(N * MS, BF),
     "un": _s(V, BF), "cu": _s(IDS, BF), "mx": _s(IDS, BF), "sc": _s(IDS, BF), "osd": _s(IDS, BF), "sd": _s(88, F32), "ofd": _s(12, U16),
-    "olt": _s(IDS, BF), "zb": _s(32, BF), "zt": _s(32, BF), "zg": _s(64, BF), "zh": _s(64, BF), "loff": _s(32, U16),
+    "olt": _s(2 * IDS, BF), "zb": _s(32, BF), "loff": _s(32, U16), "lt": _s(4, F32),
     "m": _s(1440, BF), "sn": _s(P, BF), "ts": _s(P, BF), "idf": _s(32, F32),
     "ido": _s(16, U16), "mg": _s(P, BF), "om": _s(P, BF), "sl": _s(64, F32), "off": _s(64, U16),
     "cv": _s(4 * OWN, BF), "qo": _s(OWN, CODE), "qop": _s(OWN, PL), "q": _s(WIN, CODE), "qp": _s(WIN, PL),
@@ -48,20 +48,20 @@ SCRATCH = {
 for _t in range(3):
     SCRATCH["ga%d" % _t] = _s(384, BF)
     SCRATCH["gt%d" % _t] = _s(384, BF)
-    SCRATCH["e%d" % _t] = _s(96, F32)
     SCRATCH["ti%d" % _t] = _s(96, F32)
     SCRATCH["to%d" % _t] = _s(24, U16)
 for _t in range(4):
     SCRATCH["k%dq" % _t] = _s(P, CODE)
     SCRATCH["k%dp" % _t] = _s(P, PL)
 
-SEMAPHORES = ["sv", "ss", "st", "sg", "ldx", "ldc", "ldw0", "ldw1", "arrl", "arrm", "arrq", "arrp", "lsl", "lsm", "lsq", "lsp", "own", "sty"]
+SEMAPHORES = ["sv", "ss", "st", "sg", "ldx", "ldc", "ldw0", "ldw1", "lsl", "lsm", "lsq", "lsp", "own", "arrl", "arrp", "arrq", "sty"] + ["arrm%d" % x for x in range(N)]
 
 
 def clash(a, b):
     if a[0] != b[0] or a[1] >= b[2] or b[1] >= a[2] or a[4] >= b[5] or b[4] >= a[5]:
         return False
-    return not (a[3] == b[3] and a[3] > 1 and (a[1] - b[1]) % a[3])
+    a, b = sorted((range(*a[1:4]), range(*b[1:4])), key=len)
+    return any(x in b for x in a)
 
 
 def in_order(calls):
@@ -82,16 +82,20 @@ def in_order(calls):
             chain[j] = max(chain[j], calls[j]["hold"] + chain[k])
     done, free, left, out = {}, {}, set(range(len(calls))), []
     while left:
-        start = {k: max([free.get(calls[k]["q"], 0.0)] + [done[j] + WAKE for j in calls[k]["after"]] + [done[j] - calls[j]["late"] for j in calls[k]["also"]])
+        ready = {k: max([0.0] + [done[j] + WAKE for j in calls[k]["after"]] + [done[j] - calls[j]["late"] for j in calls[k]["also"]])
                  for k in left if calls[k]["after"] | set(calls[k]["also"]) <= set(done)}
         best = []
-        for q in {calls[k]["q"] for k in start}:
-            mine = sorted((k for k in start if calls[k]["q"] == q), key=lambda k: (-chain[k], k))
-            fits = [k for k in mine if start[k] + calls[k]["hold"] <= start[mine[0]] + WAKE / 4]
-            best.append((fits + mine)[0])
-        k = min(best, key=lambda k: (start[k], k))
-        free[calls[k]["q"]] = start[k] + calls[k]["hold"]
-        done[k] = start[k] + calls[k]["hold"] + calls[k]["late"]
+        for q in {x for k in ready for x in calls[k]["q"]}:
+            start = {k: max(free.get(q, 0.0), t) for k, t in ready.items() if q in calls[k]["q"]}
+            fits = sorted(start, key=lambda k: (calls[k]["q"][0] != q, -chain[k], k))
+            while fits:
+                top = fits[0]
+                fits = [k for k in fits[1:] if start[k] + calls[k]["hold"] <= start[top] + WAKE / 4]
+            best.append((start[top], calls[top]["q"][0] != q, top, q))
+        t, _, k, q = min(best)
+        free[q] = t + calls[k]["hold"]
+        done[k] = t + calls[k]["hold"] + calls[k]["late"]
+        calls[k].update(q=q, done=done[k])
         left.remove(k)
         out.append(calls[k])
     return out
@@ -140,11 +144,11 @@ def rank_program(g, core, T, topo):
             hold = 0.06 + 16 * wide(by) * per * CYCLE
         else:
             short = per < 2 and q == "v" and all(SCRATCH[x[0]][2] in (BF, U16) for x in reads[:1] + [out])
-            hold = max(FLOOR, wide(out) * (0.5 if short else per)) * CYCLE
-        add(q, lambda: call(eng[q]).then_inc(T.sem[sem_of[q]], 1), reads + aps(by), [out], hold)
+            hold = max(FLOOR[q[0]], wide(out) * (0.5 if short else per)) * CYCLE
+        add(q, lambda q: call(eng[q]).then_inc(T.sem[sem_of[q]], 1), reads + aps(by), [out], hold)
 
     def load(q, sem, pairs, reads=(), writes=None, late=DMA, also=()):
-        def go():
+        def go(_):
             for k, (o, i) in enumerate(pairs):
                 eng[q[k % len(q)]].dma_start(o, i).then_inc(T.sem[sem], 16)
         return add(q[0], go, reads, writes, 0.06 * len(pairs), late, sem, 16 * len(pairs), also)
@@ -168,11 +172,17 @@ def rank_program(g, core, T, topo):
     def cp(out, a, q="v", by=None):
         if q == "v":
             run("v", lambda e: e.tensor_copy(ap(out), via(a, by)), [a], out, 1.0 if by is None else PICK, by)
+        elif by is None and wide(out) <= FLOOR["v"]:
+            act(out, a, 1.0)
         else:
             run("s", lambda e: e.activation(ap(out), via(a, by), Act.Copy), [a], out, 1.0 if by is None else PICK, by)
 
     def act(out, a, scale, bias=0.0):
-        run("s", lambda e: e.activation(ap(out), ap(a), Act.Identity, bias=sc_(bias, a), scale=sc_(scale, a)), [a] + aps(scale, bias), out)
+        def call(e):
+            if e is eng["v"]:
+                return e.tensor_scalar(ap(out), ap(a), sc_(scale, a), sc_(bias, a), Op.mult, Op.add)
+            return e.activation(ap(out), ap(a), Act.Identity, bias=sc_(bias, a), scale=sc_(scale, a))
+        run("sv" if wide(out) <= FLOOR["v"] else "s", call, [a] + aps(scale, bias), out)
 
     def const(out, c):
         act(out, on(A("vai", 0, wide(out)), out[4], out[5]), 0.0, c)
@@ -193,10 +203,10 @@ def rank_program(g, core, T, topo):
         run("v", lambda e: e.tensor_copy(ap(out).bitcast(dt.uint32), ap(win).bitcast(dt.uint32).indirect(ap(off))), [win], out, PICK, off)
 
     def quant(c, p, a):
-        add("v", lambda: g.vector.quantize_mx(ap(c), ap(p), ap(a)).then_inc(T.sem.sv, 1), [a], [c, p], 0.27 * wide(a) * CYCLE)
+        add("v", lambda _: g.vector.quantize_mx(ap(c), ap(p), ap(a)).then_inc(T.sem.sv, 1), [a], [c, p], 0.27 * wide(a) * CYCLE)
 
     def iota(out, pattern, base):
-        add("g", lambda: g.iota(ap(out), pattern, base, 0, allow_small_or_imprecise_dtypes=True).then_inc(T.sem.sg, 1), [], [out], 0.13 + 2 * wide(out) * CYCLE)
+        add("g", lambda _: g.iota(ap(out), pattern, base, 0, allow_small_or_imprecise_dtypes=True).then_inc(T.sem.sg, 1), [], [out], 0.13 + 2 * wide(out) * CYCLE)
 
     picked, engs = [], {}
     for x in sorted(others, key=lambda x: len(topo.engines(core, T.cores[x]))):
@@ -204,35 +214,36 @@ def rank_program(g, core, T, topo):
         picked += e
         engs[x] = e
 
-    def post(sem, lsem, srcs, dsts, lands, late=HOP, also=()):
-        def go():
+    def post(sem, lsem, srcs, dsts, lands, late=HOP, also=(), use=slice(4)):
+        def go(_):
             trs = []
             for j, x in enumerate(others):
                 rid, pid, _ = topo.addr(T.cores[x])
-                trs.append(RemoteDMATransfer(dst_ids=[DstId(rid=rid, pnc=pid)], dma_engine_mask=sum(1 << k for k in engs[x]), remote_sem=T.sem[sem], src=raw(srcs[j]), dst=raw(dsts[j])))
+                trs.append(RemoteDMATransfer(dst_ids=[DstId(rid=rid, pnc=pid)], dma_engine_mask=sum(1 << k for k in engs[x][use]), remote_sem=T.sem[sem + str(r) * apart], src=raw(srcs[j]), dst=raw(dsts[j])))
             g.remote_dma_fused(trs, local_sem=T.sem[lsem])
-        k = add("g", go, srcs, [], 0.4, 0.0, lsem, 12, also)
-        add("far", None, [], lands, 0.0, late, sem, 12, [k])
+        apart = len(lands) > 1
+        n = len(range(4)[use])
+        k = add("g", go, srcs, [], 0.4, 0.0, lsem, 3 * n, also)
+        for x, land in zip(others, lands):
+            add("f", None, [], [land], 0.0, late - NEAR * (topo.chip(T.cores[x]) == topo.chip(core)), sem + str(x) * apart, n if apart else 3 * n, [k])
         return k
 
     def turn(x, y):
         return [h for h in range(N) if h != x].index(y)
-    afar = [x for x in ((0, r), (r + 1, N)) if x[0] < x[1]]
     mine, myv = (P * r, P * r + P), (1024 + V * r, 1024 + V * r + V)
     left = ("left", 0, 1, 1, 0, 128)
 
     load("ys", "ldx", [(T.xl[16 * o:16 * o + 16, a:b], n[:, :]) for n, a, b in ((T.alt, 0, 16), (T.f2, 16, 22), (T.f1, 22, 28)) for o in range(2)], [], [quad(A("xl", 0, 28), 0)], 1.3)
-    load("y", "ldc", [(T.cv[:, 4 * P:4 * IDS], T.v[:, :]), (T.cv[:, 0:4 * P], T.c[:, :])], [], [A("cv", 0, 4 * IDS)], 2.5, [0])
+    load("y", "ldc", [(T.cv[:, 4 * P:4 * IDS], T.v[:, :]), (T.cv[:, 0:4 * P], T.c[:, :])], [], [A("cv", 0, 4 * IDS)], 4.0, [0])
 
-    iota(A("z", 0, 16), [[1, 16]], 12)
-    iota(A("z", 16, 32), [[2, 8], [-1, 2]], 13)
+    iota(A("z", 0, 16), [[1, 8], [6, 2]], 14)
+    iota(A("z", 16, 32), [[2, 4], [-1, 2], [6, 2]], 15)
     iota(A("z", 32, 64), [[1, 2], [2, 16]], 0)
     iota(A("z", 64, 96), [[1, 32]], 0)
     fill(A("one"), 1.0)
     scan(A("k0"), A("one"), A("one"))
-    act(A("ramp"), A("k0", 0, 16), 1.0, -1.0)
+    act(A("ramp"), A("k0", 0, 2), 1.0, -1.0)
     act(A("r32"), A("k0", 0, 16), 32.0, -32.0)
-    act(A("r16"), A("k0", 0, 24), 16.0, 1024.0 - 16)
     for a in range(0, 1440, 288):
         fill(A("ex", a, a + 288), 0.0)
     for x in (quad(A("xl", 28, 32), 0), quad(A("xl"), 1), high(A("xl"))):
@@ -240,8 +251,7 @@ def rank_program(g, core, T, topo):
     iota(A("ex", SP, 1024, 16), [[32, 32], [0, 2]], 0)
     iota(A("ex", 1024 + IHI, 1408, 16), [[IDS, 4], [32, 3], [0, 2]], P)
     iota(A("vai"), [[32, 11], [1, 16]], -MID)
-    for h in range(N):
-        act(A("ex", P * h + IHI, P * h + P, 16), A("ex", P * h + SP, P * h + P, 16), 1.0, float(V * h))
+    iota(A("ex", IHI, 1024, 16), [[IDS, 4], [32, 8], [0, 2]], 0)
     tr(A("zc"), A("z"))
     cp(A("gl"), A("zc", 0, 64, 32))
     i32 = A("zc", 64, 65)
@@ -249,32 +259,26 @@ def rank_program(g, core, T, topo):
     for k, (sh, m) in enumerate([(0, 15), (0, 16), (1, 7), (0, 1), (0, 7)]):
         ts(A("pci", k + 1, k + 2), A("pci", 0, 1), sh, Op.arith_shift_right, m, Op.bitwise_and)
     cp(A("pcf", 0, 5), A("pci", 1, 6))
-    i16, o16, half, odd, i8, free, xor0, xor16, lanes, sel0, ll0, less, none, half12, stay, cs, vs = [A("pcf", k, k + 1) for k in range(17)]
+    i16, o16, half, odd, i8, free, xor0, xor16, lanes, ll0, spare, none, stay, cs, vs, less = [A("pcf", k, k + 1) for k in range(16)]
     act(xor0, i32, 1.0, 16.0)
     act(xor16, o16, -2.0, xor0)
     ts(lanes, i32, float(FLAG + 12), Op.is_lt)
-    ts(sel0, i16, 10.0, Op.min, 8.0, Op.mult)
-    act(sel0, sel0, 1.0, 4.0)
     ts(stay, i32, float(FLAG + 12), Op.is_equal)
     act(cs, stay, 1.0 - 2 * BASE, -1.0)
     act(vs, stay, -1.0 - 2 * BASE, 1.0)
-    act(ll0, odd, 32.0, half)
-    act(less, i32, -1.0)
+    act(A("lt", 0, 1), odd, -23.0 / 16, 11.0 / 16)
+    act(A("lt", 1, 2), odd, 12.0, half)
+    act(ll0, A("lt", 0, 1), o16, A("lt", 1, 2))
     ts(free, i8, float(IHI), Op.not_equal)
     ts(none, i16, float(SHI), Op.is_equal, NONE, Op.mult)
-    act(half12, half, 1.0, 12.0)
-    const(A("elf"), 0.0)
-    act(A("elf", 0, 8, 2), A("ramp", 0, 4), float(ST), half12)
-    const(A("elf", 8, 11), sel0)
-    for k in (12, 13):
-        act(A("elf", k, 16, 2), A("ramp", 0, 2), 16.0, i16)
-    act(A("elf", 16, 18), A("ramp", 0, 2), 8.0, ll0)
-    cp(A("el", 0, 8), A("elf", 0, 8))
-    cp(A("el", 8, 18), A("elf", 8, 18))
-    act(A("dj"), A("r16"), 1.0, i16)
-    for t in range(3):
-        const(A("e%d" % t), 4 * NONE)
-        act(A("e%d" % t, 3, 96, 4), A("dj"), 1.0, 384.0 * t)
+    act(less, i32, -1.0)
+    for h in others:
+        ts(A("el", 4 + 2 * h, 5 + 2 * h), half, ST * h + 12.0, Op.add)
+    ts(A("el", 2, 4), A("ramp"), 8.0, Op.mult, ll0, Op.add)
+    act(spare, i16, 1.0, 1024.0 - 16)
+    for a in (0, 144):
+        const(A("e", a, a + 144), 4 * NONE)
+    act(A("e", 3, 288, 4), A("k0", 0, 72), 16.0, spare)
     for a in range(1024, PLACES - 384, 128):
         const(A("tab", a, a + 128), none)
     const(A("ex", ILO, 1408, 16), i32)
@@ -284,8 +288,8 @@ def rank_program(g, core, T, topo):
         const(A("d0", a, a + 128), lanes)
     act(A("val"), A("vai"), 1.0, o16)
     act(A("k1"), A("k0"), TINY)
-    for n, c in (("w0", BIG), ("wt", BIG), ("sd", 0.0), ("ma0", 0.0), ("mb", 1.0)):
-        const(A(n), c)
+    for n in ("w0", "wt"):
+        const(A(n), BIG)
     const(A("zb"), -float(MID))
     act(A("hm"), A("r32", 0, 8), 1.0, float(IDS * r - ZID))
     act(A("kb"), A("r32", 0, 14), 1.0, i32)
@@ -296,13 +300,13 @@ def rank_program(g, core, T, topo):
     for a in (0, 96):
         const(A("einv", a, a + 96), 0.0)
     fill(A("cv", 4 * IDS, 4 * OWN), 0.0)
-    for a in (BASE, BASE + MID):
-        const(A("lst", a, a + MID), -float(MID))
+    for a, b in ((BASE - 16, BASE), (BASE, BASE + MID), (BASE + MID, BASE + IDS)):
+        const(A("lst", a, b), -float(MID))
 
     ts(A("gi"), A("xl"), int(NONE) - 1, Op.bitwise_and, by=A("gl"))
     for k in range(4):
         cp(quad(A("rec"), k), quad(A("gi", 4, 4 + ST), 0))
-    post("arrl", "lsl", [A("rec")] * 3 + [left], [A("land", ST * r, ST * r + ST)] * 3, [A("land", ST * x, ST * x + ST) for x in others], HOP + 1.0)
+    post("arrl", "lsl", [A("rec")] * 3 + [left], [A("land", ST * r, ST * r + ST)] * 3, [A("land")], HOP + 1.0)
     k = load("y", "ldw0", [(T.wb[:, 0:2048], T.w[:, 0:2048])], [], [A("wb", 0, 2048), left], 3.5)
     load("y", "ldw1", [(T.wb[:, 2048:4096], T.w[:, 2048:4096])], [], [A("wb", 2048, 4096)], 5.0, [k])
     for a in range(0, OWN, 128):
@@ -315,7 +319,8 @@ def rank_program(g, core, T, topo):
         return A("msk", 8 * a + j, 8 * b, 8) if j < 3 else A("any", a, b)
     cp(A("rci"), A("rec"))
     ts(A("rk", 0, 8), A("rci", 12, 20), 8, Op.arith_shift_right)
-    ts(A("rk", 8, 14), A("rci", 0, 12, 2), 8, Op.arith_shift_right)
+    for k in range(2):
+        ts(A("rk", 8 + 3 * k, 11 + 3 * k), A("rci", k, 12, 4), 8, Op.arith_shift_right)
     ts(A("lf", ST * r, ST * r + ST), A("rec"), i32, Op.add)
     ts(A("rkf"), A("rk"), float(r), Op.subtract)
     ts(A("occ", 0, 8), A("rk", 0, 8), float(N), Op.is_lt)
@@ -360,24 +365,24 @@ def rank_program(g, core, T, topo):
         act(A("pr", 11 * j, 11 * j + 11), A("dm"), -1.0, -BASE - (3 - j) * BIG)
         tt(A("pq", 11 * j, 11 * j + 11), A("pr", 11 * j, 11 * j + 11), mk(j, 0, 11), Op.mult)
         act(A("wt", j, 88, 8), A("pq", 11 * j, 11 * j + 11), 1.0, BIG)
-        act(A("ma0", 8 + j, 48, 16), A("msk", 88 + 8 * j, 91 + 8 * j), A("sm", 92 + 8 * j, 93 + 8 * j))
-        act(A("mb", 16 * j + 8, 16 * j + 11), mk(j, 11, 14), -1.0, 1.0)
-    act(A("mc"), A("mb"), -float(BASE), -float(MID))
-    tt(A("ma"), A("mc"), A("ma0"), Op.subtract)
+        act(A("mb", 3 * j, 3 * j + 3), mk(j, 11, 14), -1.0, 1.0)
+    act(A("ma", 0, 3), A("sm", 92, 112, 8), 1.0, -float(BASE))
+    act(A("ma", 3, 6), A("sm", 92, 112, 8), -1.0, -float(MID))
     sca(A("lst"), A("fo", 0, 3), A("val", 128, 176))
 
-    for a, b in afar:
-        ts(A("lf", ST * a, ST * b), A("land", ST * a, ST * b), i32, Op.add)
+    for a, b in ((0, r), (r + 1, N)):
+        if a < b:
+            ts(A("lf", ST * a, ST * b), A("land", ST * a, ST * b), i32, Op.add)
     for h in others:
-        cp(A("ex", P * h + SHI, P * h + P, 16), A("lf"), "v", A("el", 2 * h, 2 * h + 1))
-        tt(A("ex", P * h + SLO, P * h + P, 16), A("lf"), A("ex", P * h + SHI, P * h + P, 16), Op.subtract, A("el", 2 * h, 2 * h + 1))
+        by = A("el", 4 + 2 * h, 5 + 2 * h)
+        cp(A("ex", P * h + SHI, P * h + P, 16), A("lf"), "v", by)
+        tt(A("ex", P * h + SLO, P * h + P, 16), A("lf"), A("ex", P * h + SHI, P * h + P, 16), Op.subtract, by)
         tr(A("tab", P * h, P * h + P), A("ex", P * h, P * h + P))
-    for n, a in (("f1f", 6), ("f2f", 0)):
-        for h in range(N):
-            act(A(n, 6 * h, 6 * h + 6), A("lf", ST * h + a, ST * h + a + 6), 1.0, less)
-    cp(A("to0"), A("f1f"))
-    act(A("e0", 0, 96, 4), A("f1f"), -1.0)
-    tt(A("svf"), A("f1f"), A("f2f"), Op.add)
+    for h in range(N):
+        act(A("ff", 12 * h, 12 * h + 12), A("lf", ST * h, ST * h + 12), 1.0, less)
+    cp(A("to0"), A("ff", 1, 48, 2))
+    act(A("e", 0, 96, 4), A("ff", 1, 48, 2), -1.0)
+    tt(A("svf"), A("ff", 0, 48, 2), A("ff", 1, 48, 2), Op.add)
     cp(A("ex", 1024 + SHI, 1408, 16), A("svf"), "s")
     tt(A("ex", 1024 + SLO, 1408, 16), A("svf"), A("ex", 1024 + SHI, 1408, 16), Op.subtract)
     tr(A("ev"), A("ex", 1024, 1408))
@@ -385,12 +390,12 @@ def rank_program(g, core, T, topo):
 
     def look(t, win):
         cp(A("ga%d" % t, 192, 384), win, "s", A("to%d" % t, 12, 24))
-        cp(A("ga%d" % t, 0, 192), win, "v", A("to%d" % t, 0, 12))
+        cp(A("ga%d" % t, 0, 192), win, "vvs"[t], A("to%d" % t, 0, 12))
         tr(A("gt%d" % t), A("ga%d" % t))
-        scan(A("ti%d" % t), A("e%d" % t), A("gt%d" % t, SHI, 384, 4), Op.min)
+        scan(A("ti%d" % t), A("e", 96 * t, 96 * t + 96), A("gt%d" % t, SHI, 384, 4), Op.min)
         if t < 2:
             cp(A("to%d" % (t + 1)), A("ti%d" % t, 3, 96, 4))
-            act(A("e%d" % (t + 1), 0, 96, 4), A("ti%d" % t, 3, 96, 4), -1.0)
+            act(A("e", 96 * t + 96, 96 * t + 192, 4), A("ti%d" % t, 3, 96, 4), -1.0)
         if t > 0:
             cp(high(A("to%d" % t)), low(A("ti%d" % t, 3, 96, 4)))
             cp(high(A("ga%d" % (t - 1))), low(A("ga%d" % t)), "s")
@@ -405,7 +410,7 @@ def rank_program(g, core, T, topo):
     cp(quad(A("sn"), 0), quad(A("tab", *mine), 0), "s")
     put(1, places, "ga0", 24)
 
-    tt(A("un"), first, A("k1"), Op.is_equal, A("rec", 6, 12))
+    tt(A("un"), first, A("k1"), Op.is_equal, A("to0", 6 * r, 6 * r + 6))
     act(low(A("cu", 0, P)), high(A("tab", *mine)), cs)
     act(low(A("cu", P, IDS)), high(A("un")), vs)
     tt(low(A("mx", 0, P)), low(A("tab", *mine)), low(A("cu", 0, P)), Op.mult)
@@ -416,27 +421,32 @@ def rank_program(g, core, T, topo):
     scan(low(A("sd")), low(A("osd", FLAG, IDS, 4)), low(A("wt")), Op.min, BIG)
     for half_ in (low, high):
         cp(half_(A("ofd", 0, 11)), low(A("sd", 4, 88, 8)))
-    tt(A("mp"), A("sd"), A("mb"), Op.mult, A("el", 8, 11))
-    for half_ in (low, high):
-        tt(half_(A("msg")), low(A("mp")), low(A("ma")), Op.add)
-    post("arrm", "lsm", [A("msg", 16 * j, 16 * j + MS) for j in range(3)], [A("landm", MS * r, MS * r + MS)] * 3, [A("landm", MS * x, MS * x + MS) for x in others])
+    tt(low(A("mc")), low(A("sd", 68, 88, 8)), low(A("ma", 0, 3)), Op.add)
+    for j in range(3):
+        act(low(A("msg", MS * j, MS * j + 8)), low(A("sd", 4, 64, 8)), 1.0, -float(BASE + MID))
+        act(low(A("msg", 8 + j, 3 * MS, MS)), low(A("mb", j, 9, 3)), A("mc", j, j + 1), A("ma", 3 + j, 4 + j))
+    cp(high(A("msg")), low(A("msg")), "s")
+    post("arrm", "lsm", [A("msg", MS * j, MS * j + MS) for j in range(3)], [A("landm", MS * r, MS * r + MS)] * 3, [A("landm", MS * x, MS * x + MS) for x in others], HOP + 0.2)
+    cp(quad(A("sn"), 1), quad(A("tab", *mine), 1), "s")
+    look(2, places)
+    act(high(A("tab", *mine)), high(A("d0")), 0.0, free)
     sca(A("lst"), A("ofd", 0, 11), A("val"))
-    tr(A("olt"), A("lst", BASE, BASE + IDS))
-    tt(A("zb", 0, 11), A("olt", 0, IDS, 32), A("olt", 16, IDS, 32), Op.max)
-    tr(A("zt"), A("zb"))
-    cp(A("zg"), A("zt"), "v", A("el", 12, 16))
-    tr(A("zh"), A("zg"))
-    ts(A("loff"), A("zh"), float(MID), Op.add, by=A("el", 16, 18))
+    n = len(calls)
+    for k in range(2):
+        tr(A("olt", IDS * k, IDS * k + IDS), A("lst", BASE - 16 * k, BASE - 16 * k + IDS))
+    sca(places, A("to2", 0, 4), A("ga1", 0, 64))
+    tt(A("zb", 0, 22), A("olt", 0, 2 * IDS, 32), A("olt", 16, 2 * IDS, 32), Op.max)
+    ts(A("loff"), A("zb"), float(MID), Op.add, by=A("el", 2, 4))
+    sca(places, A("to2", 4, 24), A("ga1", 64, 384))
     pick(A("sq"), A("qo"), A("loff", 0, 21))
+    for k in range(n, len(calls)):
+        calls[k]["also"] = [k - 1]
     cp(A("sqp"), A("qop"), "s", A("loff", 0, 21))
     at = [OWN + SLOTS * turn(x, r) for x in others]
-    k = post("arrp", "lsp", [A("sqp", SLOTS * j, SLOTS * j + SLOTS) for j in range(3)], [A("qp", x, x + SLOTS) for x in at], [A("qp", OWN, WIN)])
-    post("arrq", "lsq", [A("sq", SLOTS * j, SLOTS * j + SLOTS) for j in range(3)], [A("q", x, x + SLOTS) for x in at], [A("q", OWN, WIN)], HOP + 0.5, [k])
+    k = []
+    for n, late in (("qp", HOP), ("q", HOP + 0.5)):
+        k = [post("arr" + n[-1], "ls" + n[-1], [A("s" + n, SLOTS * j, SLOTS * j + SLOTS) for j in range(3)], [A(n, x, x + SLOTS) for x in at], [A(n, OWN, WIN)], late, k)]
 
-    cp(quad(A("sn"), 1), quad(A("tab", *mine), 1), "s")
-    act(high(A("tab", *mine)), high(A("d0")), 0.0, free)
-    look(2, places)
-    put(2, places, "ga1", 24)
     tr(low(A("ts")), low(A("sn")))
     tr(quad(A("ts"), 2), quad(A("tab", *mine), 0))
     cp(on(A("tab", *mine), 96, 112), on(A("tab", *mine), 0, 16), "s")
@@ -475,27 +485,32 @@ def rank_program(g, core, T, topo):
             for i in range(O * t, O * t + O):
                 bank = 512 * (i + (R * O - O) * (a > 0))
                 x = [A("ps", bank, bank + n), A("wq", 128 * i, 128 * i + 128), A("wp", 128 * i, 128 * i + 128), kq, kp]
-                last = [add("t", lambda x=x: g.tensor.matmul_mx(*[ap(y) for y in x], True, True).then_inc(T.sem.st, 1), x[1:], [A("ps", bank, bank + 512)], 1.2 * (n + 16) * CYCLE, also=last)]
+                last = [add("t", lambda _, x=x: g.tensor.matmul_mx(*[ap(y) for y in x], True, True).then_inc(T.sem.st, 1), x[1:], [A("ps", bank, bank + 512)], 1.2 * (n + 16) * CYCLE, also=last)]
                 reg = A("ys", P * i + a, P * i + a + n)
                 cp(reg, x[0], "vs"[i % 2])
                 load("y", "sty", [(T.y[:, reg[1]:reg[2]], ap(reg))], [reg], [], DMA + 0.4 * (R * O - i))
 
-    known, log, total = {k: {} for k in eng}, {}, {}
-    for c in in_order(calls):
-        q = c["q"]
+    known, log, total, waited = {k: {} for k in eng}, {}, {}, {}
+    seq = in_order(calls)
+    for n, c in enumerate(seq):
+        q, c["waits"] = c["q"], []
         need = [tok for regs, w in ((c["reads"], False), (c["writes"], True)) for x in regs for y, w2, tok in log.get(x[0], []) if (w or w2) and clash(x, y)]
-        for s, v, clock in sorted(need, key=lambda t: -t[1]):
+        for s, v, clock, by in sorted(need, key=lambda t: -t[3]):
             if c["go"] and known[q].get(s, 0) < v:
-                eng[q].wait_ge(T.sem[s], v)
+                c["waits"].append((s, v, by))
                 for k, x in list(clock.items()) + [(s, v)]:
                     known[q][k] = max(known[q].get(k, 0), x)
-        if c["go"]:
-            c["go"]()
         s = c["sem"] or sem_of[q]
-        total[s] = total.get(s, 0) + (c["n"] or 1)
+        total[s] = total.pop(s, 0) + (c["n"] or 1)
         for regs, w in ((c["reads"], False), (c["writes"], True)):
             for x in regs:
-                log.setdefault(x[0], []).append((x, w, (s, total[s], dict(known[q]) if c["go"] else {})))
-    for s in SEMAPHORES:
-        if s in total:
+                log.setdefault(x[0], []).append((x, w, (s, total[s], dict(known[q]) if c["go"] else {}, n)))
+    for c in seq:
+        for s, v, by in sorted(c["waits"], key=lambda t: seq[t[2]]["done"]):
+            eng[c["q"]].wait_ge(T.sem[s], v)
+            waited[s] = max(waited.get(s, 0), v)
+        if c["go"]:
+            c["go"](c["q"])
+    for s in total:
+        if waited.get(s, 0) < total[s]:
             g.wait_ge(T.sem[s], total[s])

from concourse.bass import DstId, RemoteDMATransfer
from concourse.mybir import dt, AluOpType as Op, ActivationFunctionType as Act

N, P, V, R, O = 4, 256, 96, 4, 2
SLOTS = 112
IDS = P + V
OWN = IDS + 32
WIN = OWN + 3 * SLOTS
ST, MS = 20, 11
SHI, SP, SLO, IHI, ILO = 0, 4, 8, 1, 9
KEEP = 3
FLAG = 2
BIG, BASE = 16384.0, 2048
PLACES = 1024 + 3 * 384
NONE = 8192.0
MID = 176
ZID = N * IDS
TINY = 2.0 ** -24
F32, I32, U16, BF, CODE, PL = "float32", "int32", "uint16", "bfloat16", "float8_e4m3fn_x4", "uint8"
CYCLE, FLOOR, WAKE, PICK, PUT, DMA, HOP, NEAR = 0.001, {"v": 64, "s": 90}, 0.16, 1.5, 3.8, 2.0, 1.8, 0.01


def _s(n, t):
    return ("sbuf", [128, n], t)


SCRATCH = {
    "xl": _s(32, I32), "gi": _s(32, I32), "rci": _s(ST, I32), "z": _s(96, F32), "zc": _s(96, F32), "gl": _s(2, U16), "r32": _s(16, F32),
    "pci": _s(8, I32), "pcf": _s(17, F32), "e": _s(288, F32), "ff": _s(48, F32), "rec": _s(ST, U16),
    "land": _s(N * ST, U16), "lf": _s(N * ST, F32), "ramp": _s(2, F32), "el": _s(12, U16), "kb": _s(14, F32),
    "ex": _s(1440, BF), "tab": _s(PLACES, BF), "svf": _s(24, F32), "ev": _s(384, BF),
    "rk": _s(14, I32), "rkf": _s(14, F32), "msk": _s(112, F32), "wt": _s(88, F32),
    "a1": _s(11, F32), "any": _s(14, F32), "occ": _s(11, F32), "hm": _s(8, F32), "hz": _s(8, F32),
    "kp": _s(3, F32), "kn": _s(3, F32), "einv": _s(192, BF), "dv": _s(192, BF), "d0": _s(P, BF), "w0": _s(112, F32),
    "scs": _s(448, BF), "oss": _s(448, BF), "pr": _s(33, F32), "pq": _s(33, F32), "sm": _s(112, F32), "kk": _s(14, F32), "b1": _s(14, F32), "b2": _s(14, F32),
    "dm": _s(11, F32), "fo": _s(4, U16),
    "vai": _s(176, F32), "val": _s(176, BF), "k0": _s(V, F32), "one": _s(V, F32), "k1": _s(V, BF), "lst": _s(BASE + IDS, BF),
    "ma": _s(6, F32), "mb": _s(9, F32), "mc": _s(3, F32), "msg": _s(3 * MS, BF), "landm": _s(N * MS, BF),
    "un": _s(V, BF), "cu": _s(IDS, BF), "mx": _s(IDS, BF), "sc": _s(IDS, BF), "osd": _s(IDS, BF), "sd": _s(88, F32), "ofd": _s(12, U16),
    "olt": _s(2 * IDS, BF), "zb": _s(32, BF), "loff": _s(32, U16), "lt": _s(4, F32),
    "m": _s(1440, BF), "sn": _s(P, BF), "ts": _s(P, BF), "idf": _s(32, F32),
    "ido": _s(16, U16), "mg": _s(P, BF), "om": _s(P, BF), "sl": _s(64, F32), "off": _s(64, U16),
    "cv": _s(4 * OWN, BF), "qo": _s(OWN, CODE), "qop": _s(OWN, PL), "q": _s(WIN, CODE), "qp": _s(WIN, PL),
    "sq": _s(3 * SLOTS, CODE), "sqp": _s(3 * SLOTS, PL),
    "wb": _s(4096, BF), "wq": _s(1024, CODE), "wp": _s(1024, PL), "ys": _s(2048, F32),
    "ps": ("psum", [128, 4096], F32),
}
for _t in range(3):
    SCRATCH["ga%d" % _t] = _s(384, BF)
    SCRATCH["gt%d" % _t] = _s(384, BF)
    SCRATCH["ti%d" % _t] = _s(96, F32)
    SCRATCH["to%d" % _t] = _s(24, U16)
for _t in range(4):
    SCRATCH["k%dq" % _t] = _s(P, CODE)
    SCRATCH["k%dp" % _t] = _s(P, PL)

SEMAPHORES = ["sv", "ss", "st", "sg", "ldx", "ldc", "ldw0", "ldw1", "lsl", "lsm", "lsq", "lsp", "own", "arrl", "arrp", "arrq", "sty"] + ["arrm%d" % x for x in range(N)]


def clash(a, b):
    if a[0] != b[0] or a[1] >= b[2] or b[1] >= a[2] or a[4] >= b[5] or b[4] >= a[5]:
        return False
    a, b = sorted((range(*a[1:4]), range(*b[1:4])), key=len)
    return any(x in b for x in a)


def in_order(calls):
    seen = {}
    for k, c in enumerate(calls):
        c["after"] = set()
        for regs, w in ((c["reads"], False), (c["writes"], True)):
            for x in regs:
                c["after"] |= {j for y, w2, j in seen.get(x[0], []) if (w or w2) and clash(x, y)}
        for regs, w in ((c["reads"], False), (c["writes"], True)):
            for x in regs:
                seen.setdefault(x[0], []).append((x, w, k))
    chain = [c["hold"] + c["late"] for c in calls]
    for k in reversed(range(len(calls))):
        for j in calls[k]["after"]:
            chain[j] = max(chain[j], calls[j]["hold"] + calls[j]["late"] + WAKE + chain[k])
        for j in calls[k]["also"]:
            chain[j] = max(chain[j], calls[j]["hold"] + chain[k])
    done, free, left, out = {}, {}, set(range(len(calls))), []
    while left:
        ready = {k: max([0.0] + [done[j] + WAKE for j in calls[k]["after"]] + [done[j] - calls[j]["late"] for j in calls[k]["also"]])
                 for k in left if calls[k]["after"] | set(calls[k]["also"]) <= set(done)}
        best = []
        for q in {x for k in ready for x in calls[k]["q"]}:
            start = {k: max(free.get(q, 0.0), t) for k, t in ready.items() if q in calls[k]["q"]}
            fits = sorted(start, key=lambda k: (calls[k]["q"][0] != q, -chain[k], k))
            while fits:
                top = fits[0]
                fits = [k for k in fits[1:] if start[k] + calls[k]["hold"] <= start[top] + WAKE / 4]
            best.append((start[top], calls[top]["q"][0] != q, top, q))
        t, _, k, q = min(best)
        free[q] = t + calls[k]["hold"]
        done[k] = t + calls[k]["hold"] + calls[k]["late"]
        calls[k].update(q=q, done=done[k])
        left.remove(k)
        out.append(calls[k])
    return out


def rank_program(g, core, T, topo):
    r = T.rank_of(core)
    if r is None:
        return
    others = [x for x in range(N) if x != r]
    eng = {"v": g.vector, "s": g.scalar, "t": g.tensor, "g": g, "y": g.sync}
    sem_of = {"v": "sv", "s": "ss", "t": "st", "g": "sg"}
    calls = []

    def add(q, go, reads, writes, hold, late=0.0, sem=None, n=0, also=()):
        calls.append(dict(q=q, go=go, reads=list(reads), writes=list(writes), hold=hold, late=late, sem=sem, n=n, also=also))
        return len(calls) - 1

    def ap(x):
        n, lo, hi, st, p0, p1 = x
        return T[n][p0:p1, lo:hi] if st == 1 else T[n][p0:p1, lo:hi:st]

    def raw(x):
        return ap(x).bitcast(dt.uint8) if SCRATCH[x[0]][2] == CODE else ap(x)

    def A(n, lo=0, hi=None, st=1):
        return (n, lo, SCRATCH[n][1][1] if hi is None else hi, st, 0, 128)

    def on(x, p0, p1):
        return x[:4] + (p0, p1)

    def quad(x, k):
        return on(x, 32 * k, 32 * k + 32)

    def low(x):
        return on(x, 0, 64)

    def high(x):
        return on(x, 64, 128)

    def wide(x):
        return len(range(x[1], x[2], x[3]))

    def run(q, call, reads, out, per=1.0, by=None):
        if by is not None:
            hold = 0.06 + 16 * wide(by) * per * CYCLE
        else:
            short = per < 2 and q == "v" and all(SCRATCH[x[0]][2] in (BF, U16) for x in reads[:1] + [out])
            hold = max(FLOOR[q[0]], wide(out) * (0.5 if short else per)) * CYCLE
        add(q, lambda q: call(eng[q]).then_inc(T.sem[sem_of[q]], 1), reads + aps(by), [out], hold)

    def load(q, sem, pairs, reads=(), writes=None, late=DMA, also=()):
        def go(_):
            for k, (o, i) in enumerate(pairs):
                eng[q[k % len(q)]].dma_start(o, i).then_inc(T.sem[sem], 16)
        return add(q[0], go, reads, writes, 0.06 * len(pairs), late, sem, 16 * len(pairs), also)

    def sc_(x, like):
        return ap(on(x, like[4], like[5])) if isinstance(x, tuple) else x

    def aps(*xs):
        return [x for x in xs if isinstance(x, tuple)]

    def via(a, by):
        return ap(a) if by is None else ap(a).indirect(ap(by))

    def tt(out, a, b, op, by=None):
        run("v", lambda e: e.tensor_tensor(ap(out), via(a, by), ap(b), op), [a, b], out, 2.0 if by is None else PICK, by)

    def ts(out, a, s1, op, s2=None, op1=None, by=None):
        more = () if op1 is None else (op1,)
        run("v", lambda e: e.tensor_scalar(ap(out), via(a, by), sc_(s1, a), sc_(s2, a), op, *more), [a] + aps(s1, s2), out, 1.0 if by is None else PICK, by)

    def cp(out, a, q="v", by=None):
        if q == "v":
            run("v", lambda e: e.tensor_copy(ap(out), via(a, by)), [a], out, 1.0 if by is None else PICK, by)
        elif by is None and wide(out) <= FLOOR["v"]:
            act(out, a, 1.0)
        else:
            run("s", lambda e: e.activation(ap(out), via(a, by), Act.Copy), [a], out, 1.0 if by is None else PICK, by)

    def act(out, a, scale, bias=0.0):
        def call(e):
            if e is eng["v"]:
                return e.tensor_scalar(ap(out), ap(a), sc_(scale, a), sc_(bias, a), Op.mult, Op.add)
            return e.activation(ap(out), ap(a), Act.Identity, bias=sc_(bias, a), scale=sc_(scale, a))
        run("sv" if wide(out) <= FLOOR["v"] else "s", call, [a] + aps(scale, bias), out)

    def const(out, c):
        act(out, on(A("vai", 0, wide(out)), out[4], out[5]), 0.0, c)

    def tr(out, a):
        run("v", lambda e: e.transpose(ap(out), ap(a)), [a], out)

    def scan(out, a, b, op=Op.mult, start=0.0):
        run("v", lambda e: e.tensor_tensor_scan(ap(out), ap(a), ap(b), start, op, Op.add), [a, b], out)

    def fill(out, c):
        run("v", lambda e: e.memset(ap(out), c), [], out)

    def sca(win, off, a):
        run("v", lambda e: e.tensor_copy(via(win, off), ap(a)), [a], win, PUT, off)

    def pick(out, win, off):
        run("v", lambda e: e.tensor_copy(ap(out).bitcast(dt.uint32), ap(win).bitcast(dt.uint32).indirect(ap(off))), [win], out, PICK, off)

    def quant(c, p, a):
        add("v", lambda _: g.vector.quantize_mx(ap(c), ap(p), ap(a)).then_inc(T.sem.sv, 1), [a], [c, p], 0.27 * wide(a) * CYCLE)

    def iota(out, pattern, base):
        add("g", lambda _: g.iota(ap(out), pattern, base, 0, allow_small_or_imprecise_dtypes=True).then_inc(T.sem.sg, 1), [], [out], 0.13 + 2 * wide(out) * CYCLE)

    picked, engs = [], {}
    for x in sorted(others, key=lambda x: len(topo.engines(core, T.cores[x]))):
        e = [k for k in topo.engines(core, T.cores[x]) if k not in picked][:4]
        picked += e
        engs[x] = e

    def post(sem, lsem, srcs, dsts, lands, late=HOP, also=(), use=slice(4)):
        def go(_):
            trs = []
            for j, x in enumerate(others):
                rid, pid, _ = topo.addr(T.cores[x])
                trs.append(RemoteDMATransfer(dst_ids=[DstId(rid=rid, pnc=pid)], dma_engine_mask=sum(1 << k for k in engs[x][use]), remote_sem=T.sem[sem + str(r) * apart], src=raw(srcs[j]), dst=raw(dsts[j])))
            g.remote_dma_fused(trs, local_sem=T.sem[lsem])
        apart = len(lands) > 1
        n = len(range(4)[use])
        k = add("g", go, srcs, [], 0.4, 0.0, lsem, 3 * n, also)
        for x, land in zip(others, lands):
            add("f", None, [], [land], 0.0, late - NEAR * (topo.chip(T.cores[x]) == topo.chip(core)), sem + str(x) * apart, n if apart else 3 * n, [k])
        return k

    def turn(x, y):
        return [h for h in range(N) if h != x].index(y)
    mine, myv = (P * r, P * r + P), (1024 + V * r, 1024 + V * r + V)
    left = ("left", 0, 1, 1, 0, 128)

    load("ys", "ldx", [(T.xl[16 * o:16 * o + 16, a:b], n[:, :]) for n, a, b in ((T.alt, 0, 16), (T.f2, 16, 22), (T.f1, 22, 28)) for o in range(2)], [], [quad(A("xl", 0, 28), 0)], 1.3)
    load("y", "ldc", [(T.cv[:, 4 * P:4 * IDS], T.v[:, :]), (T.cv[:, 0:4 * P], T.c[:, :])], [], [A("cv", 0, 4 * IDS)], 4.0, [0])

    iota(A("z", 0, 16), [[1, 8], [6, 2]], 14)
    iota(A("z", 16, 32), [[2, 4], [-1, 2], [6, 2]], 15)
    iota(A("z", 32, 64), [[1, 2], [2, 16]], 0)
    iota(A("z", 64, 96), [[1, 32]], 0)
    fill(A("one"), 1.0)
    scan(A("k0"), A("one"), A("one"))
    act(A("ramp"), A("k0", 0, 2), 1.0, -1.0)
    act(A("r32"), A("k0", 0, 16), 32.0, -32.0)
    for a in range(0, 1440, 288):
        fill(A("ex", a, a + 288), 0.0)
    for x in (quad(A("xl", 28, 32), 0), quad(A("xl"), 1), high(A("xl"))):
        fill(x, 0)
    iota(A("ex", SP, 1024, 16), [[32, 32], [0, 2]], 0)
    iota(A("ex", 1024 + IHI, 1408, 16), [[IDS, 4], [32, 3], [0, 2]], P)
    iota(A("vai"), [[32, 11], [1, 16]], -MID)
    iota(A("ex", IHI, 1024, 16), [[IDS, 4], [32, 8], [0, 2]], 0)
    tr(A("zc"), A("z"))
    cp(A("gl"), A("zc", 0, 64, 32))
    i32 = A("zc", 64, 65)
    cp(A("pci", 0, 1), i32)
    for k, (sh, m) in enumerate([(0, 15), (0, 16), (1, 7), (0, 1), (0, 7)]):
        ts(A("pci", k + 1, k + 2), A("pci", 0, 1), sh, Op.arith_shift_right, m, Op.bitwise_and)
    cp(A("pcf", 0, 5), A("pci", 1, 6))
    i16, o16, half, odd, i8, free, xor0, xor16, lanes, ll0, spare, none, stay, cs, vs, less = [A("pcf", k, k + 1) for k in range(16)]
    act(xor0, i32, 1.0, 16.0)
    act(xor16, o16, -2.0, xor0)
    ts(lanes, i32, float(FLAG + 12), Op.is_lt)
    ts(stay, i32, float(FLAG + 12), Op.is_equal)
    act(cs, stay, 1.0 - 2 * BASE, -1.0)
    act(vs, stay, -1.0 - 2 * BASE, 1.0)
    act(A("lt", 0, 1), odd, -23.0 / 16, 11.0 / 16)
    act(A("lt", 1, 2), odd, 12.0, half)
    act(ll0, A("lt", 0, 1), o16, A("lt", 1, 2))
    ts(free, i8, float(IHI), Op.not_equal)
    ts(none, i16, float(SHI), Op.is_equal, NONE, Op.mult)
    act(less, i32, -1.0)
    for h in others:
        ts(A("el", 4 + 2 * h, 5 + 2 * h), half, ST * h + 12.0, Op.add)
    ts(A("el", 2, 4), A("ramp"), 8.0, Op.mult, ll0, Op.add)
    act(spare, i16, 1.0, 1024.0 - 16)
    for a in (0, 144):
        const(A("e", a, a + 144), 4 * NONE)
    act(A("e", 3, 288, 4), A("k0", 0, 72), 16.0, spare)
    for a in range(1024, PLACES - 384, 128):
        const(A("tab", a, a + 128), none)
    const(A("ex", ILO, 1408, 16), i32)
    const(A("ex", 1024 + 16 + ILO, 1408, 32), xor16)
    const(A("ex", KEEP + 8, 1408, 16), 1.0)
    for a in (0, 128):
        const(A("d0", a, a + 128), lanes)
    act(A("val"), A("vai"), 1.0, o16)
    act(A("k1"), A("k0"), TINY)
    for n in ("w0", "wt"):
        const(A(n), BIG)
    const(A("zb"), -float(MID))
    act(A("hm"), A("r32", 0, 8), 1.0, float(IDS * r - ZID))
    act(A("kb"), A("r32", 0, 14), 1.0, i32)
    act(A("kn"), A("kb", 0, 3), 1.0, 1.0)
    act(A("kp"), A("kn"), TINY)
    act(A("kk"), A("kb"), -1.0, float(BASE))
    act(A("b1"), A("kb"), 1.0, BIG - BASE)
    for a in (0, 96):
        const(A("einv", a, a + 96), 0.0)
    fill(A("cv", 4 * IDS, 4 * OWN), 0.0)
    for a, b in ((BASE - 16, BASE), (BASE, BASE + MID), (BASE + MID, BASE + IDS)):
        const(A("lst", a, b), -float(MID))

    ts(A("gi"), A("xl"), int(NONE) - 1, Op.bitwise_and, by=A("gl"))
    for k in range(4):
        cp(quad(A("rec"), k), quad(A("gi", 4, 4 + ST), 0))
    post("arrl", "lsl", [A("rec")] * 3 + [left], [A("land", ST * r, ST * r + ST)] * 3, [A("land")], HOP + 1.0)
    k = load("y", "ldw0", [(T.wb[:, 0:2048], T.w[:, 0:2048])], [], [A("wb", 0, 2048), left], 3.5)
    load("y", "ldw1", [(T.wb[:, 2048:4096], T.w[:, 2048:4096])], [], [A("wb", 2048, 4096)], 5.0, [k])
    for a in range(0, OWN, 128):
        quant(A("qo", a, a + 128), A("qop", a, a + 128), A("cv", 4 * a, 4 * a + 512))
    load("y", "own", [(raw(A("q", 0, OWN)), raw(A("qo"))), (raw(A("qp", 0, OWN)), raw(A("qop")))], [A("qo"), A("qop")], [A("q", 0, OWN), A("qp", 0, OWN)], 12.0)
    for a in range(0, 1024, 128):
        quant(A("wq", a, a + 128), A("wp", a, a + 128), A("wb", 4 * a, 4 * a + 512))

    def mk(j, a=0, b=14):
        return A("msk", 8 * a + j, 8 * b, 8) if j < 3 else A("any", a, b)
    cp(A("rci"), A("rec"))
    ts(A("rk", 0, 8), A("rci", 12, 20), 8, Op.arith_shift_right)
    for k in range(2):
        ts(A("rk", 8 + 3 * k, 11 + 3 * k), A("rci", k, 12, 4), 8, Op.arith_shift_right)
    ts(A("lf", ST * r, ST * r + ST), A("rec"), i32, Op.add)
    ts(A("rkf"), A("rk"), float(r), Op.subtract)
    ts(A("occ", 0, 8), A("rk", 0, 8), float(N), Op.is_lt)
    tt(A("occ", 8, 11), A("rk", 8, 11), A("rk", 11, 14), Op.not_equal)
    tt(A("rkf", 0, 11), A("rkf", 0, 11), A("occ"), Op.mult)
    for j, x in enumerate(others):
        ts(mk(j), A("rkf"), float(x - r), Op.is_equal)
    ts(A("any"), A("rkf"), 0.0, Op.not_equal)
    tt(A("hz"), A("hm"), A("occ", 0, 8), Op.mult)
    for o in (0, 16):
        cp(A("ex", mine[0] + o + SHI, mine[1], 32), A("lf", ST * r + 12, ST * r + ST), "s")
        tt(A("ex", mine[0] + o + SLO, mine[1], 32), A("lf", ST * r + 12, ST * r + ST), A("ex", mine[0] + o + SHI, mine[1], 32), Op.subtract)
        act(A("ex", mine[0] + o + IHI, mine[1], 32), A("hz"), 1.0, float(ZID))
        act(A("ex", mine[0] + o + ILO, mine[1], 32), A("occ", 0, 8), i32)
    for j in range(4):
        act(A("ex", mine[0] + FLAG + 4 * j, mine[1], 32), mk(j, 0, 8), -1.0)
    for b in range(3):
        act(A("ex", myv[0] + 32 * b + FLAG, myv[0] + 32 * b + FLAG + 12, 4), A("msk", 64 + 8 * b, 67 + 8 * b), A("kp", b, b + 1))
    tt(A("ex", myv[0] + FLAG + 12, myv[1], 32), mk(3, 8, 11), A("kp"), Op.mult)
    tr(A("tab", *mine), A("ex", *mine))
    for j in range(3):
        cp(A("einv", FLAG + 4 * j, 96, 32), mk(j, 11, 14), "s")
        cp(A("einv", 96 + FLAG + 4 * j, 192, 32), mk(j, 8, 11), "s")
        act(A("w0", j, 64, 8), mk(j, 0, 8), 1.0 - SLOTS * j - (4 - j) * BIG, BIG)
        act(A("w0", 64 + j, 112, 8), mk(j, 8, 14), -SLOTS * (j + 1.0) - (4 - j) * BIG, BIG)
    act(A("w0", 3, 112, 8), A("any"), -BIG, BIG)
    act(A("wt", 3, 88, 8), A("any", 0, 11), -BIG, BIG)
    tt(A("b2"), A("b1"), A("any"), Op.mult)
    tt(A("w0", 4, 112, 8), A("b2"), A("kk"), Op.add)
    act(A("a1"), A("any", 0, 11), 2.0 * BASE)
    tt(A("wt", 4, 88, 8), A("a1"), A("kb", 0, 11), Op.add)
    tr(A("dv"), A("einv"))
    scan(A("scs", 0, P), A("d0"), A("tab", *mine))
    scan(A("scs", P, 448), A("d0", 0, 192), A("dv"))
    tr(A("oss", 0, P), A("scs", 0, P))
    tr(A("oss", IDS, 448), A("scs", P, IDS))
    tr(A("oss", P, IDS), A("scs", IDS, 448))
    scan(A("sm"), A("oss", FLAG, 448, 4), A("w0"), Op.min, BIG)
    ts(A("fo", 0, 3), A("sm", 92, 112, 8), -1.0, Op.mult, float(BASE), Op.add)
    tt(A("dm"), A("sm", 4, 88, 8), A("kb", 0, 11), Op.add)
    for j in range(3):
        act(A("pr", 11 * j, 11 * j + 11), A("dm"), -1.0, -BASE - (3 - j) * BIG)
        tt(A("pq", 11 * j, 11 * j + 11), A("pr", 11 * j, 11 * j + 11), mk(j, 0, 11), Op.mult)
        act(A("wt", j, 88, 8), A("pq", 11 * j, 11 * j + 11), 1.0, BIG)
        act(A("mb", 3 * j, 3 * j + 3), mk(j, 11, 14), -1.0, 1.0)
    act(A("ma", 0, 3), A("sm", 92, 112, 8), 1.0, -float(BASE))
    act(A("ma", 3, 6), A("sm", 92, 112, 8), -1.0, -float(MID))
    sca(A("lst"), A("fo", 0, 3), A("val", 128, 176))

    for a, b in ((0, r), (r + 1, N)):
        if a < b:
            ts(A("lf", ST * a, ST * b), A("land", ST * a, ST * b), i32, Op.add)
    for h in others:
        by = A("el", 4 + 2 * h, 5 + 2 * h)
        cp(A("ex", P * h + SHI, P * h + P, 16), A("lf"), "v", by)
        tt(A("ex", P * h + SLO, P * h + P, 16), A("lf"), A("ex", P * h + SHI, P * h + P, 16), Op.subtract, by)
        tr(A("tab", P * h, P * h + P), A("ex", P * h, P * h + P))
    for h in range(N):
        act(A("ff", 12 * h, 12 * h + 12), A("lf", ST * h, ST * h + 12), 1.0, less)
    cp(A("to0"), A("ff", 1, 48, 2))
    act(A("e", 0, 96, 4), A("ff", 1, 48, 2), -1.0)
    tt(A("svf"), A("ff", 0, 48, 2), A("ff", 1, 48, 2), Op.add)
    cp(A("ex", 1024 + SHI, 1408, 16), A("svf"), "s")
    tt(A("ex", 1024 + SLO, 1408, 16), A("svf"), A("ex", 1024 + SHI, 1408, 16), Op.subtract)
    tr(A("ev"), A("ex", 1024, 1408))
    first, places = A("tab", 0, 1024), A("tab")

    def look(t, win):
        cp(A("ga%d" % t, 192, 384), win, "s", A("to%d" % t, 12, 24))
        cp(A("ga%d" % t, 0, 192), win, "vvs"[t], A("to%d" % t, 0, 12))
        tr(A("gt%d" % t), A("ga%d" % t))
        scan(A("ti%d" % t), A("e", 96 * t, 96 * t + 96), A("gt%d" % t, SHI, 384, 4), Op.min)
        if t < 2:
            cp(A("to%d" % (t + 1)), A("ti%d" % t, 3, 96, 4))
            act(A("e", 96 * t + 96, 96 * t + 192, 4), A("ti%d" % t, 3, 96, 4), -1.0)
        if t > 0:
            cp(high(A("to%d" % t)), low(A("ti%d" % t, 3, 96, 4)))
            cp(high(A("ga%d" % (t - 1))), low(A("ga%d" % t)), "s")

    def put(t, win, a, n):
        for k in range(0, 24, n):
            sca(win, A("to%d" % t, k, k + n), A(a, 16 * k, 16 * (k + n)))

    look(0, first)
    put(0, first, "ev", 12)
    look(1, places)
    cp(quad(A("sn"), 0), quad(A("tab", *mine), 0), "s")
    put(1, places, "ga0", 24)

    tt(A("un"), first, A("k1"), Op.is_equal, A("to0", 6 * r, 6 * r + 6))
    act(low(A("cu", 0, P)), high(A("tab", *mine)), cs)
    act(low(A("cu", P, IDS)), high(A("un")), vs)
    tt(low(A("mx", 0, P)), low(A("tab", *mine)), low(A("cu", 0, P)), Op.mult)
    tt(low(A("mx", P, IDS)), low(A("un")), low(A("cu", P, IDS)), Op.mult)
    for a, b in ((0, P), (P, IDS)):
        scan(low(A("sc", a, b)), low(A("d0", 0, b - a)), low(A("mx", a, b)))
        tr(low(A("osd", a, b)), low(A("sc", a, b)))
    scan(low(A("sd")), low(A("osd", FLAG, IDS, 4)), low(A("wt")), Op.min, BIG)
    for half_ in (low, high):
        cp(half_(A("ofd", 0, 11)), low(A("sd", 4, 88, 8)))
    tt(low(A("mc")), low(A("sd", 68, 88, 8)), low(A("ma", 0, 3)), Op.add)
    for j in range(3):
        act(low(A("msg", MS * j, MS * j + 8)), low(A("sd", 4, 64, 8)), 1.0, -float(BASE + MID))
        act(low(A("msg", 8 + j, 3 * MS, MS)), low(A("mb", j, 9, 3)), A("mc", j, j + 1), A("ma", 3 + j, 4 + j))
    cp(high(A("msg")), low(A("msg")), "s")
    post("arrm", "lsm", [A("msg", MS * j, MS * j + MS) for j in range(3)], [A("landm", MS * r, MS * r + MS)] * 3, [A("landm", MS * x, MS * x + MS) for x in others], HOP + 0.2)
    cp(quad(A("sn"), 1), quad(A("tab", *mine), 1), "s")
    look(2, places)
    act(high(A("tab", *mine)), high(A("d0")), 0.0, free)
    sca(A("lst"), A("ofd", 0, 11), A("val"))
    n = len(calls)
    for k in range(2):
        tr(A("olt", IDS * k, IDS * k + IDS), A("lst", BASE - 16 * k, BASE - 16 * k + IDS))
    sca(places, A("to2", 0, 4), A("ga1", 0, 64))
    tt(A("zb", 0, 22), A("olt", 0, 2 * IDS, 32), A("olt", 16, 2 * IDS, 32), Op.max)
    ts(A("loff"), A("zb"), float(MID), Op.add, by=A("el", 2, 4))
    sca(places, A("to2", 4, 24), A("ga1", 64, 384))
    pick(A("sq"), A("qo"), A("loff", 0, 21))
    for k in range(n, len(calls)):
        calls[k]["also"] = [k - 1]
    cp(A("sqp"), A("qop"), "s", A("loff", 0, 21))
    at = [OWN + SLOTS * turn(x, r) for x in others]
    k = []
    for n, late in (("qp", HOP), ("q", HOP + 0.5)):
        k = [post("arr" + n[-1], "ls" + n[-1], [A("s" + n, SLOTS * j, SLOTS * j + SLOTS) for j in range(3)], [A(n, x, x + SLOTS) for x in at], [A(n, OWN, WIN)], late, k)]

    tr(low(A("ts")), low(A("sn")))
    tr(quad(A("ts"), 2), quad(A("tab", *mine), 0))
    cp(on(A("tab", *mine), 96, 112), on(A("tab", *mine), 0, 16), "s")
    tr(quad(A("ts"), 3), quad(A("tab", *mine), 3))
    scan(A("idf"), A("ts", KEEP, P, 8), A("ts", IHI, P, 8))
    for k in range(2):
        cp(A("ido", k, 16, 2), A("idf", 3, 32, 4))
    for h in range(N):
        ids = (IDS * h, IDS * h + IDS)
        if h != r:
            const(A("ex", ids[0] + SLO, ids[1], 16), float(OWN + SLOTS * (turn(r, h) - turn(h, r)) + MID))
        for o in (0, 16):
            if h != r:
                cp(A("ex", ids[0] + o + SHI, ids[1], 32), A("landm", MS * h, MS * h + MS), "s")
            else:
                cp(A("ex", ids[0] + o + SLO, ids[1], 32), A("r32", 0, 11), "s")
                const(A("ex", ids[0] + o + SHI, ids[1], 32), i32)
        tr(A("m", *ids), A("ex", *ids))
    const(A("ex", ZID, 1440, 8), IDS / 2)
    tr(A("m", ZID, 1440), A("ex", ZID, 1440))
    cp(A("mg", 128, 256), A("m"), "s", A("ido", 8, 16))
    cp(A("mg", 0, 128), A("m"), "v", A("ido", 0, 8))
    tr(A("om"), A("mg"))
    for t in range(R):
        tt(quad(A("sl", 16 * t, 16 * t + 16), 0), quad(A("om", SHI, P, 16), t), quad(A("om", SLO, P, 16), t), Op.add)
    for k in range(4):
        cp(quad(A("off"), k), quad(A("sl"), 0))

    last = []
    for t in range(R):
        n = P if t else P // 2
        for a in range(0, P, n):
            kq, kp, by = A("k%dq" % t, a, a + n), A("k%dp" % t, a, a + n), A("off", 16 * t + a // 16, 16 * t + (a + n) // 16)
            cp(kp, A("qp"), "s", by)
            pick(kq, A("q"), by)
            for i in range(O * t, O * t + O):
                bank = 512 * (i + (R * O - O) * (a > 0))
                x = [A("ps", bank, bank + n), A("wq", 128 * i, 128 * i + 128), A("wp", 128 * i, 128 * i + 128), kq, kp]
                last = [add("t", lambda _, x=x: g.tensor.matmul_mx(*[ap(y) for y in x], True, True).then_inc(T.sem.st, 1), x[1:], [A("ps", bank, bank + 512)], 1.2 * (n + 16) * CYCLE, also=last)]
                reg = A("ys", P * i + a, P * i + a + n)
                cp(reg, x[0], "vs"[i % 2])
                load("y", "sty", [(T.y[:, reg[1]:reg[2]], ap(reg))], [reg], [], DMA + 0.4 * (R * O - i))

    known, log, total, waited = {k: {} for k in eng}, {}, {}, {}
    seq = in_order(calls)
    for n, c in enumerate(seq):
        q, c["waits"] = c["q"], []
        need = [tok for regs, w in ((c["reads"], False), (c["writes"], True)) for x in regs for y, w2, tok in log.get(x[0], []) if (w or w2) and clash(x, y)]
        for s, v, clock, by in sorted(need, key=lambda t: -t[3]):
            if c["go"] and known[q].get(s, 0) < v:
                c["waits"].append((s, v, by))
                for k, x in list(clock.items()) + [(s, v)]:
                    known[q][k] = max(known[q].get(k, 0), x)
        s = c["sem"] or sem_of[q]
        total[s] = total.pop(s, 0) + (c["n"] or 1)
        for regs, w in ((c["reads"], False), (c["writes"], True)):
            for x in regs:
                log.setdefault(x[0], []).append((x, w, (s, total[s], dict(known[q]) if c["go"] else {}, n)))
    for c in seq:
        for s, v, by in sorted(c["waits"], key=lambda t: seq[t[2]]["done"]):
            eng[c["q"]].wait_ge(T.sem[s], v)
            waited[s] = max(waited.get(s, 0), v)
        if c["go"]:
            c["go"](c["q"])
    for s in total:
        if waited.get(s, 0) < total[s]:
            g.wait_ge(T.sem[s], total[s])
